import numpy as np
import ml_dtypes


def mxq(x, axis, fmt="e4m3"):
    dtype, down = {"e4m3": (ml_dtypes.float8_e4m3fn, 7), "e5m2": (ml_dtypes.float8_e5m2, 14)}[fmt]
    v = np.moveaxis(np.asarray(x, np.float32).astype(ml_dtypes.bfloat16).astype(np.float64), axis, -1)
    blocks = v.reshape(v.shape[:-1] + (-1, 32))
    amax = np.abs(blocks).max(-1, keepdims=True)
    byte = np.maximum(np.where(amax > 0, np.frexp(amax)[1] - 1 + 127, 0) - down, 1)
    scale = np.exp2(byte - 127.0)
    codes = (blocks / scale).astype(np.float32).astype(dtype).astype(np.float64)
    return np.moveaxis((codes * scale).reshape(v.shape), -1, axis)


WIDE = False


def mx_kscale(k):
    if not WIDE:
        return np.ones(k)
    levels = np.array([10, -10, 5, -5, 0])
    if k % 512:
        return np.exp2(np.random.permutation(np.resize(levels, k // 32))).repeat(32)
    a = np.empty((k // 512, 16))
    for p in range(k // 512):
        a[p, :8] = np.random.permutation(np.resize(levels, 8))
        for g in range(8):
            far = levels[np.abs(levels - a[p, g]) >= 10]
            a[p, g + 8] = far[np.random.randint(len(far))]
    return np.exp2(a.ravel()).repeat(32)


def f64(x):
    return np.asarray(x).astype(np.float64)


def striped(idx):
    return np.tile(idx.reshape(-1, 16).T, (8, 1)).astype(np.uint16)


def unstriped(offs):
    return offs[:16].T.reshape(-1).astype(np.int64)


E2M1 = np.array([0.0, 0.5, 1.0, 1.5, 2.0, 3.0, 4.0, 6.0, -0.0, -0.5, -1.0, -1.5, -2.0, -3.0, -4.0, -6.0])


def pack_weight(w, fmt):
    k, n = w.shape
    w = f64(np.asarray(w, np.float32).astype(ml_dtypes.bfloat16)).reshape(k // 32, 32, n)
    amax = np.abs(w).max(1)
    if fmt == "e4m3":
        byte = np.frexp(amax)[1] - 1 + 127 - 7
    else:
        mant, ex = np.frexp(amax / 6.0)
        byte = np.where(mant > 0.5, ex, ex - 1) + 127
    byte = np.clip(np.where(amax > 0, byte, 1), 1, 254)
    scaled = (w * np.exp2(127.0 - byte)[:, None, :]).reshape(k, n).astype(np.float32)
    by_word = np.ascontiguousarray(scaled.reshape(k // 512, 128, 4, n).transpose(0, 1, 3, 2))
    if fmt == "e4m3":
        words = by_word.astype(ml_dtypes.float8_e4m3fn).view(np.uint8)
    else:
        c = by_word.astype(ml_dtypes.float4_e2m1fn).view(np.uint8) & 0xF
        words = (c[..., 0::2] | (c[..., 1::2] << 4)).reshape(k // 512, 128, 2 * n)
    return np.ascontiguousarray(words), np.ascontiguousarray(byte.astype(np.uint8).reshape(k // 512, 16, n))


def unpack_weight(words, scales, fmt):
    g, _, n = scales.shape
    words = np.ascontiguousarray(words).reshape(g, 128, n, -1)
    if fmt == "e4m3":
        vals = words.view(ml_dtypes.float8_e4m3fn).astype(np.float64)
    else:
        nib = np.empty((g, 128, n, 4), np.uint8)
        nib[..., 0::2] = words & 0xF
        nib[..., 1::2] = words >> 4
        vals = E2M1[nib]
    vals = vals * np.repeat(np.exp2(scales.astype(np.float64) - 127.0), 8, axis=1)[..., None]
    return vals.transpose(0, 1, 3, 2).reshape(g * 512, n)


def relu2(v):
    return np.maximum(v, 0.0) ** 2


K, T, E, C, H, N = 2048, 512, 6, 256, 512, 128
TOP = 3


def by_expert(wq, xq):
    return np.concatenate([wq[e].T @ xq[:, e * C:(e + 1) * C] for e in range(E)], axis=1)


def setup_inputs():
    n = np.random.standard_normal
    s = mx_kscale(K)[:, None]
    u = mx_kscale(H)
    deal = np.repeat(np.arange(E), C).reshape(TOP, T)[:, np.random.permutation(T)]
    deal = np.take_along_axis(deal, np.argsort(np.random.rand(TOP, T), axis=0), axis=0)
    for _ in range(8):
        s_, t_ = np.random.permutation(T).reshape(2, -1); r = np.random.randint(TOP, size=T // 2); x, y = deal[r, s_].copy(), deal[r, t_].copy()
        ok = ~((deal[:, s_] == y).any(0) | (deal[:, t_] == x).any(0)); deal[r[ok], s_[ok]] = y[ok]; deal[r[ok], t_[ok]] = x[ok]
    order = np.lexsort((np.random.rand(TOP * T), deal.reshape(-1)))
    slot_token = order % T; pos = np.empty(TOP * T, np.int64); pos[order] = np.arange(TOP * T); pos = pos.reshape(TOP, T)
    g = np.random.uniform(0.5, 1.5, (TOP, T)); g = g / g.sum(0)
    w1 = [pack_weight(m, "e2m1") for m in n((E, K, H)) / np.sqrt(K) / s[None] * u[None, None, :]]
    w2 = [pack_weight(m, "e2m1") for m in n((E, H, N)) / np.sqrt(H) / u[None, :, None] ** 2]
    w_slot = np.empty(E * C)
    for r in range(TOP): w_slot[pos[r]] = g[r]
    return {
        "xT": (n((K, T)) * s).astype(np.float32),
        "w1_words": np.stack([m[0] for m in w1]),
        "w1_scales": np.stack([m[1] for m in w1]),
        "w2_words": np.stack([m[0] for m in w2]),
        "w2_scales": np.stack([m[1] for m in w2]),
        "gate": np.tile(w_slot, (K, 1)).astype(np.float32),
        "offs": striped(slot_token),
        "pos1": striped(pos[0]),
        "pos2": striped(pos[1]),
        "pos3": striped(pos[2]),
    }


def reference(xT, w1_words, w1_scales, w2_words, w2_scales, gate, offs, pos1, pos2, pos3):
    idx = unstriped(offs)
    w1 = np.stack([unpack_weight(w1_words[e], w1_scales[e], "e2m1") for e in range(E)])
    w2 = np.stack([unpack_weight(w2_words[e], w2_scales[e], "e2m1") for e in range(E)])
    xq = mxq(f64(gate) * f64(xT)[:, idx], 0, "e4m3")
    h = relu2(by_expert(w1, xq))
    y = by_expert(w2, mxq(h, 0, "e4m3"))
    return y[:, unstriped(pos1)] + y[:, unstriped(pos2)] + y[:, unstriped(pos3)]

@@ -1,0 +1,244 @@
+from contextlib import ExitStack
+
+import concourse.mybir as mybir
+from concourse.masks import make_identity
+
+K, T, E, C, H, N = 2048, 512, 6, 256, 512, 128
+SLOTS = E * C
+FLOPS = 2 * SLOTS * (K * H + H * N)
+BYTES = 4 * K * T + E * (K * H + H * N) // 2 + E * (K * H + H * N) // 32 + 4 * SLOTS + 2 * 2 * SLOTS + 4 * N * T
+
+F32 = mybir.dt.float32
+BF16 = mybir.dt.bfloat16
+I32 = mybir.dt.int32
+U32 = mybir.dt.uint32
+U16 = mybir.dt.uint16
+U8 = mybir.dt.uint8
+FP8X4 = mybir.dt.float8_e4m3fn_x4
+FP4X4 = mybir.dt.float4_e2m1fn_x4
+ACT = mybir.ActivationFunctionType
+MULT = mybir.AluOpType.mult
+ADD = mybir.AluOpType.add
+
+P = 128
+PACK = 4
+K_PASS = P * PACK
+PASSES = K // K_PASS
+GROUP = 128
+GROUPS = SLOTS // GROUP
+WINDOW = T + 32
+CHUNKS = [512, 512, 256, 128, 128]
+EARLY_GROUPS = 2
+
+
+def pieces_in_order():
+    pieces, j0 = [], 0
+    for n in CHUNKS:
+        pieces.extend((s, j0, n) for s in range(PASSES))
+        j0 += n
+    return pieces
+
+
+def tile_moe_pre_mlp_relu2_kernel(
+    tc, xT, w1_words, w1_scales, w2_words, w2_scales, gate, offs, pos1, pos2, pos3, out
+):
+    nc = tc.nc
+    with ExitStack() as ctx:
+        keep = ctx.enter_context(tc.tile_pool(name="keep", bufs=1))
+        stage = ctx.enter_context(tc.tile_pool(name="stage", bufs=3))
+        psum = ctx.enter_context(tc.psum_pool(name="psum", bufs=1))
+
+        offs_sb = keep.tile([P, SLOTS // 16], U16, name="offs_sb")
+        pos_sb = [keep.tile([P, T // 16], U16, name="pos_sb%d" % r) for r in range(3)]
+        gate_sb = keep.tile([P, SLOTS], F32, name="gate_sb")
+        x_sb = [keep.tile([P, WINDOW], F32, name="x_sb%d" % b) for b in range(PASSES * PACK)]
+        w1_sb = [keep.tile([P, PASSES, 2 * H], U8, name="w1_sb%d" % e, align_bytes=64) for e in range(E)]
+        w1_sc = keep.tile([P, E * PASSES, H], U8, name="w1_sc", align_bytes=64)
+        w2_sb = keep.tile([P, E, 2 * N], U8, name="w2_sb", align_bytes=64)
+        w2_sc = keep.tile([P, E, N], U8, name="w2_sc", align_bytes=64)
+        x_codes = keep.tile([P, PASSES, SLOTS], U32, name="x_codes", align_bytes=64)
+        x_sc = keep.tile([P, PASSES, SLOTS], U8, name="x_sc", align_bytes=64)
+        h_codes = keep.tile([P, SLOTS], U32, name="h_codes", align_bytes=64)
+        h_sc = keep.tile([P, SLOTS], U8, name="h_sc", align_bytes=64)
+        h_bf = keep.tile([P, SLOTS, PACK], BF16, name="h_bf", align_bytes=64)
+        y_sb = keep.tile([P, SLOTS], F32, name="y_sb")
+        ident = keep.tile([P, P], F32, name="ident")
+
+        def load_x(b):
+            s, t = divmod(b, PACK)
+            row = K_PASS * s + t
+            base = min(row, K - K_PASS)
+            rows = xT[base:base + K_PASS, :].rearrange("(p j) w -> p (j w)", j=PACK)
+            col = (row - base) * T
+            if col + WINDOW <= PACK * T:
+                nc.sync.dma_start(out=x_sb[b][:], in_=rows[:, col:col + WINDOW])
+            else:
+                nc.sync.dma_start(out=x_sb[b][:, :T], in_=rows[:, col:col + T])
+                nc.sync.dma_start(out=x_sb[b][:, T:], in_=rows[:, :WINDOW - T])
+
+        def load_w1_scales(e0, e1):
+            src = w1_scales[e0:e1].rearrange("e s (q r) i -> r q (e s) i", r=4)
+            for r in range(4):
+                nc.sync.dma_start(
+                    out=w1_sc[r:P:32, e0 * PASSES:e1 * PASSES, :].bitcast(I32), in_=src[r].bitcast(I32)
+                )
+
+        def load_w1(e):
+            nc.sync.dma_start(
+                out=w1_sb[e][:].bitcast(I32), in_=w1_words[e].rearrange("s p b -> p s b").bitcast(I32)
+            )
+
+        nc.vector.memset(w1_sc[:].bitcast(I32), 0)
+        nc.vector.memset(w2_sc[:].bitcast(I32), 0)
+        make_identity(nc, ident[:])
+
+        first = CHUNKS[0]
+        nc.sync.dma_start(offs_sb[:], offs)
+        load_x(0)
+        nc.sync.dma_start(out=gate_sb[:, :first], in_=gate[:P, :first])
+        for b in range(1, PASSES * PACK):
+            load_x(b)
+        load_w1_scales(0, 2)
+        w2_src = w2_scales.rearrange("e s (q r) n -> r q (e s) n", r=4)
+        for r in range(4):
+            nc.sync.dma_start(out=w2_sc[r:P:32, :, :].bitcast(I32), in_=w2_src[r].bitcast(I32))
+        load_w1(0)
+        load_w1(1)
+        nc.sync.dma_start(out=gate_sb[:, first:], in_=gate[:P, first:])
+        nc.sync.dma_start(
+            out=w2_sb[:].bitcast(I32), in_=w2_words.rearrange("e s p b -> p (e s) b").bitcast(I32)
+        )
+        load_w1_scales(2, E)
+        for e in range(2, E):
+            load_w1(e)
+        for tile, pos in zip(pos_sb, (pos1, pos2, pos3)):
+            nc.sync.dma_start(tile[:], pos)
+
+        def gather(s, j0, n):
+            picked = stage.tile([P, PACK, n], F32, name="picked")
+            for t in range(PACK):
+                nc.vector.tensor_tensor(
+                    picked[:, t, :],
+                    x_sb[PACK * s + t][:].indirect(offs_sb[:, j0 // 16:(j0 + n) // 16]),
+                    gate_sb[:, j0:j0 + n],
+                    MULT,
+                )
+            rounded = stage.tile([P, n, PACK], BF16, name="rounded", align_bytes=64)
+            nc.scalar.copy(
+                out=rounded[:].rearrange("p (c i) t -> p c t i", i=4),
+                in_=picked[:].rearrange("p t (c i) -> p c t i", i=4),
+            )
+            return rounded
+
+        def quantise_x(s, j0, n, rounded):
+            nc.vector.quantize_mx(
+                out=x_codes[:, s, j0:j0 + n].bitcast(FP8X4),
+                scales=x_sc[:, s, j0:j0 + n],
+                in_=rounded[:].rearrange("p j t -> p (j t)"),
+            )
+
+        def first_pass(g, s, acc):
+            e = g * GROUP // C
+            cols = slice(g * GROUP, (g + 1) * GROUP)
+            nc.tensor.matmul_mx(
+                out=acc[:],
+                lhsT=x_codes[:, s, cols].bitcast(FP8X4),
+                lhsT_scale=x_sc[:, s, cols],
+                rhs=w1_sb[e][:, s, :].bitcast(FP4X4),
+                rhs_scale=w1_sc[:, e * PASSES + s, :],
+                start=(s == 0),
+                stop=(s == PASSES - 1),
+            )
+
+        def hidden(g, acc):
+            cols = slice(g * GROUP, (g + 1) * GROUP)
+            relu = stage.tile([P, PACK, P], F32, name="relu")
+            nc.scalar.activation(relu[:], acc[:].rearrange("j (p t) -> j t p", t=PACK), ACT.Relu)
+            turned = psum.tile([P, PACK, GROUP], F32, name="turned", bufs=2)
+            for t in range(PACK):
+                nc.tensor.transpose(turned[:, t, :], relu[:, t, :], ident[:])
+            nc.scalar.activation(h_bf[:, cols, :], turned[:].rearrange("p t j -> p j t"), ACT.Square)
+
+        def second_layer(j0, n):
+            e = j0 // C
+            cols = slice(j0, j0 + n)
+            nc.vector.quantize_mx(
+                out=h_codes[:, cols].bitcast(FP8X4),
+                scales=h_sc[:, cols],
+                in_=h_bf[:, cols, :].rearrange("p j t -> p (j t)"),
+            )
+            y_ps = psum.tile([P, n], F32, name="y_ps", bufs=1)
+            nc.tensor.matmul_mx(
+                out=y_ps[:],
+                lhsT=w2_sb[:, e, :].bitcast(FP4X4),
+                lhsT_scale=w2_sc[:, e, :],
+                rhs=h_codes[:, cols].bitcast(FP8X4),
+                rhs_scale=h_sc[:, cols],
+                start=True,
+                stop=True,
+            )
+            nc.scalar.copy(out=y_sb[:, cols], in_=y_ps[:])
+
+        early = {}
+
+        def after_quantise(s, j0, n):
+            todo = []
+            for g in range(j0 // GROUP, (j0 + n) // GROUP):
+                if g >= GROUPS - EARLY_GROUPS:
+                    if s == 0:
+                        early[g] = psum.tile([P, H], F32, name="early_acc", bufs=EARLY_GROUPS)
+                    first_pass(g, s, early[g])
+                    if s == PASSES - 1:
+                        hidden(g, early[g])
+                        todo.append((g * GROUP, GROUP))
+                elif s == PASSES - 1:
+                    acc = psum.tile([P, H], F32, name="acc", bufs=3)
+                    for sp in range(PASSES):
+                        first_pass(g, sp, acc)
+                    hidden(g, acc)
+                    if g % 2 == 1:
+                        todo.append(((g - 1) * GROUP, C))
+            return todo
+
+        waiting = None
+        second = []
+        for piece in pieces_in_order():
+            rounded = gather(*piece)
+            if second:
+                second_layer(*second.pop(0))
+            if waiting is not None:
+                quantise_x(*waiting)
+                second.extend(after_quantise(*waiting[:3]))
+            waiting = (*piece, rounded)
+        quantise_x(*waiting)
+        second.extend(after_quantise(*waiting[:3]))
+        for job in second:
+            second_layer(*job)
+
+        half = T // 2
+        fetched = [[keep.tile([P, half], F32, name="fetched%d%d" % (c, r)) for r in range(3)] for c in range(2)]
+        pair = [keep.tile([P, half], F32, name="pair%d" % c) for c in range(2)]
+        total = [keep.tile([P, half], F32, name="total%d" % c) for c in range(2)]
+
+        def fetch(c, r):
+            nc.vector.tensor_copy(
+                fetched[c][r][:], y_sb[:].indirect(pos_sb[r][:, c * half // 16:(c + 1) * half // 16])
+            )
+
+        def add_pair(c):
+            nc.vector.tensor_tensor(pair[c][:], fetched[c][0][:], fetched[c][1][:], ADD)
+
+        def finish(c):
+            nc.vector.tensor_tensor(total[c][:], pair[c][:], fetched[c][2][:], ADD)
+            nc.sync.dma_start(out=out[:, c * half:(c + 1) * half], in_=total[c][:])
+
+        fetch(0, 0)
+        fetch(0, 1)
+        fetch(0, 2)
+        fetch(1, 0)
+        add_pair(0)
+        fetch(1, 1)
+        finish(0)
+        add_pair(1)
+        fetch(1, 2)
+        finish(1)

@@ -28,15 +28,7 @@ GROUP = 128
 GROUPS = SLOTS // GROUP
 WINDOW = T + 32
 CHUNKS = [512, 512, 256, 128, 128]
-EARLY_GROUPS = 2
-
-
-def pieces_in_order():
-    pieces, j0 = [], 0
-    for n in CHUNKS:
-        pieces.extend((s, j0, n) for s in range(PASSES))
-        j0 += n
-    return pieces
+BATCHES = [[2, 2], [2, 2], [2, 2], [4], [2, 1, 1]]
 
 
 def tile_moe_pre_mlp_relu2_kernel(
@@ -53,16 +45,18 @@ def tile_moe_pre_mlp_relu2_kernel(
         gate_sb = keep.tile([P, SLOTS], F32, name="gate_sb")
         x_sb = [keep.tile([P, WINDOW], F32, name="x_sb%d" % b) for b in range(PASSES * PACK)]
         w1_sb = [keep.tile([P, PASSES, 2 * H], U8, name="w1_sb%d" % e, align_bytes=64) for e in range(E)]
-        w1_sc = keep.tile([P, E * PASSES, H], U8, name="w1_sc", align_bytes=64)
+        w1_sc = [keep.tile([P, 2 * PASSES, H], U8, name="w1_sc%d" % u, align_bytes=64) for u in range(E // 2)]
         w2_sb = keep.tile([P, E, 2 * N], U8, name="w2_sb", align_bytes=64)
         w2_sc = keep.tile([P, E, N], U8, name="w2_sc", align_bytes=64)
-        x_codes = keep.tile([P, PASSES, SLOTS], U32, name="x_codes", align_bytes=64)
-        x_sc = keep.tile([P, PASSES, SLOTS], U8, name="x_sc", align_bytes=64)
+        x_codes = keep.tile([P, PASSES * SLOTS], U32, name="x_codes", align_bytes=64)
+        x_sc = keep.tile([P, PASSES * SLOTS], U8, name="x_sc", align_bytes=64)
         h_codes = keep.tile([P, SLOTS], U32, name="h_codes", align_bytes=64)
         h_sc = keep.tile([P, SLOTS], U8, name="h_sc", align_bytes=64)
         h_bf = keep.tile([P, SLOTS, PACK], BF16, name="h_bf", align_bytes=64)
         y_sb = keep.tile([P, SLOTS], F32, name="y_sb")
         ident = keep.tile([P, P], F32, name="ident")
+        big = PACK * max(CHUNKS)
+        ring = keep.tile([P, 2 * big], F32, name="ring")
 
         def load_x(b):
             s, t = divmod(b, PACK)
@@ -76,46 +70,57 @@ def tile_moe_pre_mlp_relu2_kernel(
                 nc.sync.dma_start(out=x_sb[b][:, :T], in_=rows[:, col:col + T])
                 nc.sync.dma_start(out=x_sb[b][:, T:], in_=rows[:, :WINDOW - T])
 
-        def load_w1_scales(e0, e1):
-            src = w1_scales[e0:e1].rearrange("e s (q r) i -> r q (e s) i", r=4)
+        def load_w1_scales(u):
+            src = w1_scales[2 * u:2 * u + 2].rearrange("e s (q r) i -> r q (e s) i", r=4)
             for r in range(4):
-                nc.sync.dma_start(
-                    out=w1_sc[r:P:32, e0 * PASSES:e1 * PASSES, :].bitcast(I32), in_=src[r].bitcast(I32)
-                )
+                nc.sync.dma_start(out=w1_sc[u][r:P:32, :, :].bitcast(I32), in_=src[r].bitcast(I32))
 
         def load_w1(e):
             nc.sync.dma_start(
                 out=w1_sb[e][:].bitcast(I32), in_=w1_words[e].rearrange("s p b -> p s b").bitcast(I32)
             )
 
-        nc.vector.memset(w1_sc[:].bitcast(I32), 0)
+        nc.vector.memset(w1_sc[0][:].bitcast(I32), 0)
         nc.vector.memset(w2_sc[:].bitcast(I32), 0)
+        for u in range(1, E // 2):
+            nc.gpsimd.memset(w1_sc[u][:].bitcast(I32), 0)
         make_identity(nc, ident[:])
 
         first = CHUNKS[0]
-        nc.sync.dma_start(offs_sb[:], offs)
         load_x(0)
         nc.sync.dma_start(out=gate_sb[:, :first], in_=gate[:P, :first])
-        for b in range(1, PASSES * PACK):
+        nc.sync.dma_start(offs_sb[:], offs)
+        for b in range(1, 8):
             load_x(b)
-        load_w1_scales(0, 2)
+        load_w1_scales(0)
+        for b in range(8, 10):
+            load_x(b)
+        load_w1(0)
+        for b in range(10, 13):
+            load_x(b)
+        load_w1(1)
+        for b in range(13, PASSES * PACK):
+            load_x(b)
+        nc.sync.dma_start(out=gate_sb[:, first:], in_=gate[:P, first:])
         w2_src = w2_scales.rearrange("e s (q r) n -> r q (e s) n", r=4)
         for r in range(4):
             nc.sync.dma_start(out=w2_sc[r:P:32, :, :].bitcast(I32), in_=w2_src[r].bitcast(I32))
-        load_w1(0)
-        load_w1(1)
-        nc.sync.dma_start(out=gate_sb[:, first:], in_=gate[:P, first:])
+        for u in range(1, E // 2):
+            load_w1_scales(u)
         nc.sync.dma_start(
             out=w2_sb[:].bitcast(I32), in_=w2_words.rearrange("e s p b -> p (e s) b").bitcast(I32)
         )
-        load_w1_scales(2, E)
         for e in range(2, E):
             load_w1(e)
         for tile, pos in zip(pos_sb, (pos1, pos2, pos3)):
             nc.sync.dma_start(tile[:], pos)
 
-        def gather(s, j0, n):
-            picked = stage.tile([P, PACK, n], F32, name="picked")
+        def gather(step, s, j0, n, rounded):
+            if n > GROUP:
+                start = (step % 2) * big
+            else:
+                start = (0, big, big + PACK * GROUP)[step % 3]
+            picked = ring[:, start:start + PACK * n].rearrange("p (t j) -> p t j", t=PACK)
             for t in range(PACK):
                 nc.vector.tensor_tensor(
                     picked[:, t, :],
@@ -123,29 +128,29 @@ def tile_moe_pre_mlp_relu2_kernel(
                     gate_sb[:, j0:j0 + n],
                     MULT,
                 )
-            rounded = stage.tile([P, n, PACK], BF16, name="rounded", align_bytes=64)
             nc.scalar.copy(
-                out=rounded[:].rearrange("p (c i) t -> p c t i", i=4),
-                in_=picked[:].rearrange("p t (c i) -> p c t i", i=4),
+                out=rounded.rearrange("p (c i) t -> p c t i", i=4),
+                in_=picked.rearrange("p t (c i) -> p c t i", i=4),
             )
-            return rounded
 
-        def quantise_x(s, j0, n, rounded):
+        def quantise_x(s0, count, j0, n, rounded):
+            cols = slice(PASSES * j0 + s0 * n, PASSES * j0 + (s0 + count) * n)
             nc.vector.quantize_mx(
-                out=x_codes[:, s, j0:j0 + n].bitcast(FP8X4),
-                scales=x_sc[:, s, j0:j0 + n],
-                in_=rounded[:].rearrange("p j t -> p (j t)"),
+                out=x_codes[:, cols].bitcast(FP8X4),
+                scales=x_sc[:, cols],
+                in_=rounded[:].rearrange("p s j t -> p (s j t)"),
             )
 
-        def first_pass(g, s, acc):
+        def first_pass(g, s, j0, n, acc):
             e = g * GROUP // C
-            cols = slice(g * GROUP, (g + 1) * GROUP)
+            start = PASSES * j0 + s * n + g * GROUP - j0
+            cols = slice(start, start + GROUP)
             nc.tensor.matmul_mx(
                 out=acc[:],
-                lhsT=x_codes[:, s, cols].bitcast(FP8X4),
-                lhsT_scale=x_sc[:, s, cols],
+                lhsT=x_codes[:, cols].bitcast(FP8X4),
+                lhsT_scale=x_sc[:, cols],
                 rhs=w1_sb[e][:, s, :].bitcast(FP4X4),
-                rhs_scale=w1_sc[:, e * PASSES + s, :],
+                rhs_scale=w1_sc[e // 2][:, e % 2 * PASSES + s, :],
                 start=(s == 0),
                 stop=(s == PASSES - 1),
             )
@@ -153,7 +158,10 @@ def tile_moe_pre_mlp_relu2_kernel(
         def hidden(g, acc):
             cols = slice(g * GROUP, (g + 1) * GROUP)
             relu = stage.tile([P, PACK, P], F32, name="relu")
-            nc.scalar.activation(relu[:], acc[:].rearrange("j (p t) -> j t p", t=PACK), ACT.Relu)
+            planes = acc[:].rearrange("j (p t) -> j t p", t=PACK)
+            part = 2 if g == GROUPS - 1 else PACK
+            for t in range(0, PACK, part):
+                nc.scalar.activation(relu[:, t:t + part, :], planes[:, t:t + part, :], ACT.Relu)
             turned = psum.tile([P, PACK, GROUP], F32, name="turned", bufs=2)
             for t in range(PACK):
                 nc.tensor.transpose(turned[:, t, :], relu[:, t, :], ident[:])
@@ -167,7 +175,7 @@ def tile_moe_pre_mlp_relu2_kernel(
                 scales=h_sc[:, cols],
                 in_=h_bf[:, cols, :].rearrange("p j t -> p (j t)"),
             )
-            y_ps = psum.tile([P, n], F32, name="y_ps", bufs=1)
+            y_ps = psum.tile([P, n], F32, name="y_ps", bufs=2)
             nc.tensor.matmul_mx(
                 out=y_ps[:],
                 lhsT=w2_sb[:, e, :].bitcast(FP4X4),
@@ -177,43 +185,68 @@ def tile_moe_pre_mlp_relu2_kernel(
                 start=True,
                 stop=True,
             )
+            return cols, y_ps
+
+        def keep_result(cols, y_ps):
             nc.scalar.copy(out=y_sb[:, cols], in_=y_ps[:])
 
-        early = {}
+        last = GROUPS - 1
+        acc = {}
+        complete, second, results = [], [], []
 
-        def after_quantise(s, j0, n):
-            todo = []
+        def multiply(s0, count, j0, n):
             for g in range(j0 // GROUP, (j0 + n) // GROUP):
-                if g >= GROUPS - EARLY_GROUPS:
-                    if s == 0:
-                        early[g] = psum.tile([P, H], F32, name="early_acc", bufs=EARLY_GROUPS)
-                    first_pass(g, s, early[g])
-                    if s == PASSES - 1:
-                        hidden(g, early[g])
-                        todo.append((g * GROUP, GROUP))
-                elif s == PASSES - 1:
-                    acc = psum.tile([P, H], F32, name="acc", bufs=3)
-                    for sp in range(PASSES):
-                        first_pass(g, sp, acc)
-                    hidden(g, acc)
-                    if g % 2 == 1:
-                        todo.append(((g - 1) * GROUP, C))
-            return todo
+                if s0 == 0:
+                    acc[g] = psum.tile([P, H], F32, name="acc", bufs=4)
+                for s in range(s0, s0 + count):
+                    first_pass(g, s, j0, n, acc[g])
+                if s0 + count == PASSES:
+                    complete.append(g)
+
+        def activate(count):
+            for g in complete[:count]:
+                hidden(g, acc[g])
+                if g >= last - 1:
+                    second.append((g * GROUP, GROUP))
+                elif g % 2 == 1:
+                    second.append(((g - 1) * GROUP, C))
+            complete[:count] = []
 
         waiting = None
-        second = []
-        for piece in pieces_in_order():
-            rounded = gather(*piece)
-            if second:
-                second_layer(*second.pop(0))
-            if waiting is not None:
-                quantise_x(*waiting)
-                second.extend(after_quantise(*waiting[:3]))
-            waiting = (*piece, rounded)
+        step, j0 = 0, 0
+        for n, batches in zip(CHUNKS, BATCHES):
+            s0 = 0
+            for count in batches:
+                rounded = stage.tile([P, count, n, PACK], BF16, name="rounded", align_bytes=64, bufs=3)
+                for s in range(s0, s0 + count):
+                    gather(step, s, j0, n, rounded[:, s - s0, :, :])
+                    if results:
+                        keep_result(*results.pop(0))
+                    if second:
+                        results.append(second_layer(*second.pop(0)))
+                    budget = {512: 2, 256: 1, 128: 1 - step % 2}[n]
+                    if waiting is None:
+                        activate(budget)
+                    elif waiting[0] + waiting[1] == PASSES:
+                        quantise_x(*waiting)
+                        multiply(*waiting[:4])
+                        activate(budget)
+                    else:
+                        quantise_x(*waiting)
+                        activate(budget)
+                        multiply(*waiting[:4])
+                    waiting = None
+                    step += 1
+                waiting = (s0, count, j0, n, rounded)
+                s0 += count
+            j0 += n
         quantise_x(*waiting)
-        second.extend(after_quantise(*waiting[:3]))
+        multiply(*waiting[:4])
+        activate(len(complete))
         for job in second:
-            second_layer(*job)
+            results.append(second_layer(*job))
+        for job in results:
+            keep_result(*job)
 
         half = T // 2
         fetched = [[keep.tile([P, half], F32, name="fetched%d%d" % (c, r)) for r in range(3)] for c in range(2)]

@@ -27,8 +27,9 @@ PASSES = K // K_PASS
 GROUP = 128
 GROUPS = SLOTS // GROUP
 WINDOW = T + 32
-CHUNKS = [512, 512, 256, 128, 128]
-BATCHES = [[2, 2], [2, 2], [2, 2], [4], [2, 1, 1]]
+WIDEST = 512
+BATCHES = [(j0, WIDEST, s0, 2) for j0 in (0, WIDEST) for s0 in (0, 2)] + [(2 * WIDEST, WIDEST, 0, 2)]
+BATCHES = BATCHES + [(j0, n, s, 1) for j0, n in ((1024, 256), (1280, 128), (1408, 128)) for s in (2, 3)]
 
 
 def tile_moe_pre_mlp_relu2_kernel(
@@ -55,7 +56,7 @@ def tile_moe_pre_mlp_relu2_kernel(
         h_bf = keep.tile([P, SLOTS, PACK], BF16, name="h_bf", align_bytes=64)
         y_sb = keep.tile([P, SLOTS], F32, name="y_sb")
         ident = keep.tile([P, P], F32, name="ident")
-        big = PACK * max(CHUNKS)
+        big = PACK * WIDEST
         ring = keep.tile([P, 2 * big], F32, name="ring")
 
         def load_x(b):
@@ -86,31 +87,31 @@ def tile_moe_pre_mlp_relu2_kernel(
             nc.gpsimd.memset(w1_sc[u][:].bitcast(I32), 0)
         make_identity(nc, ident[:])
 
-        first = CHUNKS[0]
+        first = WIDEST
         load_x(0)
         nc.sync.dma_start(out=gate_sb[:, :first], in_=gate[:P, :first])
         nc.sync.dma_start(offs_sb[:], offs)
-        for b in range(1, 8):
+        extras = {
+            3: lambda: load_w1_scales(0),
+            5: lambda: load_w1(0),
+            7: lambda: load_w1(1),
+            9: lambda: load_w1_scales(1),
+            11: lambda: load_w1(2),
+            13: lambda: load_w1(3),
+        }
+        for b in range(1, PASSES * PACK):
             load_x(b)
-        load_w1_scales(0)
-        for b in range(8, 10):
-            load_x(b)
-        load_w1(0)
-        for b in range(10, 13):
-            load_x(b)
-        load_w1(1)
-        for b in range(13, PASSES * PACK):
-            load_x(b)
+            if b in extras:
+                extras[b]()
         nc.sync.dma_start(out=gate_sb[:, first:], in_=gate[:P, first:])
         w2_src = w2_scales.rearrange("e s (q r) n -> r q (e s) n", r=4)
         for r in range(4):
             nc.sync.dma_start(out=w2_sc[r:P:32, :, :].bitcast(I32), in_=w2_src[r].bitcast(I32))
-        for u in range(1, E // 2):
-            load_w1_scales(u)
+        load_w1_scales(2)
         nc.sync.dma_start(
             out=w2_sb[:].bitcast(I32), in_=w2_words.rearrange("e s p b -> p (e s) b").bitcast(I32)
         )
-        for e in range(2, E):
+        for e in range(4, E):
             load_w1(e)
         for tile, pos in zip(pos_sb, (pos1, pos2, pos3)):
             nc.sync.dma_start(tile[:], pos)
@@ -133,17 +134,16 @@ def tile_moe_pre_mlp_relu2_kernel(
                 in_=picked.rearrange("p t (c i) -> p c t i", i=4),
             )
 
-        def quantise_x(s0, count, j0, n, rounded):
-            cols = slice(PASSES * j0 + s0 * n, PASSES * j0 + (s0 + count) * n)
+        def quantise_x(j0, n, s0, count, base, rounded):
+            cols = slice(base, base + count * n)
             nc.vector.quantize_mx(
                 out=x_codes[:, cols].bitcast(FP8X4),
                 scales=x_sc[:, cols],
                 in_=rounded[:].rearrange("p s j t -> p (s j t)"),
             )
 
-        def first_pass(g, s, j0, n, acc):
+        def first_pass(g, s, start, acc):
             e = g * GROUP // C
-            start = PASSES * j0 + s * n + g * GROUP - j0
             cols = slice(start, start + GROUP)
             nc.tensor.matmul_mx(
                 out=acc[:],
@@ -194,12 +194,12 @@ def tile_moe_pre_mlp_relu2_kernel(
         acc = {}
         complete, second, results = [], [], []
 
-        def multiply(s0, count, j0, n):
+        def multiply(j0, n, s0, count, base):
             for g in range(j0 // GROUP, (j0 + n) // GROUP):
                 if s0 == 0:
                     acc[g] = psum.tile([P, H], F32, name="acc", bufs=4)
                 for s in range(s0, s0 + count):
-                    first_pass(g, s, j0, n, acc[g])
+                    first_pass(g, s, base + (s - s0) * n + g * GROUP - j0, acc[g])
                 if s0 + count == PASSES:
                     complete.append(g)
 
@@ -213,35 +213,32 @@ def tile_moe_pre_mlp_relu2_kernel(
             complete[:count] = []
 
         waiting = None
-        step, j0 = 0, 0
-        for n, batches in zip(CHUNKS, BATCHES):
-            s0 = 0
-            for count in batches:
-                rounded = stage.tile([P, count, n, PACK], BF16, name="rounded", align_bytes=64, bufs=3)
-                for s in range(s0, s0 + count):
-                    gather(step, s, j0, n, rounded[:, s - s0, :, :])
-                    if results:
-                        keep_result(*results.pop(0))
-                    if second:
-                        results.append(second_layer(*second.pop(0)))
-                    budget = {512: 2, 256: 1, 128: 1 - step % 2}[n]
-                    if waiting is None:
-                        activate(budget)
-                    elif waiting[0] + waiting[1] == PASSES:
-                        quantise_x(*waiting)
-                        multiply(*waiting[:4])
-                        activate(budget)
-                    else:
-                        quantise_x(*waiting)
-                        activate(budget)
-                        multiply(*waiting[:4])
-                    waiting = None
-                    step += 1
-                waiting = (s0, count, j0, n, rounded)
-                s0 += count
-            j0 += n
+        step, base = 0, 0
+        for j0, n, s0, count in BATCHES:
+            rounded = stage.tile([P, count, n, PACK], BF16, name="rounded", align_bytes=64, bufs=3)
+            for s in range(s0, s0 + count):
+                gather(step, s, j0, n, rounded[:, s - s0, :, :])
+                if results:
+                    keep_result(*results.pop(0))
+                if second:
+                    results.append(second_layer(*second.pop(0)))
+                budget = {512: 2, 256: 1, 128: 1 - step % 2}[n]
+                if waiting is None:
+                    activate(budget)
+                elif waiting[2] + waiting[3] == PASSES:
+                    quantise_x(*waiting)
+                    multiply(*waiting[:5])
+                    activate(budget)
+                else:
+                    quantise_x(*waiting)
+                    activate(budget)
+                    multiply(*waiting[:5])
+                waiting = None
+                step += 1
+            waiting = (j0, n, s0, count, base, rounded)
+            base += count * n
         quantise_x(*waiting)
-        multiply(*waiting[:4])
+        multiply(*waiting[:5])
         activate(len(complete))
         for job in second:
             results.append(second_layer(*job))
@@ -249,29 +246,19 @@ def tile_moe_pre_mlp_relu2_kernel(
             keep_result(*job)
 
         half = T // 2
-        fetched = [[keep.tile([P, half], F32, name="fetched%d%d" % (c, r)) for r in range(3)] for c in range(2)]
-        pair = [keep.tile([P, half], F32, name="pair%d" % c) for c in range(2)]
-        total = [keep.tile([P, half], F32, name="total%d" % c) for c in range(2)]
+        fetched = [keep.tile([P, T], F32, name="fetched%d" % r) for r in range(3)]
+        pair = keep.tile([P, T], F32, name="pair")
+        total = keep.tile([P, T], F32, name="total")
 
-        def fetch(c, r):
-            nc.vector.tensor_copy(
-                fetched[c][r][:], y_sb[:].indirect(pos_sb[r][:, c * half // 16:(c + 1) * half // 16])
-            )
+        def fetch(r, t0, t1):
+            nc.vector.tensor_copy(fetched[r][:, t0:t1], y_sb[:].indirect(pos_sb[r][:, t0 // 16:t1 // 16]))
 
-        def add_pair(c):
-            nc.vector.tensor_tensor(pair[c][:], fetched[c][0][:], fetched[c][1][:], ADD)
-
-        def finish(c):
-            nc.vector.tensor_tensor(total[c][:], pair[c][:], fetched[c][2][:], ADD)
-            nc.sync.dma_start(out=out[:, c * half:(c + 1) * half], in_=total[c][:])
-
-        fetch(0, 0)
-        fetch(0, 1)
-        fetch(0, 2)
-        fetch(1, 0)
-        add_pair(0)
-        fetch(1, 1)
-        finish(0)
-        add_pair(1)
-        fetch(1, 2)
-        finish(1)
+        fetch(0, 0, T)
+        fetch(1, 0, T)
+        fetch(2, 0, half)
+        nc.vector.tensor_tensor(pair[:], fetched[0][:], fetched[1][:], ADD)
+        fetch(2, half, T)
+        for t0 in (0, half):
+            cols = slice(t0, t0 + half)
+            nc.vector.tensor_tensor(total[:, cols], pair[:, cols], fetched[2][:, cols], ADD)
+            nc.sync.dma_start(out=out[:, cols], in_=total[:, cols])

@@ -51,8 +51,6 @@ def tile_moe_pre_mlp_relu2_kernel(
         w2_sc = keep.tile([P, E, N], U8, name="w2_sc", align_bytes=64)
         x_codes = keep.tile([P, PASSES * SLOTS], U32, name="x_codes", align_bytes=64)
         x_sc = keep.tile([P, PASSES * SLOTS], U8, name="x_sc", align_bytes=64)
-        h_codes = keep.tile([P, SLOTS], U32, name="h_codes", align_bytes=64)
-        h_sc = keep.tile([P, SLOTS], U8, name="h_sc", align_bytes=64)
         h_bf = keep.tile([P, SLOTS, PACK], BF16, name="h_bf", align_bytes=64)
         y_sb = keep.tile([P, SLOTS], F32, name="y_sb")
         ident = keep.tile([P, P], F32, name="ident")
@@ -167,32 +165,46 @@ def tile_moe_pre_mlp_relu2_kernel(
                 nc.tensor.transpose(turned[:, t, :], relu[:, t, :], ident[:])
             nc.scalar.activation(h_bf[:, cols, :], turned[:].rearrange("p t j -> p j t"), ACT.Square)
 
-        def second_layer(j0, n):
-            e = j0 // C
-            cols = slice(j0, j0 + n)
+        memory_order = [0, 8, 1, 9, 2, 10, 3, 4, 5, 6, 7]
+        x_place, end = {}, 0
+        for b in memory_order:
+            x_place[b] = end
+            end += BATCHES[b][1] * BATCHES[b][3]
+        h_place = {
+            0: x_place[8] + GROUP - WIDEST,
+            WIDEST: x_place[9] + GROUP - WIDEST,
+            2 * WIDEST: x_place[10] + GROUP - C,
+            SLOTS - C: x_place[3],
+            SLOTS - GROUP: x_place[3] + GROUP,
+        }
+
+        def quantise_h(j0, n):
+            cols = slice(h_place[j0], h_place[j0] + n)
             nc.vector.quantize_mx(
-                out=h_codes[:, cols].bitcast(FP8X4),
-                scales=h_sc[:, cols],
-                in_=h_bf[:, cols, :].rearrange("p j t -> p (j t)"),
+                out=x_codes[:, cols].bitcast(FP8X4),
+                scales=x_sc[:, cols],
+                in_=h_bf[:, j0:j0 + n, :].rearrange("p j t -> p (j t)"),
             )
-            y_ps = psum.tile([P, n], F32, name="y_ps", bufs=2)
-            nc.tensor.matmul_mx(
-                out=y_ps[:],
-                lhsT=w2_sb[:, e, :].bitcast(FP4X4),
-                lhsT_scale=w2_sc[:, e, :],
-                rhs=h_codes[:, cols].bitcast(FP8X4),
-                rhs_scale=h_sc[:, cols],
-                start=True,
-                stop=True,
-            )
-            return cols, y_ps
 
-        def keep_result(cols, y_ps):
-            nc.scalar.copy(out=y_sb[:, cols], in_=y_ps[:])
+        def second_layer(j0, n, bank, col):
+            for j in range(j0, j0 + n, C):
+                width = min(C, n)
+                cols = slice(h_place[j0] + j - j0, h_place[j0] + j - j0 + width)
+                nc.tensor.matmul_mx(
+                    out=bank[:, col + j - j0:col + j - j0 + width],
+                    lhsT=w2_sb[:, j // C, :].bitcast(FP4X4),
+                    lhsT_scale=w2_sc[:, j // C, :],
+                    rhs=x_codes[:, cols].bitcast(FP8X4),
+                    rhs_scale=x_sc[:, cols],
+                    start=True,
+                    stop=True,
+                )
 
-        last = GROUPS - 1
+        def keep_result(j0, n, bank):
+            nc.vector.tensor_copy(y_sb[:, j0:j0 + n], bank[:, :n])
+
         acc = {}
-        complete, second, results = [], [], []
+        complete = []
 
         def multiply(j0, n, s0, count, base):
             for g in range(j0 // GROUP, (j0 + n) // GROUP):
@@ -206,22 +218,14 @@ def tile_moe_pre_mlp_relu2_kernel(
         def activate(count):
             for g in complete[:count]:
                 hidden(g, acc[g])
-                if g >= last - 1:
-                    second.append((g * GROUP, GROUP))
-                elif g % 2 == 1:
-                    second.append(((g - 1) * GROUP, C))
             complete[:count] = []
 
         waiting = None
-        step, base = 0, 0
-        for j0, n, s0, count in BATCHES:
+        step = 0
+        for b, (j0, n, s0, count) in enumerate(BATCHES):
             rounded = stage.tile([P, count, n, PACK], BF16, name="rounded", align_bytes=64, bufs=3)
             for s in range(s0, s0 + count):
                 gather(step, s, j0, n, rounded[:, s - s0, :, :])
-                if results:
-                    keep_result(*results.pop(0))
-                if second:
-                    results.append(second_layer(*second.pop(0)))
                 budget = {512: 2, 256: 1, 128: 1 - step % 2}[n]
                 if waiting is None:
                     activate(budget)
@@ -235,15 +239,26 @@ def tile_moe_pre_mlp_relu2_kernel(
                     multiply(*waiting[:5])
                 waiting = None
                 step += 1
-            waiting = (j0, n, s0, count, base, rounded)
-            base += count * n
+            waiting = (j0, n, s0, count, x_place[b], rounded)
+        y_banks = [psum.tile([P, WIDEST], F32, name="y_bank", bufs=2) for u in range(2)]
+        quantise_h(0, WIDEST)
         quantise_x(*waiting)
         multiply(*waiting[:5])
         activate(len(complete))
-        for job in second:
-            results.append(second_layer(*job))
-        for job in results:
-            keep_result(*job)
+        second_layer(0, WIDEST, y_banks[0], 0)
+        quantise_h(WIDEST, WIDEST)
+        second_layer(WIDEST, WIDEST, y_banks[1], 0)
+        y_banks.extend(psum.tile([P, H], F32, name="acc", bufs=4) for u in range(2))
+        quantise_h(2 * WIDEST, C)
+        second_layer(2 * WIDEST, C, y_banks[2], 0)
+        keep_result(0, WIDEST, y_banks[0])
+        keep_result(WIDEST, WIDEST, y_banks[1])
+        quantise_h(SLOTS - C, GROUP)
+        second_layer(SLOTS - C, GROUP, y_banks[2], C)
+        quantise_h(SLOTS - GROUP, GROUP)
+        second_layer(SLOTS - GROUP, GROUP, y_banks[3], 0)
+        keep_result(2 * WIDEST, C + GROUP, y_banks[2])
+        keep_result(SLOTS - GROUP, GROUP, y_banks[3])
 
         half = T // 2
         fetched = [keep.tile([P, T], F32, name="fetched%d" % r) for r in range(3)]
@@ -255,9 +270,10 @@ def tile_moe_pre_mlp_relu2_kernel(
 
         fetch(0, 0, T)
         fetch(1, 0, T)
-        fetch(2, 0, half)
-        nc.vector.tensor_tensor(pair[:], fetched[0][:], fetched[1][:], ADD)
-        fetch(2, half, T)
+        for t0 in (0, half):
+            cols = slice(t0, t0 + half)
+            nc.gpsimd.tensor_tensor(pair[:, cols], fetched[0][:, cols], fetched[1][:, cols], ADD)
+            fetch(2, t0, t0 + half)
         for t0 in (0, half):
             cols = slice(t0, t0 + half)
             nc.vector.tensor_tensor(total[:, cols], pair[:, cols], fetched[2][:, cols], ADD)

@@ -28,8 +28,10 @@ GROUP = 128
 GROUPS = SLOTS // GROUP
 WINDOW = T + 32
 WIDEST = 512
-BATCHES = [(j0, WIDEST, s0, 2) for j0 in (0, WIDEST) for s0 in (0, 2)] + [(2 * WIDEST, WIDEST, 0, 2)]
-BATCHES = BATCHES + [(j0, n, s, 1) for j0, n in ((1024, 256), (1280, 128), (1408, 128)) for s in (2, 3)]
+STEPS = [(j0, WIDEST, s) for s in (0, 1) for j0 in (0, WIDEST)]
+STEPS = STEPS + [(j0, WIDEST, s) for j0 in (0, WIDEST) for s in (2, 3)] + [(2 * WIDEST, WIDEST, 0)]
+STEPS = STEPS + [(2 * WIDEST, C, s) for s in (1, 2, 3)] + [(SLOTS - C, C, s) for s in (1, 2)]
+STEPS = STEPS + [(SLOTS - C, GROUP, 3), (SLOTS - GROUP, GROUP, 3)]
 
 
 def tile_moe_pre_mlp_relu2_kernel(
@@ -79,104 +81,128 @@ def tile_moe_pre_mlp_relu2_kernel(
                 out=w1_sb[e][:].bitcast(I32), in_=w1_words[e].rearrange("s p b -> p s b").bitcast(I32)
             )
 
-        nc.vector.memset(w1_sc[0][:].bitcast(I32), 0)
-        nc.vector.memset(w2_sc[:].bitcast(I32), 0)
+        nc.gpsimd.memset(w1_sc[0][:].bitcast(I32), 0)
+        make_identity(nc, ident[:])
         for u in range(1, E // 2):
             nc.gpsimd.memset(w1_sc[u][:].bitcast(I32), 0)
-        make_identity(nc, ident[:])
+        nc.gpsimd.memset(w2_sc[:].bitcast(I32), 0)
 
         first = WIDEST
         load_x(0)
-        nc.sync.dma_start(out=gate_sb[:, :first], in_=gate[:P, :first])
         nc.sync.dma_start(offs_sb[:], offs)
-        extras = {
-            3: lambda: load_w1_scales(0),
-            5: lambda: load_w1(0),
-            7: lambda: load_w1(1),
-            9: lambda: load_w1_scales(1),
-            11: lambda: load_w1(2),
-            13: lambda: load_w1(3),
-        }
+        nc.sync.dma_start(out=gate_sb[:, :first], in_=gate[:P, :first])
         for b in range(1, PASSES * PACK):
             load_x(b)
-            if b in extras:
-                extras[b]()
-        nc.sync.dma_start(out=gate_sb[:, first:], in_=gate[:P, first:])
+            if b == PACK - 1:
+                nc.sync.dma_start(out=gate_sb[:, first:2 * first], in_=gate[:P, first:2 * first])
+            if b == 2 * PACK - 1:
+                load_w1_scales(0)
+                load_w1(0)
+                load_w1(1)
+        load_w1_scales(1)
+        load_w1(2)
+        load_w1(3)
+        nc.sync.dma_start(out=gate_sb[:, 2 * first:], in_=gate[:P, 2 * first:])
+        load_w1_scales(2)
         w2_src = w2_scales.rearrange("e s (q r) n -> r q (e s) n", r=4)
         for r in range(4):
             nc.sync.dma_start(out=w2_sc[r:P:32, :, :].bitcast(I32), in_=w2_src[r].bitcast(I32))
-        load_w1_scales(2)
+        load_w1(4)
+        load_w1(5)
         nc.sync.dma_start(
             out=w2_sb[:].bitcast(I32), in_=w2_words.rearrange("e s p b -> p (e s) b").bitcast(I32)
         )
-        for e in range(4, E):
-            load_w1(e)
         for tile, pos in zip(pos_sb, (pos1, pos2, pos3)):
             nc.sync.dma_start(tile[:], pos)
 
-        def gather(step, s, j0, n, rounded):
-            if n > GROUP:
-                start = (step % 2) * big
-            else:
-                start = (0, big, big + PACK * GROUP)[step % 3]
-            picked = ring[:, start:start + PACK * n].rearrange("p (t j) -> p t j", t=PACK)
+        rounded = {}
+
+        def picked(step):
+            n = STEPS[step][1]
+            start = (step % 2) * big
+            return ring[:, start:start + PACK * n].rearrange("p (t j) -> p t j", t=PACK)
+
+        def gather(step):
+            j0, n, s = STEPS[step]
             for t in range(PACK):
                 nc.vector.tensor_tensor(
-                    picked[:, t, :],
+                    picked(step)[:, t, :],
                     x_sb[PACK * s + t][:].indirect(offs_sb[:, j0 // 16:(j0 + n) // 16]),
                     gate_sb[:, j0:j0 + n],
                     MULT,
                 )
+
+        def weave(step):
+            n = STEPS[step][1]
+            rounded[step] = stage.tile([P, n, PACK], BF16, name="rounded", align_bytes=64, bufs=3)
             nc.scalar.copy(
-                out=rounded.rearrange("p (c i) t -> p c t i", i=4),
-                in_=picked.rearrange("p t (c i) -> p c t i", i=4),
+                out=rounded[step][:].rearrange("p (c i) t -> p c t i", i=4),
+                in_=picked(step).rearrange("p t (c i) -> p c t i", i=4),
             )
 
-        def quantise_x(j0, n, s0, count, base, rounded):
-            cols = slice(base, base + count * n)
-            nc.vector.quantize_mx(
-                out=x_codes[:, cols].bitcast(FP8X4),
-                scales=x_sc[:, cols],
-                in_=rounded[:].rearrange("p s j t -> p (s j t)"),
-            )
-
-        def first_pass(g, s, start, acc):
-            e = g * GROUP // C
-            cols = slice(start, start + GROUP)
-            nc.tensor.matmul_mx(
-                out=acc[:],
-                lhsT=x_codes[:, cols].bitcast(FP8X4),
-                lhsT_scale=x_sc[:, cols],
-                rhs=w1_sb[e][:, s, :].bitcast(FP4X4),
-                rhs_scale=w1_sc[e // 2][:, e % 2 * PASSES + s, :],
-                start=(s == 0),
-                stop=(s == PASSES - 1),
-            )
-
-        def hidden(g, acc):
-            cols = slice(g * GROUP, (g + 1) * GROUP)
-            relu = stage.tile([P, PACK, P], F32, name="relu")
-            planes = acc[:].rearrange("j (p t) -> j t p", t=PACK)
-            part = 2 if g == GROUPS - 1 else PACK
-            for t in range(0, PACK, part):
-                nc.scalar.activation(relu[:, t:t + part, :], planes[:, t:t + part, :], ACT.Relu)
-            turned = psum.tile([P, PACK, GROUP], F32, name="turned", bufs=2)
-            for t in range(PACK):
-                nc.tensor.transpose(turned[:, t, :], relu[:, t, :], ident[:])
-            nc.scalar.activation(h_bf[:, cols, :], turned[:].rearrange("p t j -> p j t"), ACT.Square)
-
-        memory_order = [0, 8, 1, 9, 2, 10, 3, 4, 5, 6, 7]
+        last = len(STEPS) - 1
+        memory_order = [0, last - 2, 2, 4, last - 1, 1, 3] + list(range(5, last - 2)) + [last]
         x_place, end = {}, 0
         for b in memory_order:
             x_place[b] = end
-            end += BATCHES[b][1] * BATCHES[b][3]
+            end += STEPS[b][1]
         h_place = {
-            0: x_place[8] + GROUP - WIDEST,
-            WIDEST: x_place[9] + GROUP - WIDEST,
-            2 * WIDEST: x_place[10] + GROUP - C,
-            SLOTS - C: x_place[3],
-            SLOTS - GROUP: x_place[3] + GROUP,
+            0: x_place[last - 2] + GROUP - WIDEST,
+            WIDEST: x_place[last - 2] + GROUP,
+            2 * WIDEST: x_place[last - 1] + GROUP - C,
+            SLOTS - C: x_place[5],
+            SLOTS - GROUP: x_place[5] + GROUP,
         }
+
+        acc = {}
+
+        def quantise_x(step):
+            j0, n, s = STEPS[step]
+            base = x_place[step]
+            nc.vector.quantize_mx(
+                out=x_codes[:, base:base + n].bitcast(FP8X4),
+                scales=x_sc[:, base:base + n],
+                in_=rounded[step][:].rearrange("p j t -> p (j t)"),
+            )
+
+        def codes_of(g, s):
+            for step, (j0, n, s0) in enumerate(STEPS):
+                if s0 == s and j0 <= g * GROUP < j0 + n:
+                    return x_place[step] + g * GROUP - j0
+
+        def multiply(g, passes):
+            for s in passes:
+                if g not in acc:
+                    acc[g] = psum.tile([P, H], F32, name="acc", bufs=2)
+                e = g * GROUP // C
+                cols = slice(codes_of(g, s), codes_of(g, s) + GROUP)
+                nc.tensor.matmul_mx(
+                    out=acc[g][:],
+                    lhsT=x_codes[:, cols].bitcast(FP8X4),
+                    lhsT_scale=x_sc[:, cols],
+                    rhs=w1_sb[e][:, s, :].bitcast(FP4X4),
+                    rhs_scale=w1_sc[e // 2][:, e % 2 * PASSES + s, :],
+                    start=(s == (3 if g < 8 else 2)),
+                    stop=(s == (2 if g < 8 else 3)),
+                )
+
+        turned = {}
+
+        def rectify(g):
+            relu = stage.tile([P, PACK, P], F32, name="relu")
+            planes = acc[g][:].rearrange("j (p t) -> j t p", t=PACK)
+            part = 2 if g == GROUPS - 1 else PACK
+            for t in range(0, PACK, part):
+                nc.scalar.activation(relu[:, t:t + part, :], planes[:, t:t + part, :], ACT.Relu)
+            turned[g] = psum.tile([P, PACK, GROUP], F32, name="turned", bufs=2)
+            for t in range(PACK):
+                nc.tensor.transpose(turned[g][:, t, :], relu[:, t, :], ident[:])
+            if g < 8 and g % 4 < 2:
+                multiply(g + 2, (3, 0, 1, 2))
+
+        def square(g):
+            cols = slice(g * GROUP, (g + 1) * GROUP)
+            nc.scalar.activation(h_bf[:, cols, :], turned[g][:].rearrange("p t j -> p j t"), ACT.Square)
 
         def quantise_h(j0, n):
             cols = slice(h_place[j0], h_place[j0] + n)
@@ -200,81 +226,67 @@ def tile_moe_pre_mlp_relu2_kernel(
                     stop=True,
                 )
 
-        def keep_result(j0, n, bank):
-            nc.vector.tensor_copy(y_sb[:, j0:j0 + n], bank[:, :n])
+        jobs = []
 
-        acc = {}
-        complete = []
+        def finish(groups):
+            for g in groups:
+                jobs.append((rectify, g))
+                if g > groups[0]:
+                    jobs.append((square, g - 1))
+            jobs.append((square, groups[-1]))
 
-        def multiply(j0, n, s0, count, base):
-            for g in range(j0 // GROUP, (j0 + n) // GROUP):
-                if s0 == 0:
-                    acc[g] = psum.tile([P, H], F32, name="acc", bufs=4)
-                for s in range(s0, s0 + count):
-                    first_pass(g, s, base + (s - s0) * n + g * GROUP - j0, acc[g])
-                if s0 + count == PASSES:
-                    complete.append(g)
+        def run_jobs(count):
+            for job, g in jobs[:count]:
+                job(g)
+            jobs[:count] = []
 
-        def activate(count):
-            for g in complete[:count]:
-                hidden(g, acc[g])
-            complete[:count] = []
-
-        waiting = None
-        step = 0
-        for b, (j0, n, s0, count) in enumerate(BATCHES):
-            rounded = stage.tile([P, count, n, PACK], BF16, name="rounded", align_bytes=64, bufs=3)
-            for s in range(s0, s0 + count):
-                gather(step, s, j0, n, rounded[:, s - s0, :, :])
-                budget = {512: 2, 256: 1, 128: 1 - step % 2}[n]
-                if waiting is None:
-                    activate(budget)
-                elif waiting[2] + waiting[3] == PASSES:
-                    quantise_x(*waiting)
-                    multiply(*waiting[:5])
-                    activate(budget)
-                else:
-                    quantise_x(*waiting)
-                    activate(budget)
-                    multiply(*waiting[:5])
-                waiting = None
-                step += 1
-            waiting = (j0, n, s0, count, x_place[b], rounded)
-        y_banks = [psum.tile([P, WIDEST], F32, name="y_bank", bufs=2) for u in range(2)]
+        for step in range(len(STEPS)):
+            gather(step)
+            weave(step)
+            if step == 0:
+                continue
+            quantise_x(step - 1)
+            j0, n, s = STEPS[step - 1]
+            groups = range(j0 // GROUP, (j0 + n) // GROUP)
+            if s == PASSES - 1 and n > GROUP:
+                for g in groups[:2]:
+                    multiply(g, (3, 0, 1, 2) if g < 8 else (3,))
+                finish(list(range(j0 // GROUP, (j0 + n) // GROUP)))
+                run_jobs(4 if step < 8 else 3)
+            else:
+                run_jobs(4 if step < 8 else 2)
+                for g in groups:
+                    if g >= 8 and s >= 2:
+                        multiply(g, (2, 0, 1) if s == 2 else (3,))
+        y_banks = [psum.tile([P, WIDEST], F32, name="y_bank%d" % u) for u in range(4)]
         quantise_h(0, WIDEST)
-        quantise_x(*waiting)
-        multiply(*waiting[:5])
-        activate(len(complete))
+        quantise_x(last)
+        multiply(GROUPS - 1, (3,))
+        finish([GROUPS - 2, GROUPS - 1])
+        run_jobs(len(jobs))
         second_layer(0, WIDEST, y_banks[0], 0)
         quantise_h(WIDEST, WIDEST)
         second_layer(WIDEST, WIDEST, y_banks[1], 0)
-        y_banks.extend(psum.tile([P, H], F32, name="acc", bufs=4) for u in range(2))
+        nc.vector.tensor_copy(y_sb[:, :WIDEST], y_banks[0][:])
         quantise_h(2 * WIDEST, C)
         second_layer(2 * WIDEST, C, y_banks[2], 0)
-        keep_result(0, WIDEST, y_banks[0])
-        keep_result(WIDEST, WIDEST, y_banks[1])
+        nc.vector.tensor_copy(y_sb[:, WIDEST:2 * WIDEST], y_banks[1][:])
         quantise_h(SLOTS - C, GROUP)
         second_layer(SLOTS - C, GROUP, y_banks[2], C)
         quantise_h(SLOTS - GROUP, GROUP)
         second_layer(SLOTS - GROUP, GROUP, y_banks[3], 0)
-        keep_result(2 * WIDEST, C + GROUP, y_banks[2])
-        keep_result(SLOTS - GROUP, GROUP, y_banks[3])
+        nc.scalar.copy(y_sb[:, 2 * WIDEST:SLOTS - GROUP], y_banks[2][:, :C + GROUP])
+        nc.vector.tensor_copy(y_sb[:, SLOTS - GROUP:], y_banks[3][:, :GROUP])
 
         half = T // 2
-        fetched = [keep.tile([P, T], F32, name="fetched%d" % r) for r in range(3)]
-        pair = keep.tile([P, T], F32, name="pair")
-        total = keep.tile([P, T], F32, name="total")
-
-        def fetch(r, t0, t1):
-            nc.vector.tensor_copy(fetched[r][:, t0:t1], y_sb[:].indirect(pos_sb[r][:, t0 // 16:t1 // 16]))
-
-        fetch(0, 0, T)
-        fetch(1, 0, T)
-        for t0 in (0, half):
-            cols = slice(t0, t0 + half)
-            nc.gpsimd.tensor_tensor(pair[:, cols], fetched[0][:, cols], fetched[1][:, cols], ADD)
-            fetch(2, t0, t0 + half)
-        for t0 in (0, half):
-            cols = slice(t0, t0 + half)
-            nc.vector.tensor_tensor(total[:, cols], pair[:, cols], fetched[2][:, cols], ADD)
-            nc.sync.dma_start(out=out[:, cols], in_=total[:, cols])
+        sums = [keep.tile([P, T], F32, name="sums%d" % r) for r in range(3)]
+        for r in range(3):
+            for t0 in (0, half):
+                cols = slice(t0, t0 + half)
+                fetched = y_sb[:].indirect(pos_sb[r][:, t0 // 16:(t0 + half) // 16])
+                if r == 0:
+                    nc.vector.tensor_copy(sums[0][:, cols], fetched)
+                else:
+                    nc.vector.tensor_tensor(sums[r][:, cols], fetched, sums[r - 1][:, cols], ADD)
+        nc.sync.dma_start(out=out[:, :half], in_=sums[2][:, :half])
+        nc.scalar.dma_start(out=out[:, half:], in_=sums[2][:, half:])

@@ -26,9 +26,8 @@ K_PASS = P * PACK
 PASSES = K // K_PASS
 GROUP = 128
 GROUPS = SLOTS // GROUP
-WINDOW = T + 32
 WIDEST = 512
-STEPS = [(j0, WIDEST, s) for s in (0, 1) for j0 in (0, WIDEST)]
+STEPS = [(0, 2 * WIDEST, s) for s in (0, 1)]
 STEPS = STEPS + [(j0, WIDEST, s) for j0 in (0, WIDEST) for s in (2, 3)] + [(2 * WIDEST, WIDEST, 0)]
 STEPS = STEPS + [(2 * WIDEST, C, s) for s in (1, 2, 3)] + [(SLOTS - C, C, s) for s in (1, 2)]
 STEPS = STEPS + [(SLOTS - C, GROUP, 3), (SLOTS - GROUP, GROUP, 3)]
@@ -46,7 +45,8 @@ def tile_moe_pre_mlp_relu2_kernel(
         offs_sb = keep.tile([P, SLOTS // 16], U16, name="offs_sb")
         pos_sb = [keep.tile([P, T // 16], U16, name="pos_sb%d" % r) for r in range(3)]
         gate_sb = keep.tile([P, SLOTS], F32, name="gate_sb")
-        x_sb = [keep.tile([P, WINDOW], F32, name="x_sb%d" % b) for b in range(PASSES * PACK)]
+        window = [max(n for j0, n, s0 in STEPS if s0 == s) + 16 for s in range(PASSES)]
+        x_sb = [keep.tile([P, window[b // PACK]], F32, name="x_sb%d" % b) for b in range(PASSES * PACK)]
         w1_sb = [keep.tile([P, PASSES, 2 * H], U8, name="w1_sb%d" % e, align_bytes=64) for e in range(E)]
         w1_sc = [keep.tile([P, 2 * PASSES, H], U8, name="w1_sc%d" % u, align_bytes=64) for u in range(E // 2)]
         w2_sb = keep.tile([P, E, 2 * N], U8, name="w2_sb", align_bytes=64)
@@ -56,20 +56,13 @@ def tile_moe_pre_mlp_relu2_kernel(
         h_bf = keep.tile([P, SLOTS, PACK], BF16, name="h_bf", align_bytes=64)
         y_sb = keep.tile([P, SLOTS], F32, name="y_sb")
         ident = keep.tile([P, P], F32, name="ident")
-        big = PACK * WIDEST
-        ring = keep.tile([P, 2 * big], F32, name="ring")
+        big = PACK * STEPS[0][1]
+        ring = keep.tile([P, big + PACK * STEPS[1][1]], F32, name="ring")
 
         def load_x(b):
             s, t = divmod(b, PACK)
-            row = K_PASS * s + t
-            base = min(row, K - K_PASS)
-            rows = xT[base:base + K_PASS, :].rearrange("(p j) w -> p (j w)", j=PACK)
-            col = (row - base) * T
-            if col + WINDOW <= PACK * T:
-                nc.sync.dma_start(out=x_sb[b][:], in_=rows[:, col:col + WINDOW])
-            else:
-                nc.sync.dma_start(out=x_sb[b][:, :T], in_=rows[:, col:col + T])
-                nc.sync.dma_start(out=x_sb[b][:, T:], in_=rows[:, :WINDOW - T])
+            rows = xT[K_PASS * s:K_PASS * (s + 1), :].rearrange("(p j) w -> p j w", j=PACK)
+            nc.sync.dma_start(out=x_sb[b][:, :T], in_=rows[:, t, :])
 
         def load_w1_scales(u):
             src = w1_scales[2 * u:2 * u + 2].rearrange("e s (q r) i -> r q (e s) i", r=4)
@@ -81,34 +74,34 @@ def tile_moe_pre_mlp_relu2_kernel(
                 out=w1_sb[e][:].bitcast(I32), in_=w1_words[e].rearrange("s p b -> p s b").bitcast(I32)
             )
 
-        nc.gpsimd.memset(w1_sc[0][:].bitcast(I32), 0)
         make_identity(nc, ident[:])
-        for u in range(1, E // 2):
-            nc.gpsimd.memset(w1_sc[u][:].bitcast(I32), 0)
+        nc.vector.memset(w1_sc[0][:].bitcast(I32), 0)
+        nc.vector.memset(w1_sc[1][:].bitcast(I32), 0)
+        nc.gpsimd.memset(w1_sc[2][:].bitcast(I32), 0)
         nc.gpsimd.memset(w2_sc[:].bitcast(I32), 0)
 
-        first = WIDEST
+        cuts = [0, GROUP, 5 * GROUP, STEPS[0][1]]
         load_x(0)
         nc.sync.dma_start(offs_sb[:], offs)
-        nc.sync.dma_start(out=gate_sb[:, :first], in_=gate[:P, :first])
+        for j0, j1 in zip(cuts, cuts[1:]):
+            nc.sync.dma_start(out=gate_sb[:, j0:j1], in_=gate[:P, j0:j1])
         for b in range(1, PASSES * PACK):
             load_x(b)
-            if b == PACK - 1:
-                nc.sync.dma_start(out=gate_sb[:, first:2 * first], in_=gate[:P, first:2 * first])
-            if b == 2 * PACK - 1:
+            if b == 2 * PACK + 1:
                 load_w1_scales(0)
+            if b == 3 * PACK:
                 load_w1(0)
-                load_w1(1)
+        load_w1(1)
+        nc.sync.dma_start(out=gate_sb[:, cuts[-1]:], in_=gate[:P, cuts[-1]:])
         load_w1_scales(1)
         load_w1(2)
         load_w1(3)
-        nc.sync.dma_start(out=gate_sb[:, 2 * first:], in_=gate[:P, 2 * first:])
         load_w1_scales(2)
+        load_w1(4)
+        load_w1(5)
         w2_src = w2_scales.rearrange("e s (q r) n -> r q (e s) n", r=4)
         for r in range(4):
             nc.sync.dma_start(out=w2_sc[r:P:32, :, :].bitcast(I32), in_=w2_src[r].bitcast(I32))
-        load_w1(4)
-        load_w1(5)
         nc.sync.dma_start(
             out=w2_sb[:].bitcast(I32), in_=w2_words.rearrange("e s p b -> p (e s) b").bitcast(I32)
         )
@@ -125,64 +118,68 @@ def tile_moe_pre_mlp_relu2_kernel(
         def gather(step):
             j0, n, s = STEPS[step]
             for t in range(PACK):
-                nc.vector.tensor_tensor(
-                    picked(step)[:, t, :],
-                    x_sb[PACK * s + t][:].indirect(offs_sb[:, j0 // 16:(j0 + n) // 16]),
-                    gate_sb[:, j0:j0 + n],
-                    MULT,
-                )
+                ends = cuts if step == 0 and t == 0 else [j0, j0 + n]
+                for a, b in zip(ends, ends[1:]):
+                    nc.vector.tensor_tensor(
+                        picked(step)[:, t, a - j0:b - j0],
+                        x_sb[PACK * s + t][:].indirect(offs_sb[:, a // 16:b // 16]),
+                        gate_sb[:, a:b],
+                        MULT,
+                    )
+
+        def pieces(step):
+            j0, n, s = STEPS[step]
+            return [(j, min(n, WIDEST), s) for j in range(j0, j0 + n, WIDEST)]
 
         def weave(step):
-            n = STEPS[step][1]
-            rounded[step] = stage.tile([P, n, PACK], BF16, name="rounded", align_bytes=64, bufs=3)
-            nc.scalar.copy(
-                out=rounded[step][:].rearrange("p (c i) t -> p c t i", i=4),
-                in_=picked(step).rearrange("p t (c i) -> p c t i", i=4),
-            )
+            for j, n, s in pieces(step):
+                rounded[j, s] = stage.tile([P, n, PACK], BF16, name="rounded", align_bytes=64, bufs=5)
+                a = j - STEPS[step][0]
+                nc.scalar.copy(
+                    out=rounded[j, s][:].rearrange("p (c i) t -> p c t i", i=4),
+                    in_=picked(step)[:, :, a:a + n].rearrange("p t (c i) -> p c t i", i=4),
+                )
 
         last = len(STEPS) - 1
-        memory_order = [0, last - 2, 2, 4, last - 1, 1, 3] + list(range(5, last - 2)) + [last]
+        ahead = [(0, WIDEST, 0), STEPS[last - 2], (0, WIDEST, 1), (0, WIDEST, 2), STEPS[last - 1], (0, WIDEST, 3)]
         x_place, end = {}, 0
-        for b in memory_order:
-            x_place[b] = end
-            end += STEPS[b][1]
+        for j, n, s in ahead + [u for step in range(last + 1) for u in pieces(step) if u not in ahead]:
+            for g in range(n // GROUP):
+                x_place[j // GROUP + g, s] = end + g * GROUP
+            end += n
         h_place = {
-            0: x_place[last - 2] + GROUP - WIDEST,
-            WIDEST: x_place[last - 2] + GROUP,
-            2 * WIDEST: x_place[last - 1] + GROUP - C,
-            SLOTS - C: x_place[5],
-            SLOTS - GROUP: x_place[5] + GROUP,
+            0: x_place[GROUPS - 2, 2] - GROUP,
+            C: x_place[GROUPS - 1, 2],
+            WIDEST: x_place[GROUPS - 2, 3] + GROUP - WIDEST,
+            2 * WIDEST: x_place[2, 3],
+            SLOTS - C: x_place[0, 3],
+            SLOTS - GROUP: x_place[1, 3],
         }
 
         acc = {}
 
         def quantise_x(step):
-            j0, n, s = STEPS[step]
-            base = x_place[step]
-            nc.vector.quantize_mx(
-                out=x_codes[:, base:base + n].bitcast(FP8X4),
-                scales=x_sc[:, base:base + n],
-                in_=rounded[step][:].rearrange("p j t -> p (j t)"),
-            )
-
-        def codes_of(g, s):
-            for step, (j0, n, s0) in enumerate(STEPS):
-                if s0 == s and j0 <= g * GROUP < j0 + n:
-                    return x_place[step] + g * GROUP - j0
+            for j, n, s in pieces(step):
+                base = x_place[j // GROUP, s]
+                nc.vector.quantize_mx(
+                    out=x_codes[:, base:base + n].bitcast(FP8X4),
+                    scales=x_sc[:, base:base + n],
+                    in_=rounded[j, s][:].rearrange("p j t -> p (j t)"),
+                )
 
         def multiply(g, passes):
             for s in passes:
                 if g not in acc:
                     acc[g] = psum.tile([P, H], F32, name="acc", bufs=2)
                 e = g * GROUP // C
-                cols = slice(codes_of(g, s), codes_of(g, s) + GROUP)
+                cols = slice(x_place[g, s], x_place[g, s] + GROUP)
                 nc.tensor.matmul_mx(
                     out=acc[g][:],
                     lhsT=x_codes[:, cols].bitcast(FP8X4),
                     lhsT_scale=x_sc[:, cols],
                     rhs=w1_sb[e][:, s, :].bitcast(FP4X4),
                     rhs_scale=w1_sc[e // 2][:, e % 2 * PASSES + s, :],
-                    start=(s == (3 if g < 8 else 2)),
+                    start=(s == (3 if g < 8 else 2 if g < 10 else 1)),
                     stop=(s == (2 if g < 8 else 3)),
                 )
 
@@ -252,19 +249,23 @@ def tile_moe_pre_mlp_relu2_kernel(
                 for g in groups[:2]:
                     multiply(g, (3, 0, 1, 2) if g < 8 else (3,))
                 finish(list(range(j0 // GROUP, (j0 + n) // GROUP)))
-                run_jobs(4 if step < 8 else 3)
+                run_jobs({0: 4, WIDEST: 3}.get(j0, 2))
             else:
-                run_jobs(4 if step < 8 else 2)
+                run_jobs(4 if STEPS[step][1] == WIDEST else 2 if step < last - 2 else 1 if step == last - 2 else 0)
                 for g in groups:
-                    if g >= 8 and s >= 2:
-                        multiply(g, (2, 0, 1) if s == 2 else (3,))
+                    if g >= 10 and s >= 1:
+                        multiply(g, (1, 0) if s == 1 else (s,))
+                    elif g >= 8 and s == 2:
+                        multiply(g, (2, 0, 1))
         y_banks = [psum.tile([P, WIDEST], F32, name="y_bank%d" % u) for u in range(4)]
-        quantise_h(0, WIDEST)
+        quantise_h(0, C)
+        quantise_h(C, C)
         quantise_x(last)
         multiply(GROUPS - 1, (3,))
         finish([GROUPS - 2, GROUPS - 1])
         run_jobs(len(jobs))
-        second_layer(0, WIDEST, y_banks[0], 0)
+        second_layer(0, C, y_banks[0], 0)
+        second_layer(C, C, y_banks[0], C)
         quantise_h(WIDEST, WIDEST)
         second_layer(WIDEST, WIDEST, y_banks[1], 0)
         nc.vector.tensor_copy(y_sb[:, :WIDEST], y_banks[0][:])

@@ -135,10 +135,18 @@ def tile_moe_pre_mlp_relu2_kernel(
             for j, n, s in pieces(step):
                 rounded[j, s] = stage.tile([P, n, PACK], BF16, name="rounded", align_bytes=64, bufs=5)
                 a = j - STEPS[step][0]
+                m = n // 2 if step == len(STEPS) - 1 else n
                 nc.scalar.copy(
-                    out=rounded[j, s][:].rearrange("p (c i) t -> p c t i", i=4),
-                    in_=picked(step)[:, :, a:a + n].rearrange("p t (c i) -> p c t i", i=4),
+                    out=rounded[j, s][:, :m, :].rearrange("p (c i) t -> p c t i", i=4),
+                    in_=picked(step)[:, :, a:a + m].rearrange("p t (c i) -> p c t i", i=4),
                 )
+
+        def weave_rest(step):
+            j, n, s = STEPS[step]
+            nc.vector.tensor_copy(
+                out=rounded[j, s][:, n // 2:, :].rearrange("p (c i) t -> p c t i", i=4),
+                in_=picked(step)[:, :, n // 2:].rearrange("p t (c i) -> p c t i", i=4),
+            )
 
         last = len(STEPS) - 1
         ahead = [(0, WIDEST, 0), STEPS[last - 2], (0, WIDEST, 1), (0, WIDEST, 2), STEPS[last - 1], (0, WIDEST, 3)]
@@ -258,12 +266,13 @@ def tile_moe_pre_mlp_relu2_kernel(
                     elif g >= 8 and s == 2:
                         multiply(g, (2, 0, 1))
         y_banks = [psum.tile([P, WIDEST], F32, name="y_bank%d" % u) for u in range(4)]
+        weave_rest(last)
         quantise_h(0, C)
-        quantise_h(C, C)
         quantise_x(last)
         multiply(GROUPS - 1, (3,))
         finish([GROUPS - 2, GROUPS - 1])
         run_jobs(len(jobs))
+        quantise_h(C, C)
         second_layer(0, C, y_banks[0], 0)
         second_layer(C, C, y_banks[0], C)
         quantise_h(WIDEST, WIDEST)
@@ -282,12 +291,13 @@ def tile_moe_pre_mlp_relu2_kernel(
         half = T // 2
         sums = [keep.tile([P, T], F32, name="sums%d" % r) for r in range(3)]
         for r in range(3):
-            for t0 in (0, half):
-                cols = slice(t0, t0 + half)
-                fetched = y_sb[:].indirect(pos_sb[r][:, t0 // 16:(t0 + half) // 16])
+            ends = (0, half, T) if r < 2 else (0, half, T - GROUP, T)
+            for t0, t1 in zip(ends, ends[1:]):
+                fetched = y_sb[:].indirect(pos_sb[r][:, t0 // 16:t1 // 16])
                 if r == 0:
-                    nc.vector.tensor_copy(sums[0][:, cols], fetched)
+                    nc.vector.tensor_copy(sums[0][:, t0:t1], fetched)
                 else:
-                    nc.vector.tensor_tensor(sums[r][:, cols], fetched, sums[r - 1][:, cols], ADD)
+                    nc.vector.tensor_tensor(sums[r][:, t0:t1], fetched, sums[r - 1][:, t0:t1], ADD)
         nc.sync.dma_start(out=out[:, :half], in_=sums[2][:, :half])
-        nc.scalar.dma_start(out=out[:, half:], in_=sums[2][:, half:])
+        nc.scalar.dma_start(out=out[:, half:T - GROUP], in_=sums[2][:, half:T - GROUP])
+        nc.sync.dma_start(out=out[:, T - GROUP:], in_=sums[2][:, T - GROUP:])

@@ -27,8 +27,8 @@ PASSES = K // K_PASS
 GROUP = 128
 GROUPS = SLOTS // GROUP
 WIDEST = 512
-STEPS = [(0, 2 * WIDEST, s) for s in (0, 1)]
-STEPS = STEPS + [(j0, WIDEST, s) for j0 in (0, WIDEST) for s in (2, 3)] + [(2 * WIDEST, WIDEST, 0)]
+STEPS = [(0, SLOTS, 0), (0, 2 * WIDEST, 1)]
+STEPS = STEPS + [(j0, WIDEST, s) for j0 in (0, WIDEST) for s in (2, 3)]
 STEPS = STEPS + [(2 * WIDEST, C, s) for s in (1, 2, 3)] + [(SLOTS - C, C, s) for s in (1, 2)]
 STEPS = STEPS + [(SLOTS - C, GROUP, 3), (SLOTS - GROUP, GROUP, 3)]
 
@@ -92,7 +92,6 @@ def tile_moe_pre_mlp_relu2_kernel(
             if b == 3 * PACK:
                 load_w1(0)
         load_w1(1)
-        nc.sync.dma_start(out=gate_sb[:, cuts[-1]:], in_=gate[:P, cuts[-1]:])
         load_w1_scales(1)
         load_w1(2)
         load_w1(3)
@@ -164,7 +163,8 @@ def tile_moe_pre_mlp_relu2_kernel(
             SLOTS - GROUP: x_place[1, 3],
         }
 
-        acc = {}
+        banks = [psum.tile([P, H], F32, name="bank%d" % u) for u in range(8)]
+        acc = [banks[4 + g % 4] if g < 8 else banks[g % 2] for g in range(GROUPS)]
 
         def quantise_x(step):
             for j, n, s in pieces(step):
@@ -177,8 +177,6 @@ def tile_moe_pre_mlp_relu2_kernel(
 
         def multiply(g, passes):
             for s in passes:
-                if g not in acc:
-                    acc[g] = psum.tile([P, H], F32, name="acc", bufs=2)
                 e = g * GROUP // C
                 cols = slice(x_place[g, s], x_place[g, s] + GROUP)
                 nc.tensor.matmul_mx(
@@ -187,8 +185,8 @@ def tile_moe_pre_mlp_relu2_kernel(
                     lhsT_scale=x_sc[:, cols],
                     rhs=w1_sb[e][:, s, :].bitcast(FP4X4),
                     rhs_scale=w1_sc[e // 2][:, e % 2 * PASSES + s, :],
-                    start=(s == (3 if g < 8 else 2 if g < 10 else 1)),
-                    stop=(s == (2 if g < 8 else 3)),
+                    start=(s == (2 if g < 10 else 1)),
+                    stop=(s == 3),
                 )
 
         turned = {}
@@ -199,15 +197,13 @@ def tile_moe_pre_mlp_relu2_kernel(
             part = 2 if g == GROUPS - 1 else PACK
             for t in range(0, PACK, part):
                 nc.scalar.activation(relu[:, t:t + part, :], planes[:, t:t + part, :], ACT.Relu)
-            turned[g] = psum.tile([P, PACK, GROUP], F32, name="turned", bufs=2)
+            turned[g] = banks[2 + g % 2][:].rearrange("p (t j) -> p t j", t=PACK)
             for t in range(PACK):
                 nc.tensor.transpose(turned[g][:, t, :], relu[:, t, :], ident[:])
-            if g < 8 and g % 4 < 2:
-                multiply(g + 2, (3, 0, 1, 2))
 
         def square(g):
             cols = slice(g * GROUP, (g + 1) * GROUP)
-            nc.scalar.activation(h_bf[:, cols, :], turned[g][:].rearrange("p t j -> p j t"), ACT.Square)
+            nc.scalar.activation(h_bf[:, cols, :], turned[g].rearrange("p t j -> p j t"), ACT.Square)
 
         def quantise_h(j0, n):
             cols = slice(h_place[j0], h_place[j0] + n)
@@ -254,18 +250,18 @@ def tile_moe_pre_mlp_relu2_kernel(
             j0, n, s = STEPS[step - 1]
             groups = range(j0 // GROUP, (j0 + n) // GROUP)
             if s == PASSES - 1 and n > GROUP:
-                for g in groups[:2]:
-                    multiply(g, (3, 0, 1, 2) if g < 8 else (3,))
+                for g in groups:
+                    multiply(g, (3,))
                 finish(list(range(j0 // GROUP, (j0 + n) // GROUP)))
-                run_jobs({0: 4, WIDEST: 3}.get(j0, 2))
+                run_jobs({0: 5, WIDEST: 3}.get(j0, 2))
             else:
-                run_jobs(4 if STEPS[step][1] == WIDEST else 2 if step < last - 2 else 1 if step == last - 2 else 0)
+                run_jobs(3 if step < last - 2 else 1 if step == last - 2 else 0)
                 for g in groups:
                     if g >= 10 and s >= 1:
                         multiply(g, (1, 0) if s == 1 else (s,))
-                    elif g >= 8 and s == 2:
+                    elif s == 2:
                         multiply(g, (2, 0, 1))
-        y_banks = [psum.tile([P, WIDEST], F32, name="y_bank%d" % u) for u in range(4)]
+        y_banks = banks[4:]
         weave_rest(last)
         quantise_h(0, C)
         quantise_x(last)
@@ -286,7 +282,7 @@ def tile_moe_pre_mlp_relu2_kernel(
         quantise_h(SLOTS - GROUP, GROUP)
         second_layer(SLOTS - GROUP, GROUP, y_banks[3], 0)
         nc.scalar.copy(y_sb[:, 2 * WIDEST:SLOTS - GROUP], y_banks[2][:, :C + GROUP])
-        nc.vector.tensor_copy(y_sb[:, SLOTS - GROUP:], y_banks[3][:, :GROUP])
+        nc.scalar.copy(y_sb[:, SLOTS - GROUP:], y_banks[3][:, :GROUP])
 
         half = T // 2
         sums = [keep.tile([P, T], F32, name="sums%d" % r) for r in range(3)]

@@ -24,13 +24,26 @@ P = 128
 PACK = 4
 K_PASS = P * PACK
 PASSES = K // K_PASS
+LAST_PASS = PASSES - 1
+PER_COLUMN = 16
+RUN = 4
 GROUP = 128
 GROUPS = SLOTS // GROUP
-WIDEST = 512
-STEPS = [(0, SLOTS, 0), (0, 2 * WIDEST, 1)]
-STEPS = STEPS + [(j0, WIDEST, s) for j0 in (0, WIDEST) for s in (2, 3)]
-STEPS = STEPS + [(2 * WIDEST, C, s) for s in (1, 2, 3)] + [(SLOTS - C, C, s) for s in (1, 2)]
-STEPS = STEPS + [(SLOTS - C, GROUP, 3), (SLOTS - GROUP, GROUP, 3)]
+BLOCK = 512
+WIDE_GROUPS = 2 * BLOCK // GROUP
+PAIR = SLOTS - C
+PAIR_A, PAIR_B = GROUPS - 2, GROUPS - 1
+
+STEPS = [(0, 2 * BLOCK, s) for s in (0, 1)]
+STEPS = STEPS + [(j0, BLOCK, s) for j0 in (0, BLOCK) for s in (2, 3)] + [(2 * BLOCK, BLOCK, 0)]
+STEPS = STEPS + [(2 * BLOCK, C, s) for s in (1, 2, 3)] + [(PAIR, C, s) for s in (1, 2)]
+STEPS = STEPS + [(PAIR, GROUP, LAST_PASS), (PAIR + GROUP, GROUP, LAST_PASS)]
+LAST = len(STEPS) - 1
+
+FIRST_CUTS = [0, GROUP, GROUP + BLOCK, STEPS[0][1]]
+
+JOBS_AT_END = {0: 5, BLOCK: 3, 2 * BLOCK: 2}
+JOBS = [3] * (LAST - 2) + [1, 0, 0]
 
 
 def tile_moe_pre_mlp_relu2_kernel(
@@ -42,32 +55,37 @@ def tile_moe_pre_mlp_relu2_kernel(
         stage = ctx.enter_context(tc.tile_pool(name="stage", bufs=3))
         psum = ctx.enter_context(tc.psum_pool(name="psum", bufs=1))
 
-        offs_sb = keep.tile([P, SLOTS // 16], U16, name="offs_sb")
-        pos_sb = [keep.tile([P, T // 16], U16, name="pos_sb%d" % r) for r in range(3)]
+        offs_sb = keep.tile([P, SLOTS // PER_COLUMN], U16, name="offs_sb")
+        pos_sb = [keep.tile([P, T // PER_COLUMN], U16, name="pos_sb%d" % r) for r in range(3)]
         gate_sb = keep.tile([P, SLOTS], F32, name="gate_sb")
-        window = [max(n for j0, n, s0 in STEPS if s0 == s) + 16 for s in range(PASSES)]
+        window = [max(n for j0, n, s0 in STEPS if s0 == s) + PER_COLUMN for s in range(PASSES)]
         x_sb = [keep.tile([P, window[b // PACK]], F32, name="x_sb%d" % b) for b in range(PASSES * PACK)]
         w1_sb = [keep.tile([P, PASSES, 2 * H], U8, name="w1_sb%d" % e, align_bytes=64) for e in range(E)]
         w1_sc = [keep.tile([P, 2 * PASSES, H], U8, name="w1_sc%d" % u, align_bytes=64) for u in range(E // 2)]
         w2_sb = keep.tile([P, E, 2 * N], U8, name="w2_sb", align_bytes=64)
         w2_sc = keep.tile([P, E, N], U8, name="w2_sc", align_bytes=64)
-        x_codes = keep.tile([P, PASSES * SLOTS], U32, name="x_codes", align_bytes=64)
-        x_sc = keep.tile([P, PASSES * SLOTS], U8, name="x_sc", align_bytes=64)
+        codes = keep.tile([P, PASSES * SLOTS], U32, name="codes", align_bytes=64)
+        scales = keep.tile([P, PASSES * SLOTS], U8, name="scales", align_bytes=64)
         h_bf = keep.tile([P, SLOTS, PACK], BF16, name="h_bf", align_bytes=64)
         y_sb = keep.tile([P, SLOTS], F32, name="y_sb")
         ident = keep.tile([P, P], F32, name="ident")
-        big = PACK * STEPS[0][1]
-        ring = keep.tile([P, big + PACK * STEPS[1][1]], F32, name="ring")
+        ring_half = PACK * STEPS[0][1]
+        ring = keep.tile([P, 2 * ring_half], F32, name="ring")
 
         def load_x(b):
             s, t = divmod(b, PACK)
             rows = xT[K_PASS * s:K_PASS * (s + 1), :].rearrange("(p j) w -> p j w", j=PACK)
             nc.sync.dma_start(out=x_sb[b][:, :T], in_=rows[:, t, :])
 
-        def load_w1_scales(u):
-            src = w1_scales[2 * u:2 * u + 2].rearrange("e s (q r) i -> r q (e s) i", r=4)
+        def load_gate(j0, j1):
+            nc.sync.dma_start(out=gate_sb[:, j0:j1], in_=gate[:P, j0:j1])
+
+        def load_scale_rows(tile, src):
             for r in range(4):
-                nc.sync.dma_start(out=w1_sc[u][r:P:32, :, :].bitcast(I32), in_=src[r].bitcast(I32))
+                nc.sync.dma_start(out=tile[r:P:32, :, :].bitcast(I32), in_=src[r].bitcast(I32))
+
+        def load_w1_scales(u):
+            load_scale_rows(w1_sc[u], w1_scales[2 * u:2 * u + 2].rearrange("e s (q r) i -> r q (e s) i", r=4))
 
         def load_w1(e):
             nc.sync.dma_start(
@@ -80,124 +98,117 @@ def tile_moe_pre_mlp_relu2_kernel(
         nc.gpsimd.memset(w1_sc[2][:].bitcast(I32), 0)
         nc.gpsimd.memset(w2_sc[:].bitcast(I32), 0)
 
-        cuts = [0, GROUP, 5 * GROUP, STEPS[0][1]]
         load_x(0)
         nc.sync.dma_start(offs_sb[:], offs)
-        for j0, j1 in zip(cuts, cuts[1:]):
-            nc.sync.dma_start(out=gate_sb[:, j0:j1], in_=gate[:P, j0:j1])
+        for j0, j1 in zip(FIRST_CUTS, FIRST_CUTS[1:]):
+            load_gate(j0, j1)
         for b in range(1, PASSES * PACK):
             load_x(b)
             if b == 2 * PACK + 1:
                 load_w1_scales(0)
-            if b == 3 * PACK:
+            if b == LAST_PASS * PACK:
                 load_w1(0)
         load_w1(1)
-        load_w1_scales(1)
-        load_w1(2)
-        load_w1(3)
-        load_w1_scales(2)
-        load_w1(4)
-        load_w1(5)
-        w2_src = w2_scales.rearrange("e s (q r) n -> r q (e s) n", r=4)
-        for r in range(4):
-            nc.sync.dma_start(out=w2_sc[r:P:32, :, :].bitcast(I32), in_=w2_src[r].bitcast(I32))
+        load_gate(FIRST_CUTS[-1], SLOTS)
+        for u in range(1, E // 2):
+            load_w1_scales(u)
+            load_w1(2 * u)
+            load_w1(2 * u + 1)
+        load_scale_rows(w2_sc, w2_scales.rearrange("e s (q r) n -> r q (e s) n", r=4))
         nc.sync.dma_start(
             out=w2_sb[:].bitcast(I32), in_=w2_words.rearrange("e s p b -> p (e s) b").bitcast(I32)
         )
         for tile, pos in zip(pos_sb, (pos1, pos2, pos3)):
             nc.sync.dma_start(tile[:], pos)
 
-        rounded = {}
-
         def picked(step):
-            n = STEPS[step][1]
-            start = (step % 2) * big
-            return ring[:, start:start + PACK * n].rearrange("p (t j) -> p t j", t=PACK)
+            start = step % 2 * ring_half
+            return ring[:, start:start + PACK * STEPS[step][1]].rearrange("p (t j) -> p t j", t=PACK)
 
         def gather(step):
             j0, n, s = STEPS[step]
             for t in range(PACK):
-                ends = cuts if step == 0 and t == 0 else [j0, j0 + n]
-                for a, b in zip(ends, ends[1:]):
+                cuts = FIRST_CUTS if step == 0 and t == 0 else [j0, j0 + n]
+                for a, b in zip(cuts, cuts[1:]):
                     nc.vector.tensor_tensor(
                         picked(step)[:, t, a - j0:b - j0],
-                        x_sb[PACK * s + t][:].indirect(offs_sb[:, a // 16:b // 16]),
+                        x_sb[PACK * s + t][:].indirect(offs_sb[:, a // PER_COLUMN:b // PER_COLUMN]),
                         gate_sb[:, a:b],
                         MULT,
                     )
 
         def pieces(step):
             j0, n, s = STEPS[step]
-            return [(j, min(n, WIDEST), s) for j in range(j0, j0 + n, WIDEST)]
+            return [(j, min(n, BLOCK), s) for j in range(j0, j0 + n, BLOCK)]
+
+        rounded = {}
+
+        def woven(step, j, a, b):
+            s, first = STEPS[step][2], j - STEPS[step][0]
+            return (
+                rounded[j, s][:, a:b, :].rearrange("p (c i) t -> p c t i", i=RUN),
+                picked(step)[:, :, first + a:first + b].rearrange("p t (c i) -> p c t i", i=RUN),
+            )
 
         def weave(step):
             for j, n, s in pieces(step):
                 rounded[j, s] = stage.tile([P, n, PACK], BF16, name="rounded", align_bytes=64, bufs=5)
-                a = j - STEPS[step][0]
-                m = n // 2 if step == len(STEPS) - 1 else n
-                nc.scalar.copy(
-                    out=rounded[j, s][:, :m, :].rearrange("p (c i) t -> p c t i", i=4),
-                    in_=picked(step)[:, :, a:a + m].rearrange("p t (c i) -> p c t i", i=4),
-                )
+                nc.scalar.copy(*woven(step, j, 0, n // 2 if step == LAST else n))
 
-        def weave_rest(step):
-            j, n, s = STEPS[step]
-            nc.vector.tensor_copy(
-                out=rounded[j, s][:, n // 2:, :].rearrange("p (c i) t -> p c t i", i=4),
-                in_=picked(step)[:, :, n // 2:].rearrange("p t (c i) -> p c t i", i=4),
-            )
-
-        last = len(STEPS) - 1
-        ahead = [(0, WIDEST, 0), STEPS[last - 2], (0, WIDEST, 1), (0, WIDEST, 2), STEPS[last - 1], (0, WIDEST, 3)]
+        ahead = [(0, BLOCK, 0), STEPS[LAST - 2], (0, BLOCK, 1), (0, BLOCK, 2), STEPS[LAST - 1], (0, BLOCK, 3)]
         x_place, end = {}, 0
-        for j, n, s in ahead + [u for step in range(last + 1) for u in pieces(step) if u not in ahead]:
+        for j, n, s in ahead + [u for step in range(LAST + 1) for u in pieces(step) if u not in ahead]:
             for g in range(n // GROUP):
                 x_place[j // GROUP + g, s] = end + g * GROUP
             end += n
         h_place = {
-            0: x_place[GROUPS - 2, 2] - GROUP,
-            C: x_place[GROUPS - 1, 2],
-            WIDEST: x_place[GROUPS - 2, 3] + GROUP - WIDEST,
-            2 * WIDEST: x_place[2, 3],
-            SLOTS - C: x_place[0, 3],
-            SLOTS - GROUP: x_place[1, 3],
+            0: x_place[PAIR_A, 2] + GROUP - C,
+            C: x_place[PAIR_B, 2],
+            BLOCK: x_place[PAIR_A, LAST_PASS] + GROUP - BLOCK,
+            2 * BLOCK: x_place[2, LAST_PASS],
+            PAIR: x_place[0, LAST_PASS],
+            PAIR + GROUP: x_place[1, LAST_PASS],
         }
 
         banks = [psum.tile([P, H], F32, name="bank%d" % u) for u in range(8)]
-        acc = [banks[4 + g % 4] if g < 8 else banks[g % 2] for g in range(GROUPS)]
+        acc = [banks[4 + g % 4] if g < WIDE_GROUPS else banks[g % 2] for g in range(GROUPS)]
+        turned = [banks[2 + g % 2][:].rearrange("p (t j) -> p t j", t=PACK) for g in range(GROUPS)]
+        y_banks = banks[4:]
 
         def quantise_x(step):
             for j, n, s in pieces(step):
-                base = x_place[j // GROUP, s]
+                cols = slice(x_place[j // GROUP, s], x_place[j // GROUP, s] + n)
                 nc.vector.quantize_mx(
-                    out=x_codes[:, base:base + n].bitcast(FP8X4),
-                    scales=x_sc[:, base:base + n],
+                    out=codes[:, cols].bitcast(FP8X4),
+                    scales=scales[:, cols],
                     in_=rounded[j, s][:].rearrange("p j t -> p (j t)"),
                 )
 
-        def multiply(g, passes):
-            for s in passes:
-                e = g * GROUP // C
+        def opening(g):
+            return 1 if g >= PAIR_A else 2
+
+        def multiply(g, s0):
+            if s0 < opening(g):
+                return
+            e = g * GROUP // C
+            for s in [s0] + (list(range(s0)) if s0 == opening(g) else []):
                 cols = slice(x_place[g, s], x_place[g, s] + GROUP)
                 nc.tensor.matmul_mx(
                     out=acc[g][:],
-                    lhsT=x_codes[:, cols].bitcast(FP8X4),
-                    lhsT_scale=x_sc[:, cols],
+                    lhsT=codes[:, cols].bitcast(FP8X4),
+                    lhsT_scale=scales[:, cols],
                     rhs=w1_sb[e][:, s, :].bitcast(FP4X4),
                     rhs_scale=w1_sc[e // 2][:, e % 2 * PASSES + s, :],
-                    start=(s == (2 if g < 10 else 1)),
-                    stop=(s == 3),
+                    start=(s == opening(g)),
+                    stop=(s == LAST_PASS),
                 )
-
-        turned = {}
 
         def rectify(g):
             relu = stage.tile([P, PACK, P], F32, name="relu")
             planes = acc[g][:].rearrange("j (p t) -> j t p", t=PACK)
-            part = 2 if g == GROUPS - 1 else PACK
+            part = PACK // 2 if g == PAIR_B else PACK
             for t in range(0, PACK, part):
                 nc.scalar.activation(relu[:, t:t + part, :], planes[:, t:t + part, :], ACT.Relu)
-            turned[g] = banks[2 + g % 2][:].rearrange("p (t j) -> p t j", t=PACK)
             for t in range(PACK):
                 nc.tensor.transpose(turned[g][:, t, :], relu[:, t, :], ident[:])
 
@@ -208,28 +219,28 @@ def tile_moe_pre_mlp_relu2_kernel(
         def quantise_h(j0, n):
             cols = slice(h_place[j0], h_place[j0] + n)
             nc.vector.quantize_mx(
-                out=x_codes[:, cols].bitcast(FP8X4),
-                scales=x_sc[:, cols],
+                out=codes[:, cols].bitcast(FP8X4),
+                scales=scales[:, cols],
                 in_=h_bf[:, j0:j0 + n, :].rearrange("p j t -> p (j t)"),
             )
 
         def second_layer(j0, n, bank, col):
-            for j in range(j0, j0 + n, C):
+            for j in range(0, n, C):
                 width = min(C, n)
-                cols = slice(h_place[j0] + j - j0, h_place[j0] + j - j0 + width)
+                cols = slice(h_place[j0] + j, h_place[j0] + j + width)
                 nc.tensor.matmul_mx(
-                    out=bank[:, col + j - j0:col + j - j0 + width],
-                    lhsT=w2_sb[:, j // C, :].bitcast(FP4X4),
-                    lhsT_scale=w2_sc[:, j // C, :],
-                    rhs=x_codes[:, cols].bitcast(FP8X4),
-                    rhs_scale=x_sc[:, cols],
+                    out=bank[:, col + j:col + j + width],
+                    lhsT=w2_sb[:, (j0 + j) // C, :].bitcast(FP4X4),
+                    lhsT_scale=w2_sc[:, (j0 + j) // C, :],
+                    rhs=codes[:, cols].bitcast(FP8X4),
+                    rhs_scale=scales[:, cols],
                     start=True,
                     stop=True,
                 )
 
         jobs = []
 
-        def finish(groups):
+        def add_jobs(groups):
             for g in groups:
                 jobs.append((rectify, g))
                 if g > groups[0]:
@@ -241,59 +252,55 @@ def tile_moe_pre_mlp_relu2_kernel(
                 job(g)
             jobs[:count] = []
 
-        for step in range(len(STEPS)):
+        gather(0)
+        weave(0)
+        for step in range(1, LAST + 1):
             gather(step)
             weave(step)
-            if step == 0:
-                continue
             quantise_x(step - 1)
             j0, n, s = STEPS[step - 1]
             groups = range(j0 // GROUP, (j0 + n) // GROUP)
-            if s == PASSES - 1 and n > GROUP:
-                for g in groups:
-                    multiply(g, (3,))
-                finish(list(range(j0 // GROUP, (j0 + n) // GROUP)))
-                run_jobs({0: 5, WIDEST: 3}.get(j0, 2))
-            else:
-                run_jobs(3 if step < last - 2 else 1 if step == last - 2 else 0)
-                for g in groups:
-                    if g >= 10 and s >= 1:
-                        multiply(g, (1, 0) if s == 1 else (s,))
-                    elif s == 2:
-                        multiply(g, (2, 0, 1))
-        y_banks = banks[4:]
-        weave_rest(last)
+            ends_groups = s == LAST_PASS and j0 in JOBS_AT_END
+            if not ends_groups:
+                run_jobs(JOBS[step])
+            for g in groups:
+                multiply(g, s)
+            if ends_groups:
+                add_jobs(groups)
+                run_jobs(JOBS_AT_END[j0])
+
+        nc.vector.tensor_copy(*woven(LAST, PAIR + GROUP, GROUP // 2, GROUP))
         quantise_h(0, C)
-        quantise_x(last)
-        multiply(GROUPS - 1, (3,))
-        finish([GROUPS - 2, GROUPS - 1])
+        quantise_x(LAST)
+        multiply(PAIR_B, LAST_PASS)
+        add_jobs([PAIR_A, PAIR_B])
         run_jobs(len(jobs))
         quantise_h(C, C)
         second_layer(0, C, y_banks[0], 0)
         second_layer(C, C, y_banks[0], C)
-        quantise_h(WIDEST, WIDEST)
-        second_layer(WIDEST, WIDEST, y_banks[1], 0)
-        nc.vector.tensor_copy(y_sb[:, :WIDEST], y_banks[0][:])
-        quantise_h(2 * WIDEST, C)
-        second_layer(2 * WIDEST, C, y_banks[2], 0)
-        nc.vector.tensor_copy(y_sb[:, WIDEST:2 * WIDEST], y_banks[1][:])
-        quantise_h(SLOTS - C, GROUP)
-        second_layer(SLOTS - C, GROUP, y_banks[2], C)
-        quantise_h(SLOTS - GROUP, GROUP)
-        second_layer(SLOTS - GROUP, GROUP, y_banks[3], 0)
-        nc.scalar.copy(y_sb[:, 2 * WIDEST:SLOTS - GROUP], y_banks[2][:, :C + GROUP])
-        nc.scalar.copy(y_sb[:, SLOTS - GROUP:], y_banks[3][:, :GROUP])
+        quantise_h(BLOCK, BLOCK)
+        second_layer(BLOCK, BLOCK, y_banks[1], 0)
+        nc.vector.tensor_copy(y_sb[:, :BLOCK], y_banks[0][:])
+        quantise_h(2 * BLOCK, C)
+        second_layer(2 * BLOCK, C, y_banks[2], 0)
+        nc.vector.tensor_copy(y_sb[:, BLOCK:2 * BLOCK], y_banks[1][:])
+        quantise_h(PAIR, GROUP)
+        second_layer(PAIR, GROUP, y_banks[2], C)
+        quantise_h(PAIR + GROUP, GROUP)
+        second_layer(PAIR + GROUP, GROUP, y_banks[3], 0)
+        nc.scalar.copy(y_sb[:, 2 * BLOCK:PAIR + GROUP], y_banks[2][:, :C + GROUP])
+        nc.scalar.copy(y_sb[:, PAIR + GROUP:], y_banks[3][:, :GROUP])
 
         half = T // 2
+        out_cuts = (0, half, half + half // 2, T)
         sums = [keep.tile([P, T], F32, name="sums%d" % r) for r in range(3)]
         for r in range(3):
-            ends = (0, half, T) if r < 2 else (0, half, T - GROUP, T)
-            for t0, t1 in zip(ends, ends[1:]):
-                fetched = y_sb[:].indirect(pos_sb[r][:, t0 // 16:t1 // 16])
+            cuts = (0, half, T) if r < 2 else out_cuts
+            for t0, t1 in zip(cuts, cuts[1:]):
+                fetched = y_sb[:].indirect(pos_sb[r][:, t0 // PER_COLUMN:t1 // PER_COLUMN])
                 if r == 0:
                     nc.vector.tensor_copy(sums[0][:, t0:t1], fetched)
                 else:
                     nc.vector.tensor_tensor(sums[r][:, t0:t1], fetched, sums[r - 1][:, t0:t1], ADD)
-        nc.sync.dma_start(out=out[:, :half], in_=sums[2][:, :half])
-        nc.scalar.dma_start(out=out[:, half:T - GROUP], in_=sums[2][:, half:T - GROUP])
-        nc.sync.dma_start(out=out[:, T - GROUP:], in_=sums[2][:, T - GROUP:])
+        for t0, t1, queue in zip(out_cuts, out_cuts[1:], (nc.sync, nc.scalar, nc.sync)):
+            queue.dma_start(out=out[:, t0:t1], in_=sums[2][:, t0:t1])

@@ -35,15 +35,15 @@ PAIR = SLOTS - C
 PAIR_A, PAIR_B = GROUPS - 2, GROUPS - 1
 
 STEPS = [(0, 2 * BLOCK, s) for s in (0, 1)]
-STEPS = STEPS + [(j0, BLOCK, s) for j0 in (0, BLOCK) for s in (2, 3)] + [(2 * BLOCK, BLOCK, 0)]
-STEPS = STEPS + [(2 * BLOCK, C, s) for s in (1, 2, 3)] + [(PAIR, C, s) for s in (1, 2)]
+STEPS = STEPS + [(j0, BLOCK, s) for j0 in (0, BLOCK) for s in (2, 3)] + [(2 * BLOCK, BLOCK, s) for s in (0, 1)]
+STEPS = STEPS + [(2 * BLOCK, C, s) for s in (2, 3)] + [(PAIR, C, 2)]
 STEPS = STEPS + [(PAIR, GROUP, LAST_PASS), (PAIR + GROUP, GROUP, LAST_PASS)]
 LAST = len(STEPS) - 1
 
 FIRST_CUTS = [0, GROUP, GROUP + BLOCK, STEPS[0][1]]
 
-JOBS_AT_END = {0: 5, BLOCK: 3, 2 * BLOCK: 2}
-JOBS = [3] * (LAST - 2) + [1, 0, 0]
+JOBS_AT_END = {0: 5, BLOCK: 3, 2 * BLOCK: 1}
+JOBS = [3] * (LAST - 1) + [2, 0]
 
 
 def tile_moe_pre_mlp_relu2_kernel(
@@ -139,7 +139,7 @@ def tile_moe_pre_mlp_relu2_kernel(
 
         def pieces(step):
             j0, n, s = STEPS[step]
-            return [(j, min(n, BLOCK), s) for j in range(j0, j0 + n, BLOCK)]
+            return [(j0, n, s)]
 
         rounded = {}
 
@@ -152,10 +152,10 @@ def tile_moe_pre_mlp_relu2_kernel(
 
         def weave(step):
             for j, n, s in pieces(step):
-                rounded[j, s] = stage.tile([P, n, PACK], BF16, name="rounded", align_bytes=64, bufs=5)
+                rounded[j, s] = stage.tile([P, n, PACK], BF16, name="rounded", align_bytes=64, bufs=3)
                 nc.scalar.copy(*woven(step, j, 0, n // 2 if step == LAST else n))
 
-        ahead = [(0, BLOCK, 0), STEPS[LAST - 2], (0, BLOCK, 1), (0, BLOCK, 2), STEPS[LAST - 1], (0, BLOCK, 3)]
+        ahead = [STEPS[0], STEPS[LAST - 2], STEPS[1], STEPS[LAST - 1], (0, BLOCK, 3)]
         x_place, end = {}, 0
         for j, n, s in ahead + [u for step in range(LAST + 1) for u in pieces(step) if u not in ahead]:
             for g in range(n // GROUP):
@@ -171,9 +171,9 @@ def tile_moe_pre_mlp_relu2_kernel(
         }
 
         banks = [psum.tile([P, H], F32, name="bank%d" % u) for u in range(8)]
-        acc = [banks[4 + g % 4] if g < WIDE_GROUPS else banks[g % 2] for g in range(GROUPS)]
+        acc = [banks[4 + g % 4] if g < WIDE_GROUPS or g >= PAIR_A else banks[g % 2] for g in range(GROUPS)]
         turned = [banks[2 + g % 2][:].rearrange("p (t j) -> p t j", t=PACK) for g in range(GROUPS)]
-        y_banks = banks[4:]
+        y_banks = [banks[4], banks[5], banks[0], banks[1]]
 
         def quantise_x(step):
             for j, n, s in pieces(step):

@@ -67,7 +67,7 @@ def tile_moe_pre_mlp_relu2_kernel(
         codes = keep.tile([P, PASSES * SLOTS], U32, name="codes", align_bytes=64)
         scales = keep.tile([P, PASSES * SLOTS], U8, name="scales", align_bytes=64)
         h_bf = keep.tile([P, SLOTS, PACK], BF16, name="h_bf", align_bytes=64)
-        y_sb = keep.tile([P, SLOTS], F32, name="y_sb")
+        y_sb = keep.tile([P, SLOTS], F32, name="y_sb", align_bytes=64)
         ident = keep.tile([P, P], F32, name="ident")
         ring_half = PACK * STEPS[0][1]
         ring = keep.tile([P, 2 * ring_half], F32, name="ring")
@@ -173,7 +173,7 @@ def tile_moe_pre_mlp_relu2_kernel(
         banks = [psum.tile([P, H], F32, name="bank%d" % u) for u in range(8)]
         acc = [banks[4 + g % 4] if g < WIDE_GROUPS or g >= PAIR_A else banks[g % 2] for g in range(GROUPS)]
         turned = [banks[2 + g % 2][:].rearrange("p (t j) -> p t j", t=PACK) for g in range(GROUPS)]
-        y_banks = [banks[4], banks[5], banks[0], banks[1]]
+        y_banks = [banks[4], banks[5], banks[7], banks[1]]
 
         def quantise_x(step):
             for j, n, s in pieces(step):
@@ -208,20 +208,27 @@ def tile_moe_pre_mlp_relu2_kernel(
             planes = acc[g][:].rearrange("j (p t) -> j t p", t=PACK)
             part = PACK // 2 if g == PAIR_B else PACK
             for t in range(0, PACK, part):
-                nc.scalar.activation(relu[:, t:t + part, :], planes[:, t:t + part, :], ACT.Relu)
+                if g == PAIR_A:
+                    nc.vector.tensor_scalar_max(relu[:, t:t + part, :], planes[:, t:t + part, :], 0.0)
+                else:
+                    nc.scalar.activation(relu[:, t:t + part, :], planes[:, t:t + part, :], ACT.Relu)
             for t in range(PACK):
                 nc.tensor.transpose(turned[g][:, t, :], relu[:, t, :], ident[:])
 
+        def h_of(j0, n):
+            if j0 == PAIR + GROUP:
+                return y_sb[:, BLOCK + C:2 * BLOCK].bitcast(BF16).rearrange("p (j t) -> p j t", t=PACK)
+            return h_bf[:, j0:j0 + n, :]
+
         def square(g):
-            cols = slice(g * GROUP, (g + 1) * GROUP)
-            nc.scalar.activation(h_bf[:, cols, :], turned[g].rearrange("p t j -> p j t"), ACT.Square)
+            nc.scalar.activation(h_of(g * GROUP, GROUP), turned[g].rearrange("p t j -> p j t"), ACT.Square)
 
         def quantise_h(j0, n):
             cols = slice(h_place[j0], h_place[j0] + n)
             nc.vector.quantize_mx(
                 out=codes[:, cols].bitcast(FP8X4),
                 scales=scales[:, cols],
-                in_=h_bf[:, j0:j0 + n, :].rearrange("p j t -> p (j t)"),
+                in_=h_of(j0, n).rearrange("p j t -> p (j t)"),
             )
 
         def second_layer(j0, n, bank, col):
@@ -273,9 +280,9 @@ def tile_moe_pre_mlp_relu2_kernel(
         quantise_h(0, C)
         quantise_x(LAST)
         multiply(PAIR_B, LAST_PASS)
+        quantise_h(C, C)
         add_jobs([PAIR_A, PAIR_B])
         run_jobs(len(jobs))
-        quantise_h(C, C)
         second_layer(0, C, y_banks[0], 0)
         second_layer(C, C, y_banks[0], C)
         quantise_h(BLOCK, BLOCK)
@@ -283,11 +290,12 @@ def tile_moe_pre_mlp_relu2_kernel(
         nc.vector.tensor_copy(y_sb[:, :BLOCK], y_banks[0][:])
         quantise_h(2 * BLOCK, C)
         second_layer(2 * BLOCK, C, y_banks[2], 0)
-        nc.vector.tensor_copy(y_sb[:, BLOCK:2 * BLOCK], y_banks[1][:])
+        nc.vector.tensor_copy(y_sb[:, BLOCK:BLOCK + C], y_banks[1][:, :C])
         quantise_h(PAIR, GROUP)
         second_layer(PAIR, GROUP, y_banks[2], C)
         quantise_h(PAIR + GROUP, GROUP)
         second_layer(PAIR + GROUP, GROUP, y_banks[3], 0)
+        nc.vector.tensor_copy(y_sb[:, BLOCK + C:2 * BLOCK], y_banks[1][:, C:])
         nc.scalar.copy(y_sb[:, 2 * BLOCK:PAIR + GROUP], y_banks[2][:, :C + GROUP])
         nc.scalar.copy(y_sb[:, PAIR + GROUP:], y_banks[3][:, :GROUP])
 

@@ -42,8 +42,7 @@ LAST = len(STEPS) - 1
 
 FIRST_CUTS = [0, GROUP, GROUP + BLOCK, STEPS[0][1]]
 
-JOBS_AT_END = {0: 5, BLOCK: 3, 2 * BLOCK: 1}
-JOBS = [3] * (LAST - 1) + [2, 0]
+JOB_SHARES = {0: (5, 3), BLOCK: (4, 2, 2), 2 * BLOCK: (1, 2)}
 
 
 def tile_moe_pre_mlp_relu2_kernel(
@@ -66,7 +65,7 @@ def tile_moe_pre_mlp_relu2_kernel(
         w2_sc = keep.tile([P, E, N], U8, name="w2_sc", align_bytes=64)
         codes = keep.tile([P, PASSES * SLOTS], U32, name="codes", align_bytes=64)
         scales = keep.tile([P, PASSES * SLOTS], U8, name="scales", align_bytes=64)
-        h_bf = keep.tile([P, SLOTS, PACK], BF16, name="h_bf", align_bytes=64)
+        h_bf = keep.tile([P, SLOTS - GROUP, PACK], BF16, name="h_bf", align_bytes=64)
         y_sb = keep.tile([P, SLOTS], F32, name="y_sb", align_bytes=64)
         ident = keep.tile([P, P], F32, name="ident")
         ring_half = PACK * STEPS[0][1]
@@ -137,27 +136,22 @@ def tile_moe_pre_mlp_relu2_kernel(
                         MULT,
                     )
 
-        def pieces(step):
-            j0, n, s = STEPS[step]
-            return [(j0, n, s)]
-
         rounded = {}
 
-        def woven(step, j, a, b):
-            s, first = STEPS[step][2], j - STEPS[step][0]
+        def woven(step, a, b):
             return (
-                rounded[j, s][:, a:b, :].rearrange("p (c i) t -> p c t i", i=RUN),
-                picked(step)[:, :, first + a:first + b].rearrange("p t (c i) -> p c t i", i=RUN),
+                rounded[step][:, a:b, :].rearrange("p (c i) t -> p c t i", i=RUN),
+                picked(step)[:, :, a:b].rearrange("p t (c i) -> p c t i", i=RUN),
             )
 
         def weave(step):
-            for j, n, s in pieces(step):
-                rounded[j, s] = stage.tile([P, n, PACK], BF16, name="rounded", align_bytes=64, bufs=3)
-                nc.scalar.copy(*woven(step, j, 0, n // 2 if step == LAST else n))
+            n = STEPS[step][1]
+            rounded[step] = stage.tile([P, n, PACK], BF16, name="rounded", align_bytes=64)
+            nc.scalar.copy(*woven(step, 0, n // 2 if step == LAST else n))
 
-        ahead = [STEPS[0], STEPS[LAST - 2], STEPS[1], STEPS[LAST - 1], (0, BLOCK, 3)]
+        ahead = [STEPS[0], STEPS[LAST - 2], STEPS[1], STEPS[LAST - 1], (0, BLOCK, LAST_PASS)]
         x_place, end = {}, 0
-        for j, n, s in ahead + [u for step in range(LAST + 1) for u in pieces(step) if u not in ahead]:
+        for j, n, s in ahead + [u for u in STEPS if u not in ahead]:
             for g in range(n // GROUP):
                 x_place[j // GROUP + g, s] = end + g * GROUP
             end += n
@@ -176,13 +170,13 @@ def tile_moe_pre_mlp_relu2_kernel(
         y_banks = [banks[4], banks[5], banks[7], banks[1]]
 
         def quantise_x(step):
-            for j, n, s in pieces(step):
-                cols = slice(x_place[j // GROUP, s], x_place[j // GROUP, s] + n)
-                nc.vector.quantize_mx(
-                    out=codes[:, cols].bitcast(FP8X4),
-                    scales=scales[:, cols],
-                    in_=rounded[j, s][:].rearrange("p j t -> p (j t)"),
-                )
+            j0, n, s = STEPS[step]
+            cols = slice(x_place[j0 // GROUP, s], x_place[j0 // GROUP, s] + n)
+            nc.vector.quantize_mx(
+                out=codes[:, cols].bitcast(FP8X4),
+                scales=scales[:, cols],
+                in_=rounded[step][:].rearrange("p j t -> p (j t)"),
+            )
 
         def opening(g):
             return 1 if g >= PAIR_A else 2
@@ -245,7 +239,7 @@ def tile_moe_pre_mlp_relu2_kernel(
                     stop=True,
                 )
 
-        jobs = []
+        jobs, shares = [], []
 
         def add_jobs(groups):
             for g in groups:
@@ -254,10 +248,11 @@ def tile_moe_pre_mlp_relu2_kernel(
                     jobs.append((square, g - 1))
             jobs.append((square, groups[-1]))
 
-        def run_jobs(count):
-            for job, g in jobs[:count]:
+        def run_jobs():
+            for job, g in jobs[:shares[0]]:
                 job(g)
-            jobs[:count] = []
+            jobs[:shares[0]] = []
+            shares[:1] = []
 
         gather(0)
         weave(0)
@@ -267,22 +262,24 @@ def tile_moe_pre_mlp_relu2_kernel(
             quantise_x(step - 1)
             j0, n, s = STEPS[step - 1]
             groups = range(j0 // GROUP, (j0 + n) // GROUP)
-            ends_groups = s == LAST_PASS and j0 in JOBS_AT_END
-            if not ends_groups:
-                run_jobs(JOBS[step])
+            ends_groups = s == LAST_PASS and j0 in JOB_SHARES
+            if shares:
+                run_jobs()
             for g in groups:
                 multiply(g, s)
             if ends_groups:
                 add_jobs(groups)
-                run_jobs(JOBS_AT_END[j0])
+                shares.extend(JOB_SHARES[j0])
+                run_jobs()
 
-        nc.vector.tensor_copy(*woven(LAST, PAIR + GROUP, GROUP // 2, GROUP))
+        nc.vector.tensor_copy(*woven(LAST, GROUP // 2, GROUP))
         quantise_h(0, C)
         quantise_x(LAST)
         multiply(PAIR_B, LAST_PASS)
         quantise_h(C, C)
         add_jobs([PAIR_A, PAIR_B])
-        run_jobs(len(jobs))
+        shares.append(len(jobs))
+        run_jobs()
         second_layer(0, C, y_banks[0], 0)
         second_layer(C, C, y_banks[0], C)
         quantise_h(BLOCK, BLOCK)

@@ -40,7 +40,7 @@ STEPS = STEPS + [(2 * BLOCK, C, s) for s in (2, 3)] + [(PAIR, C, 2)]
 STEPS = STEPS + [(PAIR, GROUP, LAST_PASS), (PAIR + GROUP, GROUP, LAST_PASS)]
 LAST = len(STEPS) - 1
 
-FIRST_CUTS = [0, GROUP, GROUP + BLOCK, STEPS[0][1]]
+FIRST_CUTS = [0, GROUP, GROUP + C, STEPS[0][1]]
 
 JOB_SHARES = {0: (5, 3), BLOCK: (4, 2, 2), 2 * BLOCK: (1, 2)}
 

@@ -40,7 +40,7 @@ STEPS = STEPS + [(2 * BLOCK, C, s) for s in (2, 3)] + [(PAIR, C, 2)]
 STEPS = STEPS + [(PAIR, GROUP, LAST_PASS), (PAIR + GROUP, GROUP, LAST_PASS)]
 LAST = len(STEPS) - 1
 
-FIRST_CUTS = [0, GROUP, GROUP + C, STEPS[0][1]]
+FIRST_CUTS = [0, 128, 352, 736, STEPS[0][1]]
 
 JOB_SHARES = {0: (5, 3), BLOCK: (4, 2, 2), 2 * BLOCK: (1, 2)}
 

@@ -77,7 +77,8 @@ def tile_moe_pre_mlp_relu2_kernel(
             nc.sync.dma_start(out=x_sb[b][:, :T], in_=rows[:, t, :])
 
         def load_gate(j0, j1):
-            nc.sync.dma_start(out=gate_sb[:, j0:j1], in_=gate[:P, j0:j1])
+            queue = nc.scalar if j0 == 0 else nc.sync
+            queue.dma_start(out=gate_sb[:, j0:j1], in_=gate[:P, j0:j1])
 
         def load_scale_rows(tile, src):
             for r in range(4):

@@ -40,7 +40,7 @@ STEPS = STEPS + [(2 * BLOCK, C, s) for s in (2, 3)] + [(PAIR, C, 2)]
 STEPS = STEPS + [(PAIR, GROUP, LAST_PASS), (PAIR + GROUP, GROUP, LAST_PASS)]
 LAST = len(STEPS) - 1
 
-FIRST_CUTS = [0, 128, 352, 736, STEPS[0][1]]
+FIRST_CUTS = [0, C, C + 3 * GROUP, STEPS[0][1]]
 
 JOB_SHARES = {0: (5, 3), BLOCK: (4, 2, 2), 2 * BLOCK: (1, 2)}
 

@@ -24,25 +24,12 @@ P = 128
 PACK = 4
 K_PASS = P * PACK
 PASSES = K // K_PASS
-LAST_PASS = PASSES - 1
 PER_COLUMN = 16
 RUN = 4
 GROUP = 128
 GROUPS = SLOTS // GROUP
 BLOCK = 512
-WIDE_GROUPS = 2 * BLOCK // GROUP
-PAIR = SLOTS - C
-PAIR_A, PAIR_B = GROUPS - 2, GROUPS - 1
-
-STEPS = [(0, 2 * BLOCK, s) for s in (0, 1)]
-STEPS = STEPS + [(j0, BLOCK, s) for j0 in (0, BLOCK) for s in (2, 3)] + [(2 * BLOCK, BLOCK, s) for s in (0, 1)]
-STEPS = STEPS + [(2 * BLOCK, C, s) for s in (2, 3)] + [(PAIR, C, 2)]
-STEPS = STEPS + [(PAIR, GROUP, LAST_PASS), (PAIR + GROUP, GROUP, LAST_PASS)]
-LAST = len(STEPS) - 1
-
-FIRST_CUTS = [0, C, C + 3 * GROUP, STEPS[0][1]]
-
-JOB_SHARES = {0: (5, 3), BLOCK: (4, 2, 2), 2 * BLOCK: (1, 2)}
+WINDOW = T + PER_COLUMN
 
 
 def tile_moe_pre_mlp_relu2_kernel(
@@ -52,32 +39,30 @@ def tile_moe_pre_mlp_relu2_kernel(
     with ExitStack() as ctx:
         keep = ctx.enter_context(tc.tile_pool(name="keep", bufs=1))
         stage = ctx.enter_context(tc.tile_pool(name="stage", bufs=3))
+        four = ctx.enter_context(tc.tile_pool(name="four", bufs=4))
         psum = ctx.enter_context(tc.psum_pool(name="psum", bufs=1))
 
         offs_sb = keep.tile([P, SLOTS // PER_COLUMN], U16, name="offs_sb")
         pos_sb = [keep.tile([P, T // PER_COLUMN], U16, name="pos_sb%d" % r) for r in range(3)]
         gate_sb = keep.tile([P, SLOTS], F32, name="gate_sb")
-        window = [max(n for j0, n, s0 in STEPS if s0 == s) + PER_COLUMN for s in range(PASSES)]
-        x_sb = [keep.tile([P, window[b // PACK]], F32, name="x_sb%d" % b) for b in range(PASSES * PACK)]
+        x_sb = [keep.tile([P, WINDOW], F32, name="x_sb%d" % b) for b in range(PASSES * PACK)]
         w1_sb = [keep.tile([P, PASSES, 2 * H], U8, name="w1_sb%d" % e, align_bytes=64) for e in range(E)]
         w1_sc = [keep.tile([P, 2 * PASSES, H], U8, name="w1_sc%d" % u, align_bytes=64) for u in range(E // 2)]
         w2_sb = keep.tile([P, E, 2 * N], U8, name="w2_sb", align_bytes=64)
         w2_sc = keep.tile([P, E, N], U8, name="w2_sc", align_bytes=64)
         codes = keep.tile([P, PASSES * SLOTS], U32, name="codes", align_bytes=64)
         scales = keep.tile([P, PASSES * SLOTS], U8, name="scales", align_bytes=64)
-        h_bf = keep.tile([P, SLOTS - GROUP, PACK], BF16, name="h_bf", align_bytes=64)
+        h_codes = keep.tile([P, SLOTS], U32, name="h_codes", align_bytes=64)
+        h_scales = keep.tile([P, SLOTS], U8, name="h_scales", align_bytes=64)
+        h_bf = keep.tile([P, SLOTS, PACK], BF16, name="h_bf", align_bytes=64)
         y_sb = keep.tile([P, SLOTS], F32, name="y_sb", align_bytes=64)
         ident = keep.tile([P, P], F32, name="ident")
-        ring_half = PACK * STEPS[0][1]
-        ring = keep.tile([P, 2 * ring_half], F32, name="ring")
 
-        def load_x(b):
-            s, t = divmod(b, PACK)
+        def load_x(s, t):
             rows = xT[K_PASS * s:K_PASS * (s + 1), :].rearrange("(p j) w -> p j w", j=PACK)
-            nc.sync.dma_start(out=x_sb[b][:, :T], in_=rows[:, t, :])
+            nc.sync.dma_start(out=x_sb[PACK * s + t][:, :T], in_=rows[:, t, :])
 
-        def load_gate(j0, j1):
-            queue = nc.scalar if j0 == 0 else nc.sync
+        def load_gate(queue, j0, j1):
             queue.dma_start(out=gate_sb[:, j0:j1], in_=gate[:P, j0:j1])
 
         def load_scale_rows(tile, src):
@@ -98,22 +83,24 @@ def tile_moe_pre_mlp_relu2_kernel(
         nc.gpsimd.memset(w1_sc[2][:].bitcast(I32), 0)
         nc.gpsimd.memset(w2_sc[:].bitcast(I32), 0)
 
-        load_x(0)
+        load_x(0, 0)
         nc.sync.dma_start(offs_sb[:], offs)
-        for j0, j1 in zip(FIRST_CUTS, FIRST_CUTS[1:]):
-            load_gate(j0, j1)
-        for b in range(1, PASSES * PACK):
-            load_x(b)
-            if b == 2 * PACK + 1:
-                load_w1_scales(0)
-            if b == LAST_PASS * PACK:
-                load_w1(0)
-        load_w1(1)
-        load_gate(FIRST_CUTS[-1], SLOTS)
-        for u in range(1, E // 2):
+        load_gate(nc.scalar, BLOCK, BLOCK + C)
+        load_gate(nc.sync, BLOCK + C, 2 * BLOCK)
+        for t in range(1, PACK):
+            load_x(0, t)
+        load_gate(nc.sync, 0, BLOCK)
+        for t in range(PACK):
+            load_x(1, t)
+        for t in range(PACK):
+            load_x(3, t)
+            load_x(2, t)
+        for u in range(E // 2):
             load_w1_scales(u)
             load_w1(2 * u)
             load_w1(2 * u + 1)
+            if u == 0:
+                load_gate(nc.sync, 2 * BLOCK, SLOTS)
         load_scale_rows(w2_sc, w2_scales.rearrange("e s (q r) n -> r q (e s) n", r=4))
         nc.sync.dma_start(
             out=w2_sb[:].bitcast(I32), in_=w2_words.rearrange("e s p b -> p (e s) b").bitcast(I32)
@@ -121,192 +108,213 @@ def tile_moe_pre_mlp_relu2_kernel(
         for tile, pos in zip(pos_sb, (pos1, pos2, pos3)):
             nc.sync.dma_start(tile[:], pos)
 
-        def picked(step):
-            start = step % 2 * ring_half
-            return ring[:, start:start + PACK * STEPS[step][1]].rearrange("p (t j) -> p t j", t=PACK)
+        picked, rounded = {}, {}
 
-        def gather(step):
-            j0, n, s = STEPS[step]
+        def window(s, t, a, b):
+            return x_sb[PACK * s + t][:].indirect(offs_sb[:, a // PER_COLUMN:b // PER_COLUMN])
+
+        def gather_plain(unit):
+            j0, n, s = unit
+            picked[unit] = stage.tile([P, PACK, n], F32, name="plain")
             for t in range(PACK):
-                cuts = FIRST_CUTS if step == 0 and t == 0 else [j0, j0 + n]
-                for a, b in zip(cuts, cuts[1:]):
+                nc.scalar.activation(picked[unit][:, t, :], window(s, t, j0, j0 + n), ACT.Copy)
+
+        def gather_gated(unit, planes, cuts=None):
+            j0, n, s = unit
+            if unit not in picked:
+                picked[unit] = keep.tile([P, PACK, n], F32, name="gated")
+            for t in planes:
+                ends = cuts if cuts and t == 0 else [j0, j0 + n]
+                for a, b in zip(ends, ends[1:]):
                     nc.vector.tensor_tensor(
-                        picked(step)[:, t, a - j0:b - j0],
-                        x_sb[PACK * s + t][:].indirect(offs_sb[:, a // PER_COLUMN:b // PER_COLUMN]),
-                        gate_sb[:, a:b],
-                        MULT,
+                        picked[unit][:, t, a - j0:b - j0], window(s, t, a, b), gate_sb[:, a:b], MULT
                     )
 
-        rounded = {}
-
-        def woven(step, a, b):
+        def woven(unit):
+            j0, n, s = unit
+            rounded[unit] = stage.tile([P, n, PACK], BF16, name="rounded", align_bytes=64)
             return (
-                rounded[step][:, a:b, :].rearrange("p (c i) t -> p c t i", i=RUN),
-                picked(step)[:, :, a:b].rearrange("p t (c i) -> p c t i", i=RUN),
+                rounded[unit][:].rearrange("p (c i) t -> p c t i", i=RUN),
+                picked[unit][:].rearrange("p t (c i) -> p c t i", i=RUN),
             )
 
-        def weave(step):
-            n = STEPS[step][1]
-            rounded[step] = stage.tile([P, n, PACK], BF16, name="rounded", align_bytes=64)
-            nc.scalar.copy(*woven(step, 0, n // 2 if step == LAST else n))
+        def weave(unit):
+            nc.vector.tensor_copy(*woven(unit))
 
-        ahead = [STEPS[0], STEPS[LAST - 2], STEPS[1], STEPS[LAST - 1], (0, BLOCK, LAST_PASS)]
-        x_place, end = {}, 0
-        for j, n, s in ahead + [u for u in STEPS if u not in ahead]:
-            for g in range(n // GROUP):
-                x_place[j // GROUP + g, s] = end + g * GROUP
-            end += n
-        h_place = {
-            0: x_place[PAIR_A, 2] + GROUP - C,
-            C: x_place[PAIR_B, 2],
-            BLOCK: x_place[PAIR_A, LAST_PASS] + GROUP - BLOCK,
-            2 * BLOCK: x_place[2, LAST_PASS],
-            PAIR: x_place[0, LAST_PASS],
-            PAIR + GROUP: x_place[1, LAST_PASS],
-        }
+        def weave_gate(unit):
+            j0, n, s = unit
+            weights = gate_sb[:, j0:j0 + n].rearrange("p (c i) -> p c i", i=RUN).unsqueeze(2)
+            nc.vector.tensor_tensor(*woven(unit), weights.to_broadcast([P, n // RUN, PACK, RUN]), MULT)
 
         banks = [psum.tile([P, H], F32, name="bank%d" % u) for u in range(8)]
-        acc = [banks[4 + g % 4] if g < WIDE_GROUPS or g >= PAIR_A else banks[g % 2] for g in range(GROUPS)]
-        turned = [banks[2 + g % 2][:].rearrange("p (t j) -> p t j", t=PACK) for g in range(GROUPS)]
-        y_banks = [banks[4], banks[5], banks[7], banks[1]]
+        acc = [banks[g % 8] for g in range(GROUPS)]
+        done = {g: 0 for g in range(GROUPS)}
 
-        def quantise_x(step):
-            j0, n, s = STEPS[step]
-            cols = slice(x_place[j0 // GROUP, s], x_place[j0 // GROUP, s] + n)
+        def quantise_x(unit):
+            j0, n, s = unit
+            cols = slice(s * SLOTS + j0, s * SLOTS + j0 + n)
             nc.vector.quantize_mx(
                 out=codes[:, cols].bitcast(FP8X4),
                 scales=scales[:, cols],
-                in_=rounded[step][:].rearrange("p j t -> p (j t)"),
+                in_=rounded[unit][:].rearrange("p j t -> p (j t)"),
             )
 
-        def opening(g):
-            return 1 if g >= PAIR_A else 2
-
-        def multiply(g, s0):
-            if s0 < opening(g):
-                return
-            e = g * GROUP // C
-            for s in [s0] + (list(range(s0)) if s0 == opening(g) else []):
-                cols = slice(x_place[g, s], x_place[g, s] + GROUP)
+        def multiply(unit):
+            j0, n, s = unit
+            for g in range(j0 // GROUP, (j0 + n) // GROUP):
+                e = g * GROUP // C
+                cols = slice(s * SLOTS + g * GROUP, s * SLOTS + (g + 1) * GROUP)
                 nc.tensor.matmul_mx(
                     out=acc[g][:],
                     lhsT=codes[:, cols].bitcast(FP8X4),
                     lhsT_scale=scales[:, cols],
                     rhs=w1_sb[e][:, s, :].bitcast(FP4X4),
                     rhs_scale=w1_sc[e // 2][:, e % 2 * PASSES + s, :],
-                    start=(s == opening(g)),
-                    stop=(s == LAST_PASS),
+                    start=(done[g] == 0),
+                    stop=(done[g] == PASSES - 1),
                 )
+                done[g] = done[g] + 1
+
+        def finish(unit):
+            quantise_x(unit)
+            multiply(unit)
 
         def rectify(g):
-            relu = stage.tile([P, PACK, P], F32, name="relu")
+            relu = four.tile([P, PACK, P], F32, name="relu")
             planes = acc[g][:].rearrange("j (p t) -> j t p", t=PACK)
-            part = PACK // 2 if g == PAIR_B else PACK
-            for t in range(0, PACK, part):
-                if g == PAIR_A:
-                    nc.vector.tensor_scalar_max(relu[:, t:t + part, :], planes[:, t:t + part, :], 0.0)
-                else:
-                    nc.scalar.activation(relu[:, t:t + part, :], planes[:, t:t + part, :], ACT.Relu)
+            nc.scalar.activation(relu[:], planes, ACT.Relu)
+            turned = acc[g][:].rearrange("p (t j) -> p t j", t=PACK)
             for t in range(PACK):
-                nc.tensor.transpose(turned[g][:, t, :], relu[:, t, :], ident[:])
-
-        def h_of(j0, n):
-            if j0 == PAIR + GROUP:
-                return y_sb[:, BLOCK + C:2 * BLOCK].bitcast(BF16).rearrange("p (j t) -> p j t", t=PACK)
-            return h_bf[:, j0:j0 + n, :]
+                nc.tensor.transpose(turned[:, t, :], relu[:, t, :], ident[:])
 
         def square(g):
-            nc.scalar.activation(h_of(g * GROUP, GROUP), turned[g].rearrange("p t j -> p j t"), ACT.Square)
+            turned = acc[g][:].rearrange("p (t j) -> p j t", t=PACK)
+            nc.scalar.activation(h_bf[:, g * GROUP:(g + 1) * GROUP, :], turned, ACT.Square)
+
+        def hidden(groups):
+            for g in groups:
+                rectify(g)
+            for g in groups:
+                square(g)
 
         def quantise_h(j0, n):
-            cols = slice(h_place[j0], h_place[j0] + n)
             nc.vector.quantize_mx(
-                out=codes[:, cols].bitcast(FP8X4),
-                scales=scales[:, cols],
-                in_=h_of(j0, n).rearrange("p j t -> p (j t)"),
+                out=h_codes[:, j0:j0 + n].bitcast(FP8X4),
+                scales=h_scales[:, j0:j0 + n],
+                in_=h_bf[:, j0:j0 + n, :].rearrange("p j t -> p (j t)"),
             )
 
         def second_layer(j0, n, bank, col):
             for j in range(0, n, C):
                 width = min(C, n)
-                cols = slice(h_place[j0] + j, h_place[j0] + j + width)
+                cols = slice(j0 + j, j0 + j + width)
                 nc.tensor.matmul_mx(
                     out=bank[:, col + j:col + j + width],
                     lhsT=w2_sb[:, (j0 + j) // C, :].bitcast(FP4X4),
                     lhsT_scale=w2_sc[:, (j0 + j) // C, :],
-                    rhs=codes[:, cols].bitcast(FP8X4),
-                    rhs_scale=scales[:, cols],
+                    rhs=h_codes[:, cols].bitcast(FP8X4),
+                    rhs_scale=h_scales[:, cols],
                     start=True,
                     stop=True,
                 )
 
-        jobs, shares = [], []
+        a0, a1, a2, a3 = [(0, BLOCK, s) for s in range(PASSES)]
+        b0, b1, b2, b3 = [(BLOCK, BLOCK, s) for s in range(PASSES)]
+        c0, c1 = [(2 * BLOCK, BLOCK, s) for s in range(2)]
+        d2, d3 = [(2 * BLOCK, C, s) for s in (2, 3)]
+        e2 = (SLOTS - C, C, 2)
+        f3, g3 = (SLOTS - C, GROUP, 3), (SLOTS - GROUP, GROUP, 3)
 
-        def add_jobs(groups):
-            for g in groups:
-                jobs.append((rectify, g))
-                if g > groups[0]:
-                    jobs.append((square, g - 1))
-            jobs.append((square, groups[-1]))
-
-        def run_jobs():
-            for job, g in jobs[:shares[0]]:
-                job(g)
-            jobs[:shares[0]] = []
-            shares[:1] = []
-
-        gather(0)
-        weave(0)
-        for step in range(1, LAST + 1):
-            gather(step)
-            weave(step)
-            quantise_x(step - 1)
-            j0, n, s = STEPS[step - 1]
-            groups = range(j0 // GROUP, (j0 + n) // GROUP)
-            ends_groups = s == LAST_PASS and j0 in JOB_SHARES
-            if shares:
-                run_jobs()
-            for g in groups:
-                multiply(g, s)
-            if ends_groups:
-                add_jobs(groups)
-                shares.extend(JOB_SHARES[j0])
-                run_jobs()
-
-        nc.vector.tensor_copy(*woven(LAST, GROUP // 2, GROUP))
+        gather_plain(a0)
+        gather_gated(b0, range(PACK), [BLOCK, BLOCK + C, 2 * BLOCK])
+        gather_plain(a1)
+        gather_plain(a2)
+        weave(b0)
+        weave_gate(a0)
+        gather_plain(b1)
+        finish(b0)
+        gather_gated(a3, [0])
+        finish(a0)
+        gather_gated(a3, [1])
+        weave_gate(a1)
+        gather_plain(b2)
+        gather_gated(a3, [2])
+        finish(a1)
+        gather_gated(a3, [3])
+        weave_gate(a2)
+        gather_plain(c0)
+        weave(a3)
+        finish(a2)
+        finish(a3)
+        weave_gate(b1)
+        gather_plain(c1)
+        hidden(range(0, 4))
+        gather_gated(b3, [0])
+        finish(b1)
+        gather_gated(b3, [1, 2, 3])
+        weave_gate(b2)
+        gather_plain(d2)
+        weave(b3)
+        finish(b2)
+        finish(b3)
+        weave_gate(c0)
+        gather_plain(e2)
+        hidden(range(4, 8))
+        gather_gated(d3, [0])
+        finish(c0)
+        gather_gated(d3, [1, 2, 3])
+        weave_gate(c1)
+        weave(d3)
+        finish(c1)
+        weave_gate(d2)
+        finish(d3)
+        gather_gated(f3, [0])
+        finish(d2)
+        hidden(range(8, 10))
+        gather_gated(f3, [1, 2, 3])
+        weave_gate(e2)
+        weave(f3)
+        finish(e2)
+        gather_gated(g3, [0])
+        finish(f3)
+        gather_gated(g3, [1, 2, 3])
+        weave(g3)
         quantise_h(0, C)
-        quantise_x(LAST)
-        multiply(PAIR_B, LAST_PASS)
+        finish(g3)
+        hidden(range(10, 12))
         quantise_h(C, C)
-        add_jobs([PAIR_A, PAIR_B])
-        shares.append(len(jobs))
-        run_jobs()
-        second_layer(0, C, y_banks[0], 0)
-        second_layer(C, C, y_banks[0], C)
+        second_layer(0, BLOCK, banks[4], 0)
         quantise_h(BLOCK, BLOCK)
-        second_layer(BLOCK, BLOCK, y_banks[1], 0)
-        nc.vector.tensor_copy(y_sb[:, :BLOCK], y_banks[0][:])
+        second_layer(BLOCK, BLOCK, banks[5], 0)
+        nc.vector.tensor_copy(y_sb[:, :BLOCK], banks[4][:])
         quantise_h(2 * BLOCK, C)
-        second_layer(2 * BLOCK, C, y_banks[2], 0)
-        nc.vector.tensor_copy(y_sb[:, BLOCK:BLOCK + C], y_banks[1][:, :C])
-        quantise_h(PAIR, GROUP)
-        second_layer(PAIR, GROUP, y_banks[2], C)
-        quantise_h(PAIR + GROUP, GROUP)
-        second_layer(PAIR + GROUP, GROUP, y_banks[3], 0)
-        nc.vector.tensor_copy(y_sb[:, BLOCK + C:2 * BLOCK], y_banks[1][:, C:])
-        nc.scalar.copy(y_sb[:, 2 * BLOCK:PAIR + GROUP], y_banks[2][:, :C + GROUP])
-        nc.scalar.copy(y_sb[:, PAIR + GROUP:], y_banks[3][:, :GROUP])
+        second_layer(2 * BLOCK, C, banks[6], 0)
+        nc.vector.tensor_copy(y_sb[:, BLOCK:2 * BLOCK], banks[5][:])
+        quantise_h(SLOTS - C, GROUP)
+        second_layer(SLOTS - C, GROUP, banks[6], C)
+        quantise_h(SLOTS - GROUP, GROUP)
+        second_layer(SLOTS - GROUP, GROUP, banks[7], 0)
+        nc.scalar.copy(y_sb[:, 2 * BLOCK:SLOTS - GROUP], banks[6][:, :C + GROUP])
+        nc.vector.tensor_copy(y_sb[:, SLOTS - GROUP:], banks[7][:, :GROUP])
 
-        half = T // 2
-        out_cuts = (0, half, half + half // 2, T)
-        sums = [keep.tile([P, T], F32, name="sums%d" % r) for r in range(3)]
-        for r in range(3):
-            cuts = (0, half, T) if r < 2 else out_cuts
-            for t0, t1 in zip(cuts, cuts[1:]):
-                fetched = y_sb[:].indirect(pos_sb[r][:, t0 // PER_COLUMN:t1 // PER_COLUMN])
-                if r == 0:
-                    nc.vector.tensor_copy(sums[0][:, t0:t1], fetched)
-                else:
-                    nc.vector.tensor_tensor(sums[r][:, t0:t1], fetched, sums[r - 1][:, t0:t1], ADD)
-        for t0, t1, queue in zip(out_cuts, out_cuts[1:], (nc.sync, nc.scalar, nc.sync)):
-            queue.dma_start(out=out[:, t0:t1], in_=sums[2][:, t0:t1])
+        half, quarter = T // 2, T // 4
+        first = keep.tile([P, T], F32, name="first")
+        part = keep.tile([P, T], F32, name="part")
+        more = keep.tile([P, half], F32, name="more")
+        total = keep.tile([P, T], F32, name="total")
+
+        def fetched(r, t0, t1):
+            return y_sb[:].indirect(pos_sb[r][:, t0 // PER_COLUMN:t1 // PER_COLUMN])
+
+        for t0, t1 in ((half, half + quarter), (half + quarter, T), (0, half)):
+            nc.scalar.activation(first[:, t0:t1], fetched(0, t0, t1), ACT.Copy)
+        nc.vector.tensor_copy(part[:, :half], fetched(1, 0, half))
+        lo, hi = slice(half, half + quarter), slice(half + quarter, T)
+        nc.vector.tensor_tensor(part[:, lo], fetched(1, lo.start, lo.stop), first[:, lo], ADD)
+        nc.vector.tensor_tensor(more[:], fetched(2, 0, half), part[:, :half], ADD)
+        nc.vector.tensor_tensor(part[:, hi], fetched(1, hi.start, hi.stop), first[:, hi], ADD)
+        nc.vector.tensor_tensor(total[:, :half], more[:], first[:, :half], ADD)
+        nc.vector.tensor_tensor(total[:, lo], fetched(2, lo.start, lo.stop), part[:, lo], ADD)
+        nc.vector.tensor_tensor(total[:, hi], fetched(2, hi.start, hi.stop), part[:, hi], ADD)
+        for cols, queue in zip((slice(0, half), lo, hi), (nc.sync, nc.scalar, nc.sync)):
+            queue.dma_start(out=out[:, cols], in_=total[:, cols])

@@ -77,6 +77,10 @@ def tile_moe_pre_mlp_relu2_kernel(
                 out=w1_sb[e][:].bitcast(I32), in_=w1_words[e].rearrange("s p b -> p s b").bitcast(I32)
             )
 
+        warm = keep.tile([P, 16], F32, name="warm")
+        nc.vector.memset(warm[:, :8], 0.0)
+        nc.scalar.activation(warm[:, 8:9], warm[:, 0:1], ACT.Copy)
+
         make_identity(nc, ident[:])
         nc.vector.memset(w1_sc[0][:].bitcast(I32), 0)
         nc.vector.memset(w1_sc[1][:].bitcast(I32), 0)

@@ -94,11 +94,9 @@ def tile_moe_pre_mlp_relu2_kernel(
         for t in range(1, PACK):
             load_x(0, t)
         load_gate(nc.sync, 0, BLOCK)
-        for t in range(PACK):
-            load_x(1, t)
-        for t in range(PACK):
-            load_x(3, t)
-            load_x(2, t)
+        for s in range(1, PASSES):
+            for t in range(PACK):
+                load_x(s, t)
         for u in range(E // 2):
             load_w1_scales(u)
             load_w1(2 * u)
@@ -117,9 +115,11 @@ def tile_moe_pre_mlp_relu2_kernel(
         def window(s, t, a, b):
             return x_sb[PACK * s + t][:].indirect(offs_sb[:, a // PER_COLUMN:b // PER_COLUMN])
 
-        def gather_plain(unit):
+        plain = [keep.tile([P, PACK * BLOCK], F32, name="plain%d" % u) for u in range(3)]
+
+        def gather_plain(unit, buffer):
             j0, n, s = unit
-            picked[unit] = stage.tile([P, PACK, n], F32, name="plain")
+            picked[unit] = plain[buffer][:, :PACK * n].rearrange("p (t j) -> p t j", t=PACK)
             for t in range(PACK):
                 nc.scalar.activation(picked[unit][:, t, :], window(s, t, j0, j0 + n), ACT.Copy)
 
@@ -136,9 +136,12 @@ def tile_moe_pre_mlp_relu2_kernel(
 
         def woven(unit):
             j0, n, s = unit
-            rounded[unit] = stage.tile([P, n, PACK], BF16, name="rounded", align_bytes=64)
+            if unit in held:
+                rounded[unit] = h_bf[:, held[unit]:held[unit] + n, :]
+            else:
+                rounded[unit] = stage.tile([P, n, PACK], BF16, name="rounded", align_bytes=64)[:]
             return (
-                rounded[unit][:].rearrange("p (c i) t -> p c t i", i=RUN),
+                rounded[unit].rearrange("p (c i) t -> p c t i", i=RUN),
                 picked[unit][:].rearrange("p t (c i) -> p c t i", i=RUN),
             )
 
@@ -154,24 +157,34 @@ def tile_moe_pre_mlp_relu2_kernel(
         acc = [banks[g % 8] for g in range(GROUPS)]
         done = {g: 0 for g in range(GROUPS)}
 
-        def quantise_x(unit):
-            j0, n, s = unit
+        late = {
+            GROUPS - 2: (h_codes[:, 64:64 + GROUP], h_scales[:, 64:64 + GROUP]),
+            GROUPS - 1: (h_codes[:, BLOCK - 64:BLOCK + 64], h_scales[:, 2 * BLOCK + 64:2 * BLOCK + 64 + GROUP]),
+        }
+
+        def x_operand(j0, n, s):
+            if s == PASSES - 1 and j0 // GROUP in late:
+                return late[j0 // GROUP]
             cols = slice(s * SLOTS + j0, s * SLOTS + j0 + n)
+            return codes[:, cols], scales[:, cols]
+
+        def quantise_x(unit):
+            words, exponents = x_operand(*unit)
             nc.vector.quantize_mx(
-                out=codes[:, cols].bitcast(FP8X4),
-                scales=scales[:, cols],
-                in_=rounded[unit][:].rearrange("p j t -> p (j t)"),
+                out=words.bitcast(FP8X4),
+                scales=exponents,
+                in_=rounded[unit].rearrange("p j t -> p (j t)"),
             )
 
         def multiply(unit):
             j0, n, s = unit
             for g in range(j0 // GROUP, (j0 + n) // GROUP):
                 e = g * GROUP // C
-                cols = slice(s * SLOTS + g * GROUP, s * SLOTS + (g + 1) * GROUP)
+                words, exponents = x_operand(g * GROUP, GROUP, s)
                 nc.tensor.matmul_mx(
                     out=acc[g][:],
-                    lhsT=codes[:, cols].bitcast(FP8X4),
-                    lhsT_scale=scales[:, cols],
+                    lhsT=words.bitcast(FP8X4),
+                    lhsT_scale=exponents,
                     rhs=w1_sb[e][:, s, :].bitcast(FP4X4),
                     rhs_scale=w1_sc[e // 2][:, e % 2 * PASSES + s, :],
                     start=(done[g] == 0),
@@ -186,7 +199,10 @@ def tile_moe_pre_mlp_relu2_kernel(
         def rectify(g):
             relu = four.tile([P, PACK, P], F32, name="relu")
             planes = acc[g][:].rearrange("j (p t) -> j t p", t=PACK)
-            nc.scalar.activation(relu[:], planes, ACT.Relu)
+            if g == GROUPS - 1:
+                nc.vector.tensor_scalar_max(relu[:], planes, 0.0)
+            else:
+                nc.scalar.activation(relu[:], planes, ACT.Relu)
             turned = acc[g][:].rearrange("p (t j) -> p t j", t=PACK)
             for t in range(PACK):
                 nc.tensor.transpose(turned[:, t, :], relu[:, t, :], ident[:])
@@ -194,12 +210,6 @@ def tile_moe_pre_mlp_relu2_kernel(
         def square(g):
             turned = acc[g][:].rearrange("p (t j) -> p j t", t=PACK)
             nc.scalar.activation(h_bf[:, g * GROUP:(g + 1) * GROUP, :], turned, ACT.Square)
-
-        def hidden(groups):
-            for g in groups:
-                rectify(g)
-            for g in groups:
-                square(g)
 
         def quantise_h(j0, n):
             nc.vector.quantize_mx(
@@ -229,63 +239,75 @@ def tile_moe_pre_mlp_relu2_kernel(
         e2 = (SLOTS - C, C, 2)
         f3, g3 = (SLOTS - C, GROUP, 3), (SLOTS - GROUP, GROUP, 3)
 
-        gather_plain(a0)
+        held = {b2: 0, d3: BLOCK, d2: BLOCK + C}
+
+        gather_plain(a0, 0)
         gather_gated(b0, range(PACK), [BLOCK, BLOCK + C, 2 * BLOCK])
-        gather_plain(a1)
-        gather_plain(a2)
+        gather_plain(a1, 1)
+        gather_plain(a2, 2)
         weave(b0)
         weave_gate(a0)
-        gather_plain(b1)
+        gather_plain(a3, 0)
         finish(b0)
-        gather_gated(a3, [0])
+        gather_gated(b1, [0])
         finish(a0)
-        gather_gated(a3, [1])
+        gather_gated(b1, [1])
         weave_gate(a1)
-        gather_plain(b2)
-        gather_gated(a3, [2])
+        gather_plain(b2, 1)
+        gather_gated(b1, [2])
         finish(a1)
-        gather_gated(a3, [3])
+        gather_gated(b1, [3])
         weave_gate(a2)
-        gather_plain(c0)
-        weave(a3)
+        gather_plain(b3, 2)
+        weave(b1)
         finish(a2)
-        finish(a3)
-        weave_gate(b1)
-        gather_plain(c1)
-        hidden(range(0, 4))
-        gather_gated(b3, [0])
+        weave_gate(a3)
         finish(b1)
-        gather_gated(b3, [1, 2, 3])
+        gather_gated(c0, [0])
+        finish(a3)
+        for g in range(0, 4):
+            rectify(g)
+        gather_gated(c0, [1, 2, 3])
         weave_gate(b2)
-        gather_plain(d2)
-        weave(b3)
+        gather_plain(c1, 1)
+        weave(c0)
         finish(b2)
-        finish(b3)
-        weave_gate(c0)
-        gather_plain(e2)
-        hidden(range(4, 8))
-        gather_gated(d3, [0])
+        for g in range(0, 4):
+            square(g)
+        weave_gate(b3)
+        gather_plain(d2, 2)
         finish(c0)
+        gather_gated(d3, [0])
+        finish(b3)
+        for g in range(4, 8):
+            rectify(g)
         gather_gated(d3, [1, 2, 3])
         weave_gate(c1)
+        gather_plain(e2, 1)
         weave(d3)
         finish(c1)
         weave_gate(d2)
         finish(d3)
         gather_gated(f3, [0])
         finish(d2)
-        hidden(range(8, 10))
+        rectify(8)
+        rectify(9)
+        for g in range(4, 10):
+            square(g)
         gather_gated(f3, [1, 2, 3])
         weave_gate(e2)
         weave(f3)
         finish(e2)
         gather_gated(g3, [0])
         finish(f3)
+        rectify(10)
         gather_gated(g3, [1, 2, 3])
         weave(g3)
         quantise_h(0, C)
         finish(g3)
-        hidden(range(10, 12))
+        rectify(11)
+        square(10)
+        square(11)
         quantise_h(C, C)
         second_layer(0, BLOCK, banks[4], 0)
         quantise_h(BLOCK, BLOCK)

@@ -30,6 +30,7 @@ GROUP = 128
 GROUPS = SLOTS // GROUP
 BLOCK = 512
 WINDOW = T + PER_COLUMN
+POOL_SLOTS = 128
 
 
 def tile_moe_pre_mlp_relu2_kernel(
@@ -81,6 +82,9 @@ def tile_moe_pre_mlp_relu2_kernel(
         nc.vector.memset(warm[:, :8], 0.0)
         nc.scalar.activation(warm[:, 8:9], warm[:, 0:1], ACT.Copy)
 
+        gate_rows = keep.tile([P, GROUP], F32, name="gate_rows")
+        gate_cols = keep.tile([P, GROUPS], F32, name="gate_cols")
+        nc.gpsimd.memset(gate_rows[:], 0.0)
         make_identity(nc, ident[:])
         nc.vector.memset(w1_sc[0][:].bitcast(I32), 0)
         nc.vector.memset(w1_sc[1][:].bitcast(I32), 0)
@@ -91,9 +95,11 @@ def tile_moe_pre_mlp_relu2_kernel(
         nc.sync.dma_start(offs_sb[:], offs)
         load_gate(nc.scalar, BLOCK, BLOCK + C)
         load_gate(nc.sync, BLOCK + C, 2 * BLOCK)
-        for t in range(1, PACK):
+        load_x(0, 1)
+        nc.sync.dma_start(out=gate_rows[:GROUPS, :], in_=gate[0, :].rearrange("(g j) -> g j", j=GROUP))
+        for t in range(2, PACK):
             load_x(0, t)
-        load_gate(nc.sync, 0, BLOCK)
+        load_gate(nc.sync, 0, POOL_SLOTS)
         for s in range(1, PASSES):
             for t in range(PACK):
                 load_x(s, t)
@@ -123,10 +129,13 @@ def tile_moe_pre_mlp_relu2_kernel(
             for t in range(PACK):
                 nc.scalar.activation(picked[unit][:, t, :], window(s, t, j0, j0 + n), ACT.Copy)
 
+        gated = keep.tile([P, PACK * BLOCK], F32, name="gated")
+        shared = keep.tile([P, BLOCK, PACK], BF16, name="shared", align_bytes=64)
+
         def gather_gated(unit, planes, cuts=None):
             j0, n, s = unit
-            if unit not in picked:
-                picked[unit] = keep.tile([P, PACK, n], F32, name="gated")
+            start = gated_place.get(unit, 0)
+            picked[unit] = gated[:, start:start + PACK * n].rearrange("p (t j) -> p t j", t=PACK)
             for t in planes:
                 ends = cuts if cuts and t == 0 else [j0, j0 + n]
                 for a, b in zip(ends, ends[1:]):
@@ -134,27 +143,42 @@ def tile_moe_pre_mlp_relu2_kernel(
                         picked[unit][:, t, a - j0:b - j0], window(s, t, a, b), gate_sb[:, a:b], MULT
                     )
 
-        def woven(unit):
+        def woven(unit, a, b):
+            return (
+                rounded[unit][:, a:b, :].rearrange("p (c i) t -> p c t i", i=RUN),
+                picked[unit][:, :, a:b].rearrange("p t (c i) -> p c t i", i=RUN),
+            )
+
+        def weave(unit):
             j0, n, s = unit
             if unit in held:
                 rounded[unit] = h_bf[:, held[unit]:held[unit] + n, :]
             else:
                 rounded[unit] = stage.tile([P, n, PACK], BF16, name="rounded", align_bytes=64)[:]
-            return (
-                rounded[unit].rearrange("p (c i) t -> p c t i", i=RUN),
-                picked[unit][:].rearrange("p t (c i) -> p c t i", i=RUN),
-            )
+            nc.vector.tensor_copy(*woven(unit, 0, n))
 
-        def weave(unit):
-            nc.vector.tensor_copy(*woven(unit))
+        banks = [psum.tile([P, H], F32, name="bank%d" % u) for u in range(8)]
+        acc = [banks[u] for u in (0, 1, 2, 3, 4, 5, 6, 0, 1, 2, 3, 7)]
+        gate_bank = banks[7]
+
+        def spread_gate(j0):
+            for g in range(BLOCK // GROUP):
+                column = gate_cols[:, j0 // GROUP + g:j0 // GROUP + g + 1].to_broadcast([P, P])
+                nc.tensor.transpose(gate_bank[:, g * GROUP:(g + 1) * GROUP], column, ident[:])
 
         def weave_gate(unit):
             j0, n, s = unit
-            weights = gate_sb[:, j0:j0 + n].rearrange("p (c i) -> p c i", i=RUN).unsqueeze(2)
-            nc.vector.tensor_tensor(*woven(unit), weights.to_broadcast([P, n // RUN, PACK, RUN]), MULT)
+            rounded[unit] = shared[:, :n, :]
+            m = POOL_SLOTS if n == BLOCK else 0
+            if n == BLOCK:
+                weights = gate_sb[:, j0:j0 + m].unsqueeze(2).to_broadcast([P, m, PACK])
+                planes = picked[unit][:, :, :m].rearrange("p t j -> p j t")
+                nc.gpsimd.tensor_tensor(rounded[unit][:, :m, :], planes, weights, MULT)
+            first = j0 % BLOCK
+            weights = gate_bank[:, first + m:first + n].rearrange("p (c i) -> p c i", i=RUN).unsqueeze(2)
+            nc.vector.tensor_tensor(*woven(unit, m, n), weights.to_broadcast([P, (n - m) // RUN, PACK, RUN]), MULT)
 
-        banks = [psum.tile([P, H], F32, name="bank%d" % u) for u in range(8)]
-        acc = [banks[g % 8] for g in range(GROUPS)]
+        waiting = {g: [] for g in range(7, GROUPS)}
         done = {g: 0 for g in range(GROUPS)}
 
         late = {
@@ -176,25 +200,32 @@ def tile_moe_pre_mlp_relu2_kernel(
                 in_=rounded[unit].rearrange("p j t -> p (j t)"),
             )
 
-        def multiply(unit):
-            j0, n, s = unit
-            for g in range(j0 // GROUP, (j0 + n) // GROUP):
-                e = g * GROUP // C
-                words, exponents = x_operand(g * GROUP, GROUP, s)
-                nc.tensor.matmul_mx(
-                    out=acc[g][:],
-                    lhsT=words.bitcast(FP8X4),
-                    lhsT_scale=exponents,
-                    rhs=w1_sb[e][:, s, :].bitcast(FP4X4),
-                    rhs_scale=w1_sc[e // 2][:, e % 2 * PASSES + s, :],
-                    start=(done[g] == 0),
-                    stop=(done[g] == PASSES - 1),
-                )
-                done[g] = done[g] + 1
+        def multiply(g, s):
+            if g in waiting:
+                waiting[g].append(s)
+                return
+            e = g * GROUP // C
+            words, exponents = x_operand(g * GROUP, GROUP, s)
+            nc.tensor.matmul_mx(
+                out=acc[g][:],
+                lhsT=words.bitcast(FP8X4),
+                lhsT_scale=exponents,
+                rhs=w1_sb[e][:, s, :].bitcast(FP4X4),
+                rhs_scale=w1_sc[e // 2][:, e % 2 * PASSES + s, :],
+                start=(done[g] == 0),
+                stop=(done[g] == PASSES - 1),
+            )
+            done[g] = done[g] + 1
+
+        def open_sum(g):
+            for s in waiting.pop(g):
+                multiply(g, s)
 
         def finish(unit):
+            j0, n, s = unit
             quantise_x(unit)
-            multiply(unit)
+            for g in range(j0 // GROUP, (j0 + n) // GROUP):
+                multiply(g, s)
 
         def rectify(g):
             relu = four.tile([P, PACK, P], F32, name="relu")
@@ -239,55 +270,61 @@ def tile_moe_pre_mlp_relu2_kernel(
         e2 = (SLOTS - C, C, 2)
         f3, g3 = (SLOTS - C, GROUP, 3), (SLOTS - GROUP, GROUP, 3)
 
-        held = {b2: 0, d3: BLOCK, d2: BLOCK + C}
+        held = {c0: 0, d3: BLOCK, d2: BLOCK + C}
+        gated_place = {d2: PACK * C, g3: PACK * GROUP}
 
+        nc.tensor.transpose(banks[6][:, :GROUP], gate_rows[:], ident[:])
+        nc.vector.tensor_copy(gate_cols[:], banks[6][:, :GROUPS])
+        spread_gate(0)
         gather_plain(a0, 0)
         gather_gated(b0, range(PACK), [BLOCK, BLOCK + C, 2 * BLOCK])
         gather_plain(a1, 1)
         gather_plain(a2, 2)
-        weave(b0)
         weave_gate(a0)
         gather_plain(a3, 0)
-        finish(b0)
-        gather_gated(b1, [0])
+        weave(b0)
         finish(a0)
-        gather_gated(b1, [1])
+        gather_gated(b1, [0])
         weave_gate(a1)
         gather_plain(b2, 1)
-        gather_gated(b1, [2])
+        finish(b0)
+        gather_gated(b1, [1, 2])
         finish(a1)
         gather_gated(b1, [3])
         weave_gate(a2)
         gather_plain(b3, 2)
         weave(b1)
         finish(a2)
-        weave_gate(a3)
         finish(b1)
-        gather_gated(c0, [0])
+        weave_gate(a3)
+        spread_gate(BLOCK)
+        gather_gated(c0, [0, 1, 2])
         finish(a3)
         for g in range(0, 4):
             rectify(g)
-        gather_gated(c0, [1, 2, 3])
+        gather_gated(c0, [3])
         weave_gate(b2)
         gather_plain(c1, 1)
         weave(c0)
         finish(b2)
+        finish(c0)
         for g in range(0, 4):
             square(g)
+            open_sum(7 + g)
         weave_gate(b3)
-        gather_plain(d2, 2)
-        finish(c0)
-        gather_gated(d3, [0])
+        spread_gate(2 * BLOCK)
+        gather_gated(d3, [0, 1, 2])
         finish(b3)
         for g in range(4, 8):
             rectify(g)
-        gather_gated(d3, [1, 2, 3])
+        gather_gated(d3, [3])
         weave_gate(c1)
         gather_plain(e2, 1)
         weave(d3)
         finish(c1)
-        weave_gate(d2)
+        gather_gated(d2, range(PACK))
         finish(d3)
+        weave(d2)
         gather_gated(f3, [0])
         finish(d2)
         rectify(8)
@@ -296,6 +333,7 @@ def tile_moe_pre_mlp_relu2_kernel(
             square(g)
         gather_gated(f3, [1, 2, 3])
         weave_gate(e2)
+        open_sum(11)
         weave(f3)
         finish(e2)
         gather_gated(g3, [0])
@@ -319,9 +357,9 @@ def tile_moe_pre_mlp_relu2_kernel(
         quantise_h(SLOTS - C, GROUP)
         second_layer(SLOTS - C, GROUP, banks[6], C)
         quantise_h(SLOTS - GROUP, GROUP)
-        second_layer(SLOTS - GROUP, GROUP, banks[7], 0)
+        second_layer(SLOTS - GROUP, GROUP, banks[0], 0)
         nc.scalar.copy(y_sb[:, 2 * BLOCK:SLOTS - GROUP], banks[6][:, :C + GROUP])
-        nc.vector.tensor_copy(y_sb[:, SLOTS - GROUP:], banks[7][:, :GROUP])
+        nc.vector.tensor_copy(y_sb[:, SLOTS - GROUP:], banks[0][:, :GROUP])
 
         half, quarter = T // 2, T // 4
         first = keep.tile([P, T], F32, name="first")

@@ -82,9 +82,7 @@ def tile_moe_pre_mlp_relu2_kernel(
         nc.vector.memset(warm[:, :8], 0.0)
         nc.scalar.activation(warm[:, 8:9], warm[:, 0:1], ACT.Copy)
 
-        gate_rows = keep.tile([P, GROUP], F32, name="gate_rows")
-        gate_cols = keep.tile([P, GROUPS], F32, name="gate_cols")
-        nc.gpsimd.memset(gate_rows[:], 0.0)
+        gate_cols = keep.tile([P, SLOTS // BLOCK, RUN], F32, name="gate_cols")
         make_identity(nc, ident[:])
         nc.vector.memset(w1_sc[0][:].bitcast(I32), 0)
         nc.vector.memset(w1_sc[1][:].bitcast(I32), 0)
@@ -94,21 +92,21 @@ def tile_moe_pre_mlp_relu2_kernel(
         load_x(0, 0)
         nc.sync.dma_start(offs_sb[:], offs)
         load_gate(nc.scalar, BLOCK, BLOCK + C)
+        nc.scalar.dma_start(out=gate_cols[:], in_=gate[0, :].rearrange("(b c i) -> c b i", c=P, i=RUN))
         load_gate(nc.sync, BLOCK + C, 2 * BLOCK)
         load_x(0, 1)
-        nc.sync.dma_start(out=gate_rows[:GROUPS, :], in_=gate[0, :].rearrange("(g j) -> g j", j=GROUP))
         for t in range(2, PACK):
             load_x(0, t)
-        load_gate(nc.sync, 0, POOL_SLOTS)
+        load_gate(nc.sync, 0, BLOCK)
         for s in range(1, PASSES):
             for t in range(PACK):
                 load_x(s, t)
+            if s == 2:
+                load_gate(nc.sync, 2 * BLOCK, SLOTS)
         for u in range(E // 2):
             load_w1_scales(u)
             load_w1(2 * u)
             load_w1(2 * u + 1)
-            if u == 0:
-                load_gate(nc.sync, 2 * BLOCK, SLOTS)
         load_scale_rows(w2_sc, w2_scales.rearrange("e s (q r) n -> r q (e s) n", r=4))
         nc.sync.dma_start(
             out=w2_sb[:].bitcast(I32), in_=w2_words.rearrange("e s p b -> p (e s) b").bitcast(I32)
@@ -123,9 +121,9 @@ def tile_moe_pre_mlp_relu2_kernel(
 
         plain = [keep.tile([P, PACK * BLOCK], F32, name="plain%d" % u) for u in range(3)]
 
-        def gather_plain(unit, buffer):
+        def gather_plain(unit, buffer, start=0):
             j0, n, s = unit
-            picked[unit] = plain[buffer][:, :PACK * n].rearrange("p (t j) -> p t j", t=PACK)
+            picked[unit] = plain[buffer][:, start:start + PACK * n].rearrange("p (t j) -> p t j", t=PACK)
             for t in range(PACK):
                 nc.scalar.activation(picked[unit][:, t, :], window(s, t, j0, j0 + n), ACT.Copy)
 
@@ -159,26 +157,27 @@ def tile_moe_pre_mlp_relu2_kernel(
 
         banks = [psum.tile([P, H], F32, name="bank%d" % u) for u in range(8)]
         acc = [banks[u] for u in (0, 1, 2, 3, 4, 5, 6, 0, 1, 2, 3, 7)]
-        gate_bank = banks[7]
+        gate_banks = [banks[7], banks[6], banks[7]]
 
         def spread_gate(j0):
-            for g in range(BLOCK // GROUP):
-                column = gate_cols[:, j0 // GROUP + g:j0 // GROUP + g + 1].to_broadcast([P, P])
-                nc.tensor.transpose(gate_bank[:, g * GROUP:(g + 1) * GROUP], column, ident[:])
+            for i in range(RUN):
+                column = gate_cols[:, j0 // BLOCK, i:i + 1].to_broadcast([P, P])
+                nc.tensor.transpose(gate_banks[j0 // BLOCK][:, i * P:(i + 1) * P], column, ident[:])
 
         def weave_gate(unit):
             j0, n, s = unit
-            rounded[unit] = shared[:, :n, :]
+            rounded[unit] = shared[:, C:C + n, :] if n == GROUP else shared[:, :n, :]
             m = POOL_SLOTS if n == BLOCK else 0
             if n == BLOCK:
                 weights = gate_sb[:, j0:j0 + m].unsqueeze(2).to_broadcast([P, m, PACK])
                 planes = picked[unit][:, :, :m].rearrange("p t j -> p j t")
                 nc.gpsimd.tensor_tensor(rounded[unit][:, :m, :], planes, weights, MULT)
             first = j0 % BLOCK
-            weights = gate_bank[:, first + m:first + n].rearrange("p (c i) -> p c i", i=RUN).unsqueeze(2)
+            spread = gate_banks[j0 // BLOCK][:].rearrange("p (i c) -> p c i", i=RUN)
+            weights = spread[:, (first + m) // RUN:(first + n) // RUN, :].unsqueeze(2)
             nc.vector.tensor_tensor(*woven(unit, m, n), weights.to_broadcast([P, (n - m) // RUN, PACK, RUN]), MULT)
 
-        waiting = {g: [] for g in range(7, GROUPS)}
+        waiting = {g: [] for g in range(6, GROUPS)}
         done = {g: 0 for g in range(GROUPS)}
 
         late = {
@@ -273,14 +272,15 @@ def tile_moe_pre_mlp_relu2_kernel(
         held = {c0: 0, d3: BLOCK, d2: BLOCK + C}
         gated_place = {d2: PACK * C, g3: PACK * GROUP}
 
-        nc.tensor.transpose(banks[6][:, :GROUP], gate_rows[:], ident[:])
-        nc.vector.tensor_copy(gate_cols[:], banks[6][:, :GROUPS])
         spread_gate(0)
+        spread_gate(BLOCK)
         gather_plain(a0, 0)
         gather_gated(b0, range(PACK), [BLOCK, BLOCK + C, 2 * BLOCK])
         gather_plain(a1, 1)
         gather_plain(a2, 2)
-        weave_gate(a0)
+        rounded[a0] = shared[:]
+        weights = gate_sb[:, :BLOCK].rearrange("p (c i) -> p c i", i=RUN).unsqueeze(2)
+        nc.vector.tensor_tensor(*woven(a0, 0, BLOCK), weights.to_broadcast([P, BLOCK // RUN, PACK, RUN]), MULT)
         gather_plain(a3, 0)
         weave(b0)
         finish(a0)
@@ -297,7 +297,7 @@ def tile_moe_pre_mlp_relu2_kernel(
         finish(a2)
         finish(b1)
         weave_gate(a3)
-        spread_gate(BLOCK)
+        spread_gate(2 * BLOCK)
         gather_gated(c0, [0, 1, 2])
         finish(a3)
         for g in range(0, 4):
@@ -312,7 +312,7 @@ def tile_moe_pre_mlp_relu2_kernel(
             square(g)
             open_sum(7 + g)
         weave_gate(b3)
-        spread_gate(2 * BLOCK)
+        open_sum(6)
         gather_gated(d3, [0, 1, 2])
         finish(b3)
         for g in range(4, 8):
@@ -320,25 +320,26 @@ def tile_moe_pre_mlp_relu2_kernel(
         gather_gated(d3, [3])
         weave_gate(c1)
         gather_plain(e2, 1)
+        gather_plain(f3, 1, PACK * C)
         weave(d3)
         finish(c1)
         gather_gated(d2, range(PACK))
         finish(d3)
         weave(d2)
-        gather_gated(f3, [0])
+        weave_gate(e2)
         finish(d2)
         rectify(8)
         rectify(9)
-        for g in range(4, 10):
-            square(g)
-        gather_gated(f3, [1, 2, 3])
-        weave_gate(e2)
+        weave_gate(f3)
         open_sum(11)
-        weave(f3)
         finish(e2)
         gather_gated(g3, [0])
         finish(f3)
+        for g in range(4, 8):
+            square(g)
         rectify(10)
+        square(8)
+        square(9)
         gather_gated(g3, [1, 2, 3])
         weave(g3)
         quantise_h(0, C)
@@ -361,24 +362,26 @@ def tile_moe_pre_mlp_relu2_kernel(
         nc.scalar.copy(y_sb[:, 2 * BLOCK:SLOTS - GROUP], banks[6][:, :C + GROUP])
         nc.vector.tensor_copy(y_sb[:, SLOTS - GROUP:], banks[0][:, :GROUP])
 
-        half, quarter = T // 2, T // 4
+        quarter = T // 4
+        head, middle, rest = slice(0, quarter), slice(quarter, 2 * quarter), slice(2 * quarter, T)
         first = keep.tile([P, T], F32, name="first")
+        second = keep.tile([P, T], F32, name="second")
         part = keep.tile([P, T], F32, name="part")
-        more = keep.tile([P, half], F32, name="more")
         total = keep.tile([P, T], F32, name="total")
 
-        def fetched(r, t0, t1):
-            return y_sb[:].indirect(pos_sb[r][:, t0 // PER_COLUMN:t1 // PER_COLUMN])
+        def fetched(r, cols):
+            return y_sb[:].indirect(pos_sb[r][:, cols.start // PER_COLUMN:cols.stop // PER_COLUMN])
 
-        for t0, t1 in ((half, half + quarter), (half + quarter, T), (0, half)):
-            nc.scalar.activation(first[:, t0:t1], fetched(0, t0, t1), ACT.Copy)
-        nc.vector.tensor_copy(part[:, :half], fetched(1, 0, half))
-        lo, hi = slice(half, half + quarter), slice(half + quarter, T)
-        nc.vector.tensor_tensor(part[:, lo], fetched(1, lo.start, lo.stop), first[:, lo], ADD)
-        nc.vector.tensor_tensor(more[:], fetched(2, 0, half), part[:, :half], ADD)
-        nc.vector.tensor_tensor(part[:, hi], fetched(1, hi.start, hi.stop), first[:, hi], ADD)
-        nc.vector.tensor_tensor(total[:, :half], more[:], first[:, :half], ADD)
-        nc.vector.tensor_tensor(total[:, lo], fetched(2, lo.start, lo.stop), part[:, lo], ADD)
-        nc.vector.tensor_tensor(total[:, hi], fetched(2, hi.start, hi.stop), part[:, hi], ADD)
-        for cols, queue in zip((slice(0, half), lo, hi), (nc.sync, nc.scalar, nc.sync)):
+        nc.scalar.activation(first[:, middle], fetched(0, middle), ACT.Copy)
+        nc.scalar.activation(first[:, rest], fetched(0, rest), ACT.Copy)
+        nc.scalar.activation(second[:, rest], fetched(1, rest), ACT.Copy)
+        nc.scalar.activation(first[:, head], fetched(0, head), ACT.Copy)
+        nc.vector.tensor_copy(second[:, head], fetched(1, head))
+        nc.vector.tensor_tensor(part[:, head], fetched(2, head), second[:, head], ADD)
+        nc.vector.tensor_tensor(part[:, middle], fetched(1, middle), first[:, middle], ADD)
+        nc.vector.tensor_tensor(part[:, rest], fetched(2, rest), first[:, rest], ADD)
+        nc.vector.tensor_tensor(total[:, middle], fetched(2, middle), part[:, middle], ADD)
+        nc.vector.tensor_tensor(total[:, rest], part[:, rest], second[:, rest], ADD)
+        nc.vector.tensor_tensor(total[:, head], part[:, head], first[:, head], ADD)
+        for cols, queue in zip((middle, rest, head), (nc.sync, nc.scalar, nc.sync)):
             queue.dma_start(out=out[:, cols], in_=total[:, cols])

@@ -156,28 +156,32 @@ def tile_moe_pre_mlp_relu2_kernel(
             nc.vector.tensor_copy(*woven(unit, 0, n))
 
         banks = [psum.tile([P, H], F32, name="bank%d" % u) for u in range(8)]
-        acc = [banks[u] for u in (0, 1, 2, 3, 4, 5, 6, 0, 1, 2, 3, 7)]
-        gate_banks = [banks[7], banks[6], banks[7]]
+        acc = [banks[u] for u in (0, 1, 2, 3, 4, 7, 6, 0, 1, 2, 3, 5)]
+        gate_banks = [banks[7], banks[6], banks[5]]
 
         def spread_gate(j0):
             for i in range(RUN):
                 column = gate_cols[:, j0 // BLOCK, i:i + 1].to_broadcast([P, P])
                 nc.tensor.transpose(gate_banks[j0 // BLOCK][:, i * P:(i + 1) * P], column, ident[:])
 
-        def weave_gate(unit):
+        def weave_shared(unit):
             j0, n, s = unit
-            rounded[unit] = shared[:, C:C + n, :] if n == GROUP else shared[:, :n, :]
-            m = POOL_SLOTS if n == BLOCK else 0
-            if n == BLOCK:
-                weights = gate_sb[:, j0:j0 + m].unsqueeze(2).to_broadcast([P, m, PACK])
-                planes = picked[unit][:, :, :m].rearrange("p t j -> p j t")
-                nc.gpsimd.tensor_tensor(rounded[unit][:, :m, :], planes, weights, MULT)
-            first = j0 % BLOCK
+            rounded[unit] = shared[:]
+            m = POOL_SLOTS
+            weights = gate_sb[:, j0:j0 + m].unsqueeze(2).to_broadcast([P, m, PACK])
+            planes = picked[unit][:, :, :m].rearrange("p t j -> p j t")
+            nc.gpsimd.tensor_tensor(rounded[unit][:, :m, :], planes, weights, MULT)
             spread = gate_banks[j0 // BLOCK][:].rearrange("p (i c) -> p c i", i=RUN)
-            weights = spread[:, (first + m) // RUN:(first + n) // RUN, :].unsqueeze(2)
+            weights = spread[:, m // RUN:, :].unsqueeze(2)
             nc.vector.tensor_tensor(*woven(unit, m, n), weights.to_broadcast([P, (n - m) // RUN, PACK, RUN]), MULT)
 
-        waiting = {g: [] for g in range(6, GROUPS)}
+        def weave_gate(unit, start=0):
+            j0, n, s = unit
+            rounded[unit] = shared[:, start:start + n, :]
+            weights = gate_sb[:, j0:j0 + n].rearrange("p (c i) -> p c i", i=RUN).unsqueeze(2)
+            nc.vector.tensor_tensor(*woven(unit, 0, n), weights.to_broadcast([P, n // RUN, PACK, RUN]), MULT)
+
+        waiting = {g: [] for g in range(5, GROUPS)}
         done = {g: 0 for g in range(GROUPS)}
 
         late = {
@@ -220,17 +224,20 @@ def tile_moe_pre_mlp_relu2_kernel(
             for s in waiting.pop(g):
                 multiply(g, s)
 
-        def finish(unit):
+        def finish(unit, opens=()):
             j0, n, s = unit
             quantise_x(unit)
             for g in range(j0 // GROUP, (j0 + n) // GROUP):
-                multiply(g, s)
+                earlier = waiting.pop(g) if g in opens else []
+                for u in [s] + earlier:
+                    multiply(g, u)
 
         def rectify(g):
             relu = four.tile([P, PACK, P], F32, name="relu")
             planes = acc[g][:].rearrange("j (p t) -> j t p", t=PACK)
             if g == GROUPS - 1:
-                nc.vector.tensor_scalar_max(relu[:], planes, 0.0)
+                for t in (0, 2):
+                    nc.vector.tensor_scalar_max(relu[:, t:t + 2, :], planes[:, t:t + 2, :], 0.0)
             else:
                 nc.scalar.activation(relu[:], planes, ACT.Relu)
             turned = acc[g][:].rearrange("p (t j) -> p t j", t=PACK)
@@ -274,73 +281,71 @@ def tile_moe_pre_mlp_relu2_kernel(
 
         spread_gate(0)
         spread_gate(BLOCK)
+        spread_gate(2 * BLOCK)
         gather_plain(a0, 0)
         gather_gated(b0, range(PACK), [BLOCK, BLOCK + C, 2 * BLOCK])
         gather_plain(a1, 1)
         gather_plain(a2, 2)
-        rounded[a0] = shared[:]
-        weights = gate_sb[:, :BLOCK].rearrange("p (c i) -> p c i", i=RUN).unsqueeze(2)
-        nc.vector.tensor_tensor(*woven(a0, 0, BLOCK), weights.to_broadcast([P, BLOCK // RUN, PACK, RUN]), MULT)
+        weave_gate(a0)
         gather_plain(a3, 0)
         weave(b0)
         finish(a0)
         gather_gated(b1, [0])
-        weave_gate(a1)
+        weave_shared(a1)
         gather_plain(b2, 1)
         finish(b0)
         gather_gated(b1, [1, 2])
         finish(a1)
         gather_gated(b1, [3])
-        weave_gate(a2)
+        weave_shared(a2)
         gather_plain(b3, 2)
         weave(b1)
         finish(a2)
         finish(b1)
-        weave_gate(a3)
-        spread_gate(2 * BLOCK)
+        weave_shared(a3)
+        open_sum(5)
         gather_gated(c0, [0, 1, 2])
         finish(a3)
         for g in range(0, 4):
             rectify(g)
         gather_gated(c0, [3])
-        weave_gate(b2)
+        weave_shared(b2)
         gather_plain(c1, 1)
         weave(c0)
         finish(b2)
         finish(c0)
         for g in range(0, 4):
             square(g)
-            open_sum(7 + g)
-        weave_gate(b3)
+        weave_shared(b3)
         open_sum(6)
         gather_gated(d3, [0, 1, 2])
-        finish(b3)
+        finish(b3, [7])
         for g in range(4, 8):
             rectify(g)
         gather_gated(d3, [3])
-        weave_gate(c1)
+        weave_shared(c1)
         gather_plain(e2, 1)
         gather_plain(f3, 1, PACK * C)
         weave(d3)
-        finish(c1)
+        finish(c1, [8, 9, 10, 11])
         gather_gated(d2, range(PACK))
         finish(d3)
         weave(d2)
-        weave_gate(e2)
+        gather_gated(g3, [0])
         finish(d2)
         rectify(8)
         rectify(9)
-        weave_gate(f3)
-        open_sum(11)
+        weave_gate(e2)
+        weave_gate(f3, C)
         finish(e2)
-        gather_gated(g3, [0])
+        gather_gated(g3, [1])
         finish(f3)
         for g in range(4, 8):
             square(g)
         rectify(10)
         square(8)
         square(9)
-        gather_gated(g3, [1, 2, 3])
+        gather_gated(g3, [2, 3])
         weave(g3)
         quantise_h(0, C)
         finish(g3)
@@ -350,11 +355,11 @@ def tile_moe_pre_mlp_relu2_kernel(
         quantise_h(C, C)
         second_layer(0, BLOCK, banks[4], 0)
         quantise_h(BLOCK, BLOCK)
-        second_layer(BLOCK, BLOCK, banks[5], 0)
+        second_layer(BLOCK, BLOCK, banks[7], 0)
         nc.vector.tensor_copy(y_sb[:, :BLOCK], banks[4][:])
         quantise_h(2 * BLOCK, C)
         second_layer(2 * BLOCK, C, banks[6], 0)
-        nc.vector.tensor_copy(y_sb[:, BLOCK:2 * BLOCK], banks[5][:])
+        nc.vector.tensor_copy(y_sb[:, BLOCK:2 * BLOCK], banks[7][:])
         quantise_h(SLOTS - C, GROUP)
         second_layer(SLOTS - C, GROUP, banks[6], C)
         quantise_h(SLOTS - GROUP, GROUP)

@@ -30,7 +30,6 @@ GROUP = 128
 GROUPS = SLOTS // GROUP
 BLOCK = 512
 WINDOW = T + PER_COLUMN
-POOL_SLOTS = 128
 
 
 def tile_moe_pre_mlp_relu2_kernel(
@@ -39,7 +38,6 @@ def tile_moe_pre_mlp_relu2_kernel(
     nc = tc.nc
     with ExitStack() as ctx:
         keep = ctx.enter_context(tc.tile_pool(name="keep", bufs=1))
-        stage = ctx.enter_context(tc.tile_pool(name="stage", bufs=3))
         four = ctx.enter_context(tc.tile_pool(name="four", bufs=4))
         psum = ctx.enter_context(tc.psum_pool(name="psum", bufs=1))
 
@@ -51,8 +49,8 @@ def tile_moe_pre_mlp_relu2_kernel(
         w1_sc = [keep.tile([P, 2 * PASSES, H], U8, name="w1_sc%d" % u, align_bytes=64) for u in range(E // 2)]
         w2_sb = keep.tile([P, E, 2 * N], U8, name="w2_sb", align_bytes=64)
         w2_sc = keep.tile([P, E, N], U8, name="w2_sc", align_bytes=64)
-        codes = keep.tile([P, PASSES * SLOTS], U32, name="codes", align_bytes=64)
-        scales = keep.tile([P, PASSES * SLOTS], U8, name="scales", align_bytes=64)
+        codes = keep.tile([P, PASSES * SLOTS - C], U32, name="codes", align_bytes=64)
+        scales = keep.tile([P, PASSES * SLOTS - C], U8, name="scales", align_bytes=64)
         h_codes = keep.tile([P, SLOTS], U32, name="h_codes", align_bytes=64)
         h_scales = keep.tile([P, SLOTS], U8, name="h_scales", align_bytes=64)
         h_bf = keep.tile([P, SLOTS, PACK], BF16, name="h_bf", align_bytes=64)
@@ -82,7 +80,18 @@ def tile_moe_pre_mlp_relu2_kernel(
         nc.vector.memset(warm[:, :8], 0.0)
         nc.scalar.activation(warm[:, 8:9], warm[:, 0:1], ACT.Copy)
 
-        gate_cols = keep.tile([P, SLOTS // BLOCK, RUN], F32, name="gate_cols")
+        wide = [keep.tile([P, PACK * 2 * BLOCK], F32, name="wide%d" % u) for u in range(3)]
+        wide = [tile[:].rearrange("p (t j) -> p t j", t=PACK) for tile in wide]
+        rows = keep.tile([P, 2 * PACK * BLOCK], F32, name="rows")
+        narrow = rows[:].rearrange("p (u t j) -> p u t j", u=2, t=PACK)
+        seams = rows[:].rearrange("p (u h j) -> p u h j", u=2, h=2)[:, :, :, BLOCK - 1:BLOCK + 1]
+        first_cols = keep.tile([P, 2, 2], F32, name="first_cols")
+        gate_cols = [first_cols[:], seams[:, 0], seams[:, 1]]
+
+        def load_gate_cols(queue, block):
+            row = gate[0, block * BLOCK:(block + 1) * BLOCK]
+            queue.dma_start(out=gate_cols[block], in_=row.rearrange("(c h e) -> c h e", h=2, e=2))
+
         make_identity(nc, ident[:])
         nc.vector.memset(w1_sc[0][:].bitcast(I32), 0)
         nc.vector.memset(w1_sc[1][:].bitcast(I32), 0)
@@ -91,18 +100,16 @@ def tile_moe_pre_mlp_relu2_kernel(
 
         load_x(0, 0)
         nc.sync.dma_start(offs_sb[:], offs)
-        load_gate(nc.scalar, BLOCK, BLOCK + C)
-        nc.scalar.dma_start(out=gate_cols[:], in_=gate[0, :].rearrange("(b c i) -> c b i", c=P, i=RUN))
-        load_gate(nc.sync, BLOCK + C, 2 * BLOCK)
-        load_x(0, 1)
-        for t in range(2, PACK):
+        load_gate_cols(nc.scalar, 0)
+        for t in range(1, PACK):
             load_x(0, t)
-        load_gate(nc.sync, 0, BLOCK)
+        load_gate(nc.sync, 0, 2 * BLOCK)
         for s in range(1, PASSES):
             for t in range(PACK):
                 load_x(s, t)
-            if s == 2:
-                load_gate(nc.sync, 2 * BLOCK, SLOTS)
+        load_gate_cols(nc.sync, 1)
+        load_gate_cols(nc.sync, 2)
+        load_gate(nc.sync, 2 * BLOCK, SLOTS)
         for u in range(E // 2):
             load_w1_scales(u)
             load_w1(2 * u)
@@ -114,46 +121,72 @@ def tile_moe_pre_mlp_relu2_kernel(
         for tile, pos in zip(pos_sb, (pos1, pos2, pos3)):
             nc.sync.dma_start(tile[:], pos)
 
-        picked, rounded = {}, {}
+        a0, a1, a2, a3 = [(0, BLOCK, s) for s in range(PASSES)]
+        b0, b1, b2, b3 = [(BLOCK, BLOCK, s) for s in range(PASSES)]
+        c0, c1, c2 = [(2 * BLOCK, BLOCK, s) for s in range(3)]
+        d2, d3 = [(2 * BLOCK, C, s) for s in (2, 3)]
+        e2 = (SLOTS - C, C, 2)
+        f3, g3 = (SLOTS - C, GROUP, 3), (SLOTS - GROUP, GROUP, 3)
+
+        gathered = {
+            a0: (wide[0], 0), b0: (wide[0], BLOCK), c0: (wide[0], C), f3: (wide[0], C),
+            a1: (wide[1], 0), b1: (wide[1], BLOCK), c1: (narrow[:, 0], 0), g3: (narrow[:, 0], 0),
+            a3: (wide[2], 0), a2: (wide[2], BLOCK), c2: (wide[2], C), d2: (wide[2], C), e2: (wide[2], BLOCK),
+            b3: (narrow[:, 0], 0), b2: (narrow[:, 1], 0), d3: (narrow[:, 1], 0),
+        }
+        line = keep.tile([P, 13 * GROUP, PACK], BF16, name="line", align_bytes=64)
+        batches = [
+            (264, [(0, 8, 0)]),
+            (0, [(0, 4, 2), (0, 2, 1), (0, 4, 3), (2, 2, 1)]),
+            (128, [(5, 3, 1), (4, 4, 3), (4, 4, 2), (4, 1, 1)]),
+            (128, [(8, 2, 2), (8, 4, 1), (8, 4, 0), (8, 2, 3)]),
+            (640, [(10, 2, 2), (10, 2, 3)]),
+        ]
+        place, column, first_column, filled = {}, {}, [], 0
+        for start, pieces in batches:
+            first_column.append(filled)
+            for g0, count, s in pieces:
+                for g in range(g0, g0 + count):
+                    place[g, s], column[g, s] = start, filled
+                    start, filled = start + GROUP, filled + GROUP
 
         def window(s, t, a, b):
             return x_sb[PACK * s + t][:].indirect(offs_sb[:, a // PER_COLUMN:b // PER_COLUMN])
 
-        plain = [keep.tile([P, PACK * BLOCK], F32, name="plain%d" % u) for u in range(3)]
+        def planes(unit, a, b):
+            tile, start = gathered[unit]
+            return tile[:, :, start + a:start + b]
 
-        def gather_plain(unit, buffer, start=0):
+        def rounded(unit, a, b):
             j0, n, s = unit
-            picked[unit] = plain[buffer][:, start:start + PACK * n].rearrange("p (t j) -> p t j", t=PACK)
+            start = place[(j0 + a) // GROUP, s] + a % GROUP
+            return line[:, start:start + b - a, :]
+
+        def gather_scalar(unit):
+            j0, n, s = unit
             for t in range(PACK):
-                nc.scalar.activation(picked[unit][:, t, :], window(s, t, j0, j0 + n), ACT.Copy)
+                nc.scalar.activation(planes(unit, 0, n)[:, t, :], window(s, t, j0, j0 + n), ACT.Copy)
 
-        gated = keep.tile([P, PACK * BLOCK], F32, name="gated")
-        shared = keep.tile([P, BLOCK, PACK], BF16, name="shared", align_bytes=64)
-
-        def gather_gated(unit, planes, cuts=None):
+        def gather_vector(unit):
             j0, n, s = unit
-            start = gated_place.get(unit, 0)
-            picked[unit] = gated[:, start:start + PACK * n].rearrange("p (t j) -> p t j", t=PACK)
-            for t in planes:
-                ends = cuts if cuts and t == 0 else [j0, j0 + n]
-                for a, b in zip(ends, ends[1:]):
-                    nc.vector.tensor_tensor(
-                        picked[unit][:, t, a - j0:b - j0], window(s, t, a, b), gate_sb[:, a:b], MULT
-                    )
+            for t in range(PACK):
+                nc.vector.tensor_copy(planes(unit, 0, n)[:, t, :], window(s, t, j0, j0 + n))
+
+        def gather_gated(unit, ts):
+            j0, n, s = unit
+            for t in ts:
+                nc.vector.tensor_tensor(
+                    planes(unit, 0, n)[:, t, :], window(s, t, j0, j0 + n), gate_sb[:, j0:j0 + n], MULT
+                )
 
         def woven(unit, a, b):
             return (
-                rounded[unit][:, a:b, :].rearrange("p (c i) t -> p c t i", i=RUN),
-                picked[unit][:, :, a:b].rearrange("p t (c i) -> p c t i", i=RUN),
+                rounded(unit, a, b).rearrange("p (c i) t -> p c t i", i=RUN),
+                planes(unit, a, b).rearrange("p t (c i) -> p c t i", i=RUN),
             )
 
         def weave(unit):
-            j0, n, s = unit
-            if unit in held:
-                rounded[unit] = h_bf[:, held[unit]:held[unit] + n, :]
-            else:
-                rounded[unit] = stage.tile([P, n, PACK], BF16, name="rounded", align_bytes=64)[:]
-            nc.vector.tensor_copy(*woven(unit, 0, n))
+            nc.vector.tensor_copy(*woven(unit, 0, unit[1]))
 
         banks = [psum.tile([P, H], F32, name="bank%d" % u) for u in range(8)]
         acc = [banks[u] for u in (0, 1, 2, 3, 4, 7, 6, 0, 1, 2, 3, 5)]
@@ -161,27 +194,27 @@ def tile_moe_pre_mlp_relu2_kernel(
 
         def spread_gate(j0):
             for i in range(RUN):
-                column = gate_cols[:, j0 // BLOCK, i:i + 1].to_broadcast([P, P])
-                nc.tensor.transpose(gate_banks[j0 // BLOCK][:, i * P:(i + 1) * P], column, ident[:])
+                col = gate_cols[j0 // BLOCK][:, i // 2, i % 2:i % 2 + 1].to_broadcast([P, P])
+                nc.tensor.transpose(gate_banks[j0 // BLOCK][:, i * P:(i + 1) * P], col, ident[:])
 
-        def weave_shared(unit):
-            j0, n, s = unit
-            rounded[unit] = shared[:]
-            m = POOL_SLOTS
-            weights = gate_sb[:, j0:j0 + m].unsqueeze(2).to_broadcast([P, m, PACK])
-            planes = picked[unit][:, :, :m].rearrange("p t j -> p j t")
-            nc.gpsimd.tensor_tensor(rounded[unit][:, :m, :], planes, weights, MULT)
-            spread = gate_banks[j0 // BLOCK][:].rearrange("p (i c) -> p c i", i=RUN)
-            weights = spread[:, m // RUN:, :].unsqueeze(2)
-            nc.vector.tensor_tensor(*woven(unit, m, n), weights.to_broadcast([P, (n - m) // RUN, PACK, RUN]), MULT)
+        def weave_pool(unit, a, b):
+            j0 = unit[0]
+            weights = gate_sb[:, j0 + a:j0 + b].unsqueeze(2).to_broadcast([P, b - a, PACK])
+            nc.gpsimd.tensor_tensor(
+                rounded(unit, a, b), planes(unit, a, b).rearrange("p t j -> p j t"), weights, MULT
+            )
 
-        def weave_gate(unit, start=0):
+        def weave_vector(unit, a, b):
+            j0 = unit[0] % BLOCK
+            spread = gate_banks[unit[0] // BLOCK][:].rearrange("p (i c) -> p c i", i=RUN)
+            weights = spread[:, (j0 + a) // RUN:(j0 + b) // RUN, :].unsqueeze(2)
+            nc.vector.tensor_tensor(*woven(unit, a, b), weights.to_broadcast([P, (b - a) // RUN, PACK, RUN]), MULT)
+
+        def weave_gate(unit):
             j0, n, s = unit
-            rounded[unit] = shared[:, start:start + n, :]
             weights = gate_sb[:, j0:j0 + n].rearrange("p (c i) -> p c i", i=RUN).unsqueeze(2)
             nc.vector.tensor_tensor(*woven(unit, 0, n), weights.to_broadcast([P, n // RUN, PACK, RUN]), MULT)
 
-        waiting = {g: [] for g in range(5, GROUPS)}
         done = {g: 0 for g in range(GROUPS)}
 
         late = {
@@ -189,26 +222,23 @@ def tile_moe_pre_mlp_relu2_kernel(
             GROUPS - 1: (h_codes[:, BLOCK - 64:BLOCK + 64], h_scales[:, 2 * BLOCK + 64:2 * BLOCK + 64 + GROUP]),
         }
 
-        def x_operand(j0, n, s):
-            if s == PASSES - 1 and j0 // GROUP in late:
-                return late[j0 // GROUP]
-            cols = slice(s * SLOTS + j0, s * SLOTS + j0 + n)
+        def x_operand(g, s, n=GROUP):
+            if s == PASSES - 1 and g in late:
+                return late[g]
+            cols = slice(column[g, s], column[g, s] + n)
             return codes[:, cols], scales[:, cols]
 
-        def quantise_x(unit):
-            words, exponents = x_operand(*unit)
+        def quantise_x(g, s, n):
+            words, exponents = x_operand(g, s, n)
             nc.vector.quantize_mx(
                 out=words.bitcast(FP8X4),
                 scales=exponents,
-                in_=rounded[unit].rearrange("p j t -> p (j t)"),
+                in_=line[:, place[g, s]:place[g, s] + n, :].rearrange("p j t -> p (j t)"),
             )
 
         def multiply(g, s):
-            if g in waiting:
-                waiting[g].append(s)
-                return
             e = g * GROUP // C
-            words, exponents = x_operand(g * GROUP, GROUP, s)
+            words, exponents = x_operand(g, s)
             nc.tensor.matmul_mx(
                 out=acc[g][:],
                 lhsT=words.bitcast(FP8X4),
@@ -220,17 +250,10 @@ def tile_moe_pre_mlp_relu2_kernel(
             )
             done[g] = done[g] + 1
 
-        def open_sum(g):
-            for s in waiting.pop(g):
-                multiply(g, s)
-
-        def finish(unit, opens=()):
-            j0, n, s = unit
-            quantise_x(unit)
-            for g in range(j0 // GROUP, (j0 + n) // GROUP):
-                earlier = waiting.pop(g) if g in opens else []
-                for u in [s] + earlier:
-                    multiply(g, u)
+        def multiply_all(groups, passes):
+            for g in groups:
+                for s in passes:
+                    multiply(g, s)
 
         def rectify(g):
             relu = four.tile([P, PACK, P], F32, name="relu")
@@ -269,86 +292,86 @@ def tile_moe_pre_mlp_relu2_kernel(
                     stop=True,
                 )
 
-        a0, a1, a2, a3 = [(0, BLOCK, s) for s in range(PASSES)]
-        b0, b1, b2, b3 = [(BLOCK, BLOCK, s) for s in range(PASSES)]
-        c0, c1 = [(2 * BLOCK, BLOCK, s) for s in range(2)]
-        d2, d3 = [(2 * BLOCK, C, s) for s in (2, 3)]
-        e2 = (SLOTS - C, C, 2)
-        f3, g3 = (SLOTS - C, GROUP, 3), (SLOTS - GROUP, GROUP, 3)
-
-        held = {c0: 0, d3: BLOCK, d2: BLOCK + C}
-        gated_place = {d2: PACK * C, g3: PACK * GROUP}
-
         spread_gate(0)
         spread_gate(BLOCK)
         spread_gate(2 * BLOCK)
-        gather_plain(a0, 0)
-        gather_gated(b0, range(PACK), [BLOCK, BLOCK + C, 2 * BLOCK])
-        gather_plain(a1, 1)
-        gather_plain(a2, 2)
-        weave_gate(a0)
-        gather_plain(a3, 0)
-        weave(b0)
-        finish(a0)
-        gather_gated(b1, [0])
-        weave_shared(a1)
-        gather_plain(b2, 1)
-        finish(b0)
-        gather_gated(b1, [1, 2])
-        finish(a1)
-        gather_gated(b1, [3])
-        weave_shared(a2)
-        gather_plain(b3, 2)
-        weave(b1)
-        finish(a2)
-        finish(b1)
-        weave_shared(a3)
-        open_sum(5)
-        gather_gated(c0, [0, 1, 2])
-        finish(a3)
+        gather_scalar(a0)
+        gather_vector(b0)
+        gather_scalar(a1)
+        gather_scalar(a2)
+        gather_scalar(a3)
+        gather_scalar(b3)
+        gather_scalar(b2)
+
+        weave_pool(a0, 480, 2 * BLOCK)
+        weave_vector(a0, 0, 480)
+        gather_vector(b1)
+        quantise_x(4, 0, BLOCK)
+        quantise_x(0, 0, BLOCK)
+        multiply_all(range(0, 5), [0])
+
+        weave_pool(a1, 256, 640)
+        weave_pool(a2, 0, 352)
+        weave_vector(a1, 0, 256)
+        gather_vector(c0)
+        weave_vector(a2, 352, BLOCK)
+        weave_vector(a3, 0, BLOCK)
+        quantise_x(0, 2, 2 * BLOCK)
+        quantise_x(2, 3, BLOCK)
+        multiply_all([0, 1], [1, 2, 3])
+        multiply_all([2, 3], [2, 3, 1])
+        multiply(5, 0)
         for g in range(0, 4):
             rectify(g)
-        gather_gated(c0, [3])
-        weave_shared(b2)
-        gather_plain(c1, 1)
-        weave(c0)
-        finish(b2)
-        finish(c0)
+
+        weave_pool(b3, 0, BLOCK)
+        weave_pool(b2, 0, 160)
+        weave_vector(b1, GROUP, BLOCK)
+        gather_vector(c2)
+        weave_vector(b2, 160, BLOCK)
+        gather_scalar(c1)
+        quantise_x(5, 1, 2 * BLOCK)
+        quantise_x(5, 2, BLOCK)
         for g in range(0, 4):
             square(g)
-        weave_shared(b3)
-        open_sum(6)
-        gather_gated(d3, [0, 1, 2])
-        finish(b3, [7])
+        multiply_all([4], [3, 2, 1])
+        multiply_all([5], [3, 1, 2])
+        multiply_all([6, 7], [3, 1, 0, 2])
         for g in range(4, 8):
             rectify(g)
-        gather_gated(d3, [3])
-        weave_shared(c1)
-        gather_plain(e2, 1)
-        gather_plain(f3, 1, PACK * C)
-        weave(d3)
-        finish(c1, [8, 9, 10, 11])
-        gather_gated(d2, range(PACK))
-        finish(d3)
-        weave(d2)
-        gather_gated(g3, [0])
-        finish(d2)
+
+        weave_pool(d2, 0, C)
+        weave_pool(c1, 0, 304)
+        weave_vector(c0, 0, BLOCK)
+        gather_vector(d3)
+        weave_vector(c1, 304, BLOCK)
+        weave_vector(d3, 0, C)
+        gather_scalar(f3)
+        quantise_x(10, 1, 2 * BLOCK)
+        quantise_x(8, 2, BLOCK)
+        for g in range(4, 8):
+            square(g)
+        multiply_all([8, 9], [0, 3, 1, 2])
+        multiply_all([10, 11], [1, 0])
         rectify(8)
         rectify(9)
+
         weave_gate(e2)
-        weave_gate(f3, C)
-        finish(e2)
+        weave_gate(f3)
+        gather_gated(g3, [0])
+        quantise_x(10, 2, C)
+        multiply_all([10, 11], [2])
         gather_gated(g3, [1])
-        finish(f3)
-        for g in range(4, 8):
-            square(g)
+        quantise_x(10, 3, GROUP)
+        multiply(10, 3)
         rectify(10)
         square(8)
         square(9)
         gather_gated(g3, [2, 3])
         weave(g3)
         quantise_h(0, C)
-        finish(g3)
+        quantise_x(11, 3, GROUP)
+        multiply(11, 3)
         rectify(11)
         square(10)
         square(11)

@@ -44,7 +44,7 @@ def tile_moe_pre_mlp_relu2_kernel(
         offs_sb = keep.tile([P, SLOTS // PER_COLUMN], U16, name="offs_sb")
         pos_sb = [keep.tile([P, T // PER_COLUMN], U16, name="pos_sb%d" % r) for r in range(3)]
         gate_sb = keep.tile([P, SLOTS], F32, name="gate_sb")
-        x_sb = [keep.tile([P, WINDOW], F32, name="x_sb%d" % b) for b in range(PASSES * PACK)]
+        x_sb = [keep.tile([P, WINDOW], F32, name="x_sb%d" % b, align_bytes=64) for b in range(PASSES * PACK)]
         w1_sb = [keep.tile([P, PASSES, 2 * H], U8, name="w1_sb%d" % e, align_bytes=64) for e in range(E)]
         w1_sc = [keep.tile([P, 2 * PASSES, H], U8, name="w1_sc%d" % u, align_bytes=64) for u in range(E // 2)]
         w2_sb = keep.tile([P, E, 2 * N], U8, name="w2_sb", align_bytes=64)
@@ -53,7 +53,7 @@ def tile_moe_pre_mlp_relu2_kernel(
         scales = keep.tile([P, PASSES * SLOTS - C], U8, name="scales", align_bytes=64)
         h_codes = keep.tile([P, SLOTS], U32, name="h_codes", align_bytes=64)
         h_scales = keep.tile([P, SLOTS], U8, name="h_scales", align_bytes=64)
-        h_bf = keep.tile([P, SLOTS, PACK], BF16, name="h_bf", align_bytes=64)
+        h_bf = keep.tile([P, 2 * BLOCK, PACK], BF16, name="h_bf", align_bytes=64)
         y_sb = keep.tile([P, SLOTS], F32, name="y_sb", align_bytes=64)
         ident = keep.tile([P, P], F32, name="ident")
 
@@ -126,11 +126,11 @@ def tile_moe_pre_mlp_relu2_kernel(
         c0, c1, c2 = [(2 * BLOCK, BLOCK, s) for s in range(3)]
         d2, d3 = [(2 * BLOCK, C, s) for s in (2, 3)]
         e2 = (SLOTS - C, C, 2)
-        f3, g3 = (SLOTS - C, GROUP, 3), (SLOTS - GROUP, GROUP, 3)
+        e3 = (SLOTS - C, C, 3)
 
         gathered = {
-            a0: (wide[0], 0), b0: (wide[0], BLOCK), c0: (wide[0], C), f3: (wide[0], C),
-            a1: (wide[1], 0), b1: (wide[1], BLOCK), c1: (narrow[:, 0], 0), g3: (narrow[:, 0], 0),
+            a0: (wide[0], 0), b0: (wide[0], BLOCK), c0: (wide[0], C),
+            a1: (wide[1], 0), b1: (wide[1], BLOCK), c1: (wide[1], 0), e3: (narrow[:, 0], 0),
             a3: (wide[2], 0), a2: (wide[2], BLOCK), c2: (wide[2], C), d2: (wide[2], C), e2: (wide[2], BLOCK),
             b3: (narrow[:, 0], 0), b2: (narrow[:, 1], 0), d3: (narrow[:, 1], 0),
         }
@@ -139,8 +139,9 @@ def tile_moe_pre_mlp_relu2_kernel(
             (264, [(0, 8, 0)]),
             (0, [(0, 4, 2), (0, 2, 1), (0, 4, 3), (2, 2, 1)]),
             (128, [(5, 3, 1), (4, 4, 3), (4, 4, 2), (4, 1, 1)]),
-            (128, [(8, 2, 2), (8, 4, 1), (8, 4, 0), (8, 2, 3)]),
-            (640, [(10, 2, 2), (10, 2, 3)]),
+            (128, [(8, 2, 2), (8, 2, 0), (8, 2, 1), (8, 2, 3)]),
+            (128, [(10, 2, 0), (10, 2, 2), (10, 2, 1)]),
+            (768, [(10, 2, 3)]),
         ]
         place, column, first_column, filled = {}, {}, [], 0
         for start, pieces in batches:
@@ -172,21 +173,11 @@ def tile_moe_pre_mlp_relu2_kernel(
             for t in range(PACK):
                 nc.vector.tensor_copy(planes(unit, 0, n)[:, t, :], window(s, t, j0, j0 + n))
 
-        def gather_gated(unit, ts):
-            j0, n, s = unit
-            for t in ts:
-                nc.vector.tensor_tensor(
-                    planes(unit, 0, n)[:, t, :], window(s, t, j0, j0 + n), gate_sb[:, j0:j0 + n], MULT
-                )
-
         def woven(unit, a, b):
             return (
                 rounded(unit, a, b).rearrange("p (c i) t -> p c t i", i=RUN),
                 planes(unit, a, b).rearrange("p t (c i) -> p c t i", i=RUN),
             )
-
-        def weave(unit):
-            nc.vector.tensor_copy(*woven(unit, 0, unit[1]))
 
         banks = [psum.tile([P, H], F32, name="bank%d" % u) for u in range(8)]
         acc = [banks[u] for u in (0, 1, 2, 3, 4, 7, 6, 0, 1, 2, 3, 5)]
@@ -256,26 +247,42 @@ def tile_moe_pre_mlp_relu2_kernel(
                     multiply(g, s)
 
         def rectify(g):
-            relu = four.tile([P, PACK, P], F32, name="relu")
-            planes = acc[g][:].rearrange("j (p t) -> j t p", t=PACK)
-            if g == GROUPS - 1:
-                for t in (0, 2):
-                    nc.vector.tensor_scalar_max(relu[:, t:t + 2, :], planes[:, t:t + 2, :], 0.0)
+            if g < PACK:
+                relu = wide[1][:, g, :BLOCK].rearrange("p (t j) -> p t j", t=PACK)
+            elif g < 2 * PACK:
+                relu = narrow[:, 0, g - PACK, :].rearrange("p (t j) -> p t j", t=PACK)
+            elif g not in late:
+                words = h_bf[:, (g - 8) * C:(g - 7) * C, :].rearrange("p j t -> p (j t)").bitcast(F32)
+                relu = words.rearrange("p (t j) -> p t j", t=PACK)
+            elif g == GROUPS - 1:
+                relu = y_sb[:, BLOCK:2 * BLOCK].rearrange("p (t j) -> p t j", t=PACK)
             else:
-                nc.scalar.activation(relu[:], planes, ACT.Relu)
+                relu = four.tile([P, PACK, P], F32, name="relu")[:]
+            planes = acc[g][:].rearrange("j (p t) -> j t p", t=PACK)
+            if g in late:
+                nc.vector.tensor_scalar_max(relu, planes, 0.0)
+            else:
+                nc.scalar.activation(relu, planes, ACT.Relu)
             turned = acc[g][:].rearrange("p (t j) -> p t j", t=PACK)
             for t in range(PACK):
                 nc.tensor.transpose(turned[:, t, :], relu[:, t, :], ident[:])
 
+        h_first = []
+
+        def hidden(j0, n):
+            if j0 < BLOCK:
+                return h_first[0][:, j0:j0 + n, :]
+            return h_bf[:, j0 - BLOCK:j0 - BLOCK + n, :]
+
         def square(g):
             turned = acc[g][:].rearrange("p (t j) -> p j t", t=PACK)
-            nc.scalar.activation(h_bf[:, g * GROUP:(g + 1) * GROUP, :], turned, ACT.Square)
+            nc.scalar.activation(hidden(g * GROUP, GROUP), turned, ACT.Square)
 
         def quantise_h(j0, n):
             nc.vector.quantize_mx(
                 out=h_codes[:, j0:j0 + n].bitcast(FP8X4),
                 scales=h_scales[:, j0:j0 + n],
-                in_=h_bf[:, j0:j0 + n, :].rearrange("p j t -> p (j t)"),
+                in_=hidden(j0, n).rearrange("p j t -> p (j t)"),
             )
 
         def second_layer(j0, n, bank, col):
@@ -321,60 +328,57 @@ def tile_moe_pre_mlp_relu2_kernel(
         multiply_all([0, 1], [1, 2, 3])
         multiply_all([2, 3], [2, 3, 1])
         multiply(5, 0)
-        for g in range(0, 4):
-            rectify(g)
 
         weave_pool(b3, 0, BLOCK)
         weave_pool(b2, 0, 160)
         weave_vector(b1, GROUP, BLOCK)
+        for g in range(0, 4):
+            rectify(g)
         gather_vector(c2)
         weave_vector(b2, 160, BLOCK)
         gather_scalar(c1)
         quantise_x(5, 1, 2 * BLOCK)
         quantise_x(5, 2, BLOCK)
+        h_first.append(keep.tile([P, BLOCK, PACK], BF16, name="x_sb%d" % (2 * PACK - 1), align_bytes=64))
         for g in range(0, 4):
             square(g)
         multiply_all([4], [3, 2, 1])
         multiply_all([5], [3, 1, 2])
         multiply_all([6, 7], [3, 1, 0, 2])
-        for g in range(4, 8):
-            rectify(g)
 
         weave_pool(d2, 0, C)
-        weave_pool(c1, 0, 304)
-        weave_vector(c0, 0, BLOCK)
+        weave_pool(c0, 0, 160)
+        weave_vector(c0, 160, C)
         gather_vector(d3)
-        weave_vector(c1, 304, BLOCK)
+        weave_vector(c1, 0, C)
         weave_vector(d3, 0, C)
-        gather_scalar(f3)
-        quantise_x(10, 1, 2 * BLOCK)
-        quantise_x(8, 2, BLOCK)
+        quantise_x(8, 2, 2 * BLOCK)
+        multiply_all([8, 9], [2, 0, 1, 3])
+
+        weave_pool(e2, 0, 176)
+        weave_vector(c0, C, BLOCK)
+        weave_vector(c1, C, BLOCK)
+        weave_vector(e2, 176, C)
         for g in range(4, 8):
-            square(g)
-        multiply_all([8, 9], [0, 3, 1, 2])
-        multiply_all([10, 11], [1, 0])
+            rectify(g)
+        gather_scalar(e3)
         rectify(8)
         rectify(9)
+        quantise_x(10, 0, 3 * GROUP)
+        quantise_x(11, 2, 3 * GROUP)
+        for g in range(4, 8):
+            square(g)
+        multiply_all([10, 11], [0, 2, 1])
 
-        weave_gate(e2)
-        weave_gate(f3)
-        gather_gated(g3, [0])
-        quantise_x(10, 2, C)
-        multiply_all([10, 11], [2])
-        gather_gated(g3, [1])
+        weave_gate(e3)
         quantise_x(10, 3, GROUP)
-        multiply(10, 3)
-        rectify(10)
-        square(8)
-        square(9)
-        gather_gated(g3, [2, 3])
-        weave(g3)
-        quantise_h(0, C)
         quantise_x(11, 3, GROUP)
-        multiply(11, 3)
+        multiply_all([10, 11], [3])
+        rectify(10)
         rectify(11)
-        square(10)
-        square(11)
+        for g in range(8, 12):
+            square(g)
+        quantise_h(0, C)
         quantise_h(C, C)
         second_layer(0, BLOCK, banks[4], 0)
         quantise_h(BLOCK, BLOCK)
@@ -382,7 +386,7 @@ def tile_moe_pre_mlp_relu2_kernel(
         nc.vector.tensor_copy(y_sb[:, :BLOCK], banks[4][:])
         quantise_h(2 * BLOCK, C)
         second_layer(2 * BLOCK, C, banks[6], 0)
-        nc.vector.tensor_copy(y_sb[:, BLOCK:2 * BLOCK], banks[7][:])
+        nc.scalar.copy(y_sb[:, BLOCK:2 * BLOCK], banks[7][:])
         quantise_h(SLOTS - C, GROUP)
         second_layer(SLOTS - C, GROUP, banks[6], C)
         quantise_h(SLOTS - GROUP, GROUP)

@@ -28,8 +28,10 @@ PER_COLUMN = 16
 RUN = 4
 GROUP = 128
 GROUPS = SLOTS // GROUP
-BLOCK = 512
+THIRD = 512
 WINDOW = T + PER_COLUMN
+
+CUT_1, CUT_2, CUT_3, CUT_4, CUT_5 = 456, 384, 184, 192, 200
 
 
 def tile_moe_pre_mlp_relu2_kernel(
@@ -38,7 +40,6 @@ def tile_moe_pre_mlp_relu2_kernel(
     nc = tc.nc
     with ExitStack() as ctx:
         keep = ctx.enter_context(tc.tile_pool(name="keep", bufs=1))
-        four = ctx.enter_context(tc.tile_pool(name="four", bufs=4))
         psum = ctx.enter_context(tc.psum_pool(name="psum", bufs=1))
 
         offs_sb = keep.tile([P, SLOTS // PER_COLUMN], U16, name="offs_sb")
@@ -53,16 +54,16 @@ def tile_moe_pre_mlp_relu2_kernel(
         scales = keep.tile([P, PASSES * SLOTS - C], U8, name="scales", align_bytes=64)
         h_codes = keep.tile([P, SLOTS], U32, name="h_codes", align_bytes=64)
         h_scales = keep.tile([P, SLOTS], U8, name="h_scales", align_bytes=64)
-        h_bf = keep.tile([P, 2 * BLOCK, PACK], BF16, name="h_bf", align_bytes=64)
+        h_rest = keep.tile([P, 2 * THIRD, PACK], BF16, name="h_rest", align_bytes=64)
         y_sb = keep.tile([P, SLOTS], F32, name="y_sb", align_bytes=64)
         ident = keep.tile([P, P], F32, name="ident")
 
         def load_x(s, t):
-            rows = xT[K_PASS * s:K_PASS * (s + 1), :].rearrange("(p j) w -> p j w", j=PACK)
-            nc.sync.dma_start(out=x_sb[PACK * s + t][:, :T], in_=rows[:, t, :])
+            rows_of_pass = xT[K_PASS * s:K_PASS * (s + 1), :].rearrange("(p j) w -> p j w", j=PACK)
+            nc.sync.dma_start(out=x_sb[PACK * s + t][:, :T], in_=rows_of_pass[:, t, :])
 
-        def load_gate(queue, j0, j1):
-            queue.dma_start(out=gate_sb[:, j0:j1], in_=gate[:P, j0:j1])
+        def load_gate(j0, j1):
+            nc.sync.dma_start(out=gate_sb[:, j0:j1], in_=gate[:P, j0:j1])
 
         def load_scale_rows(tile, src):
             for r in range(4):
@@ -80,17 +81,18 @@ def tile_moe_pre_mlp_relu2_kernel(
         nc.vector.memset(warm[:, :8], 0.0)
         nc.scalar.activation(warm[:, 8:9], warm[:, 0:1], ACT.Copy)
 
-        wide = [keep.tile([P, PACK * 2 * BLOCK], F32, name="wide%d" % u) for u in range(3)]
+        wide = [keep.tile([P, PACK * 2 * THIRD], F32, name="wide%d" % u) for u in range(3)]
         wide = [tile[:].rearrange("p (t j) -> p t j", t=PACK) for tile in wide]
-        rows = keep.tile([P, 2 * PACK * BLOCK], F32, name="rows")
-        narrow = rows[:].rearrange("p (u t j) -> p u t j", u=2, t=PACK)
-        seams = rows[:].rearrange("p (u h j) -> p u h j", u=2, h=2)[:, :, :, BLOCK - 1:BLOCK + 1]
+        narrow_pair = keep.tile([P, 2 * PACK * THIRD], F32, name="narrow_pair")
+        narrow = narrow_pair[:].rearrange("p (u t j) -> p u t j", u=2, t=PACK)
+
+        seams = narrow_pair[:].rearrange("p (u h j) -> p u h j", u=2, h=2)[:, :, :, THIRD - 1:THIRD + 1]
         first_cols = keep.tile([P, 2, 2], F32, name="first_cols")
         gate_cols = [first_cols[:], seams[:, 0], seams[:, 1]]
 
-        def load_gate_cols(queue, block):
-            row = gate[0, block * BLOCK:(block + 1) * BLOCK]
-            queue.dma_start(out=gate_cols[block], in_=row.rearrange("(c h e) -> c h e", h=2, e=2))
+        def load_gate_cols(queue, third):
+            row = gate[0, third * THIRD:(third + 1) * THIRD]
+            queue.dma_start(out=gate_cols[third], in_=row.rearrange("(c h e) -> c h e", h=2, e=2))
 
         make_identity(nc, ident[:])
         nc.vector.memset(w1_sc[0][:].bitcast(I32), 0)
@@ -103,13 +105,13 @@ def tile_moe_pre_mlp_relu2_kernel(
         load_gate_cols(nc.scalar, 0)
         for t in range(1, PACK):
             load_x(0, t)
-        load_gate(nc.sync, 0, 2 * BLOCK)
+        load_gate(0, 2 * THIRD)
         for s in range(1, PASSES):
             for t in range(PACK):
                 load_x(s, t)
         load_gate_cols(nc.sync, 1)
         load_gate_cols(nc.sync, 2)
-        load_gate(nc.sync, 2 * BLOCK, SLOTS)
+        load_gate(2 * THIRD, SLOTS)
         for u in range(E // 2):
             load_w1_scales(u)
             load_w1(2 * u)
@@ -121,31 +123,31 @@ def tile_moe_pre_mlp_relu2_kernel(
         for tile, pos in zip(pos_sb, (pos1, pos2, pos3)):
             nc.sync.dma_start(tile[:], pos)
 
-        a0, a1, a2, a3 = [(0, BLOCK, s) for s in range(PASSES)]
-        b0, b1, b2, b3 = [(BLOCK, BLOCK, s) for s in range(PASSES)]
-        c0, c1, c2 = [(2 * BLOCK, BLOCK, s) for s in range(3)]
-        d2, d3 = [(2 * BLOCK, C, s) for s in (2, 3)]
-        e2 = (SLOTS - C, C, 2)
-        e3 = (SLOTS - C, C, 3)
+        a0, a1, a2, a3 = [(0, THIRD, s) for s in range(PASSES)]
+        b0, b1, b2, b3 = [(THIRD, THIRD, s) for s in range(PASSES)]
+        c0, c1, c2 = [(2 * THIRD, THIRD, s) for s in range(3)]
+        d2, d3 = [(2 * THIRD, C, s) for s in (2, 3)]
+        e2, e3 = [(SLOTS - C, C, s) for s in (2, 3)]
 
         gathered = {
-            a0: (wide[0], 0), b0: (wide[0], BLOCK), c0: (wide[0], C),
-            a1: (wide[1], 0), b1: (wide[1], BLOCK), c1: (wide[1], 0), e3: (narrow[:, 0], 0),
-            a3: (wide[2], 0), a2: (wide[2], BLOCK), c2: (wide[2], C), d2: (wide[2], C), e2: (wide[2], BLOCK),
-            b3: (narrow[:, 0], 0), b2: (narrow[:, 1], 0), d3: (narrow[:, 1], 0),
+            a0: (wide[0], 0), b0: (wide[0], THIRD), c0: (wide[0], C),
+            a1: (wide[1], 0), b1: (wide[1], THIRD), c1: (wide[1], 0),
+            a3: (wide[2], 0), a2: (wide[2], THIRD), c2: (wide[2], C), d2: (wide[2], C), e2: (wide[2], THIRD),
+            b3: (narrow[:, 0], 0), e3: (narrow[:, 0], 0),
+            b2: (narrow[:, 1], 0), d3: (narrow[:, 1], 0),
         }
+
         line = keep.tile([P, 13 * GROUP, PACK], BF16, name="line", align_bytes=64)
-        batches = [
+        stretches = [
             (264, [(0, 8, 0)]),
             (0, [(0, 4, 2), (0, 2, 1), (0, 4, 3), (2, 2, 1)]),
             (128, [(5, 3, 1), (4, 4, 3), (4, 4, 2), (4, 1, 1)]),
             (128, [(8, 2, 2), (8, 2, 0), (8, 2, 1), (8, 2, 3)]),
-            (128, [(10, 2, 0), (10, 2, 2), (10, 2, 1)]),
+            (120, [(10, 2, 0), (10, 2, 2), (10, 2, 1)]),
             (768, [(10, 2, 3)]),
         ]
-        place, column, first_column, filled = {}, {}, [], 0
-        for start, pieces in batches:
-            first_column.append(filled)
+        place, column, filled = {}, {}, 0
+        for start, pieces in stretches:
             for g0, count, s in pieces:
                 for g in range(g0, g0 + count):
                     place[g, s], column[g, s] = start, filled
@@ -155,8 +157,8 @@ def tile_moe_pre_mlp_relu2_kernel(
             return x_sb[PACK * s + t][:].indirect(offs_sb[:, a // PER_COLUMN:b // PER_COLUMN])
 
         def planes(unit, a, b):
-            tile, start = gathered[unit]
-            return tile[:, :, start + a:start + b]
+            buffer, start = gathered[unit]
+            return buffer[:, :, start + a:start + b]
 
         def rounded(unit, a, b):
             j0, n, s = unit
@@ -173,44 +175,38 @@ def tile_moe_pre_mlp_relu2_kernel(
             for t in range(PACK):
                 nc.vector.tensor_copy(planes(unit, 0, n)[:, t, :], window(s, t, j0, j0 + n))
 
-        def woven(unit, a, b):
-            return (
-                rounded(unit, a, b).rearrange("p (c i) t -> p c t i", i=RUN),
-                planes(unit, a, b).rearrange("p t (c i) -> p c t i", i=RUN),
-            )
-
         banks = [psum.tile([P, H], F32, name="bank%d" % u) for u in range(8)]
-        acc = [banks[u] for u in (0, 1, 2, 3, 4, 7, 6, 0, 1, 2, 3, 5)]
+        sums = [banks[u] for u in (0, 1, 2, 3, 4, 7, 6, 0, 1, 2, 3, 5)]
         gate_banks = [banks[7], banks[6], banks[5]]
 
-        def spread_gate(j0):
+        def spread_gate(third):
             for i in range(RUN):
-                col = gate_cols[j0 // BLOCK][:, i // 2, i % 2:i % 2 + 1].to_broadcast([P, P])
-                nc.tensor.transpose(gate_banks[j0 // BLOCK][:, i * P:(i + 1) * P], col, ident[:])
+                col = gate_cols[third][:, i // 2, i % 2:i % 2 + 1].to_broadcast([P, P])
+                nc.tensor.transpose(gate_banks[third][:, i * P:(i + 1) * P], col, ident[:])
 
-        def weave_pool(unit, a, b):
+        def weave_gpsimd(unit, a, b):
             j0 = unit[0]
             weights = gate_sb[:, j0 + a:j0 + b].unsqueeze(2).to_broadcast([P, b - a, PACK])
             nc.gpsimd.tensor_tensor(
                 rounded(unit, a, b), planes(unit, a, b).rearrange("p t j -> p j t"), weights, MULT
             )
 
+        def weave_in_runs(unit, a, b, weights):
+            nc.vector.tensor_tensor(
+                rounded(unit, a, b).rearrange("p (c i) t -> p c t i", i=RUN),
+                planes(unit, a, b).rearrange("p t (c i) -> p c t i", i=RUN),
+                weights.unsqueeze(2).to_broadcast([P, (b - a) // RUN, PACK, RUN]),
+                MULT,
+            )
+
         def weave_vector(unit, a, b):
-            j0 = unit[0] % BLOCK
-            spread = gate_banks[unit[0] // BLOCK][:].rearrange("p (i c) -> p c i", i=RUN)
-            weights = spread[:, (j0 + a) // RUN:(j0 + b) // RUN, :].unsqueeze(2)
-            nc.vector.tensor_tensor(*woven(unit, a, b), weights.to_broadcast([P, (b - a) // RUN, PACK, RUN]), MULT)
-
-        def weave_gate(unit):
-            j0, n, s = unit
-            weights = gate_sb[:, j0:j0 + n].rearrange("p (c i) -> p c i", i=RUN).unsqueeze(2)
-            nc.vector.tensor_tensor(*woven(unit, 0, n), weights.to_broadcast([P, n // RUN, PACK, RUN]), MULT)
-
-        done = {g: 0 for g in range(GROUPS)}
+            j0 = unit[0] % THIRD
+            spread = gate_banks[unit[0] // THIRD][:].rearrange("p (i c) -> p c i", i=RUN)
+            weave_in_runs(unit, a, b, spread[:, (j0 + a) // RUN:(j0 + b) // RUN, :])
 
         late = {
             GROUPS - 2: (h_codes[:, 64:64 + GROUP], h_scales[:, 64:64 + GROUP]),
-            GROUPS - 1: (h_codes[:, BLOCK - 64:BLOCK + 64], h_scales[:, 2 * BLOCK + 64:2 * BLOCK + 64 + GROUP]),
+            GROUPS - 1: (h_codes[:, THIRD - 64:THIRD + 64], h_scales[:, 2 * THIRD + 64:2 * THIRD + 64 + GROUP]),
         }
 
         def x_operand(g, s, n=GROUP):
@@ -227,63 +223,58 @@ def tile_moe_pre_mlp_relu2_kernel(
                 in_=line[:, place[g, s]:place[g, s] + n, :].rearrange("p j t -> p (j t)"),
             )
 
-        def multiply(g, s):
-            e = g * GROUP // C
-            words, exponents = x_operand(g, s)
-            nc.tensor.matmul_mx(
-                out=acc[g][:],
-                lhsT=words.bitcast(FP8X4),
-                lhsT_scale=exponents,
-                rhs=w1_sb[e][:, s, :].bitcast(FP4X4),
-                rhs_scale=w1_sc[e // 2][:, e % 2 * PASSES + s, :],
-                start=(done[g] == 0),
-                stop=(done[g] == PASSES - 1),
-            )
-            done[g] = done[g] + 1
+        passes_done = {g: 0 for g in range(GROUPS)}
 
-        def multiply_all(groups, passes):
+        def multiply(groups, passes):
             for g in groups:
+                e = g * GROUP // C
                 for s in passes:
-                    multiply(g, s)
+                    words, exponents = x_operand(g, s)
+                    nc.tensor.matmul_mx(
+                        out=sums[g][:],
+                        lhsT=words.bitcast(FP8X4),
+                        lhsT_scale=exponents,
+                        rhs=w1_sb[e][:, s, :].bitcast(FP4X4),
+                        rhs_scale=w1_sc[e // 2][:, e % 2 * PASSES + s, :],
+                        start=(passes_done[g] == 0),
+                        stop=(passes_done[g] == PASSES - 1),
+                    )
+                    passes_done[g] = passes_done[g] + 1
+
+        relu_spare = keep.tile([P, H], F32, name="relu_spare")
+        h_b_words = h_rest[:, :THIRD, :].rearrange("p j t -> p (j t)").bitcast(F32)
+        relu_places = (
+            [wide[1][:, u, :H] for u in range(4)]
+            + [narrow[:, 0, u, :] for u in range(4)]
+            + [h_b_words[:, :H], h_b_words[:, H:]]
+            + [relu_spare[:], y_sb[:, THIRD:2 * THIRD]]
+        )
 
         def rectify(g):
-            if g < PACK:
-                relu = wide[1][:, g, :BLOCK].rearrange("p (t j) -> p t j", t=PACK)
-            elif g < 2 * PACK:
-                relu = narrow[:, 0, g - PACK, :].rearrange("p (t j) -> p t j", t=PACK)
-            elif g not in late:
-                words = h_bf[:, (g - 8) * C:(g - 7) * C, :].rearrange("p j t -> p (j t)").bitcast(F32)
-                relu = words.rearrange("p (t j) -> p t j", t=PACK)
-            elif g == GROUPS - 1:
-                relu = y_sb[:, BLOCK:2 * BLOCK].rearrange("p (t j) -> p t j", t=PACK)
+            relu = relu_places[g].rearrange("j (t p) -> j t p", t=PACK)
+            by_plane = sums[g][:].rearrange("j (p t) -> j t p", t=PACK)
+            if g == GROUPS - 2:
+                nc.vector.tensor_scalar_max(relu, by_plane, 0.0)
             else:
-                relu = four.tile([P, PACK, P], F32, name="relu")[:]
-            planes = acc[g][:].rearrange("j (p t) -> j t p", t=PACK)
-            if g in late:
-                nc.vector.tensor_scalar_max(relu, planes, 0.0)
-            else:
-                nc.scalar.activation(relu, planes, ACT.Relu)
-            turned = acc[g][:].rearrange("p (t j) -> p t j", t=PACK)
+                nc.scalar.activation(relu, by_plane, ACT.Relu)
+            turned = sums[g][:].rearrange("p (t j) -> p t j", t=PACK)
             for t in range(PACK):
                 nc.tensor.transpose(turned[:, t, :], relu[:, t, :], ident[:])
 
-        h_first = []
+        def square(g, h):
+            turned = sums[g][:].rearrange("p (t j) -> p j t", t=PACK)
+            nc.scalar.activation(h, turned, ACT.Square)
 
-        def hidden(j0, n):
-            if j0 < BLOCK:
-                return h_first[0][:, j0:j0 + n, :]
-            return h_bf[:, j0 - BLOCK:j0 - BLOCK + n, :]
-
-        def square(g):
-            turned = acc[g][:].rearrange("p (t j) -> p j t", t=PACK)
-            nc.scalar.activation(hidden(g * GROUP, GROUP), turned, ACT.Square)
-
-        def quantise_h(j0, n):
+        def quantise_h(j0, h):
+            n = h.shape[1]
             nc.vector.quantize_mx(
                 out=h_codes[:, j0:j0 + n].bitcast(FP8X4),
                 scales=h_scales[:, j0:j0 + n],
-                in_=hidden(j0, n).rearrange("p j t -> p (j t)"),
+                in_=h.rearrange("p j t -> p (j t)"),
             )
+
+        def later_h(j0, n):
+            return h_rest[:, j0 - THIRD:j0 - THIRD + n, :]
 
         def second_layer(j0, n, bank, col):
             for j in range(0, n, C):
@@ -299,66 +290,63 @@ def tile_moe_pre_mlp_relu2_kernel(
                     stop=True,
                 )
 
-        spread_gate(0)
-        spread_gate(BLOCK)
-        spread_gate(2 * BLOCK)
+        for third in range(3):
+            spread_gate(third)
         gather_scalar(a0)
         gather_vector(b0)
-        gather_scalar(a1)
-        gather_scalar(a2)
-        gather_scalar(a3)
-        gather_scalar(b3)
-        gather_scalar(b2)
+        for unit in (a1, a2, a3, b3, b2):
+            gather_scalar(unit)
 
-        weave_pool(a0, 480, 2 * BLOCK)
-        weave_vector(a0, 0, 480)
+        weave_gpsimd(a0, CUT_1, 2 * THIRD)
+        weave_vector(a0, 0, CUT_1)
         gather_vector(b1)
-        quantise_x(4, 0, BLOCK)
-        quantise_x(0, 0, BLOCK)
-        multiply_all(range(0, 5), [0])
+        quantise_x(4, 0, THIRD)
+        quantise_x(0, 0, THIRD)
+        multiply(range(0, 5), [0])
 
-        weave_pool(a1, 256, 640)
-        weave_pool(a2, 0, 352)
-        weave_vector(a1, 0, 256)
+        weave_gpsimd(a1, C, THIRD + GROUP)
+        weave_gpsimd(a2, 0, CUT_2)
+        weave_vector(a1, 0, C)
         gather_vector(c0)
-        weave_vector(a2, 352, BLOCK)
-        weave_vector(a3, 0, BLOCK)
-        quantise_x(0, 2, 2 * BLOCK)
-        quantise_x(2, 3, BLOCK)
-        multiply_all([0, 1], [1, 2, 3])
-        multiply_all([2, 3], [2, 3, 1])
-        multiply(5, 0)
+        weave_vector(a2, CUT_2, THIRD)
+        weave_vector(a3, 0, THIRD)
+        quantise_x(0, 2, 2 * THIRD)
+        quantise_x(2, 3, THIRD)
+        multiply([0, 1], [1, 2, 3])
+        multiply([2, 3], [2, 3, 1])
+        multiply([5], [0])
 
-        weave_pool(b3, 0, BLOCK)
-        weave_pool(b2, 0, 160)
-        weave_vector(b1, GROUP, BLOCK)
+        weave_gpsimd(b3, 0, THIRD)
+        weave_gpsimd(b2, 0, CUT_3)
+        weave_vector(b1, GROUP, THIRD)
         for g in range(0, 4):
             rectify(g)
         gather_vector(c2)
-        weave_vector(b2, 160, BLOCK)
+        weave_vector(b2, CUT_3, THIRD)
         gather_scalar(c1)
-        quantise_x(5, 1, 2 * BLOCK)
-        quantise_x(5, 2, BLOCK)
-        h_first.append(keep.tile([P, BLOCK, PACK], BF16, name="x_sb%d" % (2 * PACK - 1), align_bytes=64))
+        quantise_x(5, 1, 2 * THIRD)
+        quantise_x(5, 2, THIRD)
+        h_first = keep.tile([P, THIRD, PACK], BF16, name="x_sb%d" % (2 * PACK - 1), align_bytes=64)
         for g in range(0, 4):
-            square(g)
-        multiply_all([4], [3, 2, 1])
-        multiply_all([5], [3, 1, 2])
-        multiply_all([6, 7], [3, 1, 0, 2])
+            square(g, h_first[:, g * GROUP:(g + 1) * GROUP, :])
+        multiply([4], [3, 2, 1])
+        multiply([5], [3, 1, 2])
+        multiply([6, 7], [3, 1, 0, 2])
 
-        weave_pool(d2, 0, C)
-        weave_pool(c0, 0, 160)
-        weave_vector(c0, 160, C)
+        weave_gpsimd(d2, 0, C)
+        weave_gpsimd(c0, 0, CUT_4)
         gather_vector(d3)
         weave_vector(c1, 0, C)
         weave_vector(d3, 0, C)
-        quantise_x(8, 2, 2 * BLOCK)
-        multiply_all([8, 9], [2, 0, 1, 3])
+        weave_vector(c0, CUT_4, C)
+        quantise_x(8, 1, THIRD)
+        quantise_x(8, 2, THIRD)
+        multiply([8, 9], [1, 3, 2, 0])
 
-        weave_pool(e2, 0, 176)
-        weave_vector(c0, C, BLOCK)
-        weave_vector(c1, C, BLOCK)
-        weave_vector(e2, 176, C)
+        weave_gpsimd(e2, 0, CUT_5)
+        weave_vector(c0, C, THIRD)
+        weave_vector(c1, C, THIRD)
+        weave_vector(e2, CUT_5, C)
         for g in range(4, 8):
             rectify(g)
         gather_scalar(e3)
@@ -367,31 +355,34 @@ def tile_moe_pre_mlp_relu2_kernel(
         quantise_x(10, 0, 3 * GROUP)
         quantise_x(11, 2, 3 * GROUP)
         for g in range(4, 8):
-            square(g)
-        multiply_all([10, 11], [0, 2, 1])
+            square(g, later_h(g * GROUP, GROUP))
+        multiply([10, 11], [0, 2, 1])
 
-        weave_gate(e3)
+        for a in (0, GROUP):
+            weights = gate_sb[:, SLOTS - C + a:SLOTS - C + a + GROUP]
+            weave_in_runs(e3, a, a + GROUP, weights.rearrange("p (c i) -> p c i", i=RUN))
         quantise_x(10, 3, GROUP)
         quantise_x(11, 3, GROUP)
-        multiply_all([10, 11], [3])
+        multiply([10, 11], [3])
         rectify(10)
         rectify(11)
         for g in range(8, 12):
-            square(g)
-        quantise_h(0, C)
-        quantise_h(C, C)
-        second_layer(0, BLOCK, banks[4], 0)
-        quantise_h(BLOCK, BLOCK)
-        second_layer(BLOCK, BLOCK, banks[7], 0)
-        nc.vector.tensor_copy(y_sb[:, :BLOCK], banks[4][:])
-        quantise_h(2 * BLOCK, C)
-        second_layer(2 * BLOCK, C, banks[6], 0)
-        nc.scalar.copy(y_sb[:, BLOCK:2 * BLOCK], banks[7][:])
-        quantise_h(SLOTS - C, GROUP)
+            square(g, later_h(g * GROUP, GROUP))
+
+        quantise_h(0, h_first[:, :C, :])
+        quantise_h(C, h_first[:, C:, :])
+        second_layer(0, THIRD, banks[4], 0)
+        quantise_h(THIRD, later_h(THIRD, THIRD))
+        second_layer(THIRD, THIRD, banks[7], 0)
+        nc.vector.tensor_copy(y_sb[:, :THIRD], banks[4][:])
+        quantise_h(2 * THIRD, later_h(2 * THIRD, C))
+        second_layer(2 * THIRD, C, banks[6], 0)
+        nc.scalar.copy(y_sb[:, THIRD:2 * THIRD], banks[7][:])
+        quantise_h(SLOTS - C, later_h(SLOTS - C, GROUP))
         second_layer(SLOTS - C, GROUP, banks[6], C)
-        quantise_h(SLOTS - GROUP, GROUP)
+        quantise_h(SLOTS - GROUP, later_h(SLOTS - GROUP, GROUP))
         second_layer(SLOTS - GROUP, GROUP, banks[0], 0)
-        nc.scalar.copy(y_sb[:, 2 * BLOCK:SLOTS - GROUP], banks[6][:, :C + GROUP])
+        nc.scalar.copy(y_sb[:, 2 * THIRD:SLOTS - GROUP], banks[6][:, :C + GROUP])
         nc.vector.tensor_copy(y_sb[:, SLOTS - GROUP:], banks[0][:, :GROUP])
 
         quarter = T // 4

@@ -332,6 +332,17 @@ def tile_moe_pre_mlp_relu2_kernel(
         multiply([4], [3, 2, 1])
         multiply([5], [3, 1, 2])
         multiply([6, 7], [3, 1, 0, 2])
+        for s in range(PASSES):
+            words, exponents = x_operand(7, s)
+            nc.tensor.matmul_mx(
+                out=sums[10][:],
+                lhsT=words.bitcast(FP8X4),
+                lhsT_scale=exponents,
+                rhs=w1_sb[3][:, s, :].bitcast(FP4X4),
+                rhs_scale=w1_sc[1][:, PASSES + s, :],
+                start=True,
+                stop=True,
+            )
 
         weave_gpsimd(d2, 0, C)
         weave_gpsimd(c0, 0, CUT_4)

from contextlib import ExitStack

import concourse.mybir as mybir
from concourse.masks import make_identity

K, T, E, C, H, N = 2048, 512, 6, 256, 512, 128
SLOTS = E * C
FLOPS = 2 * SLOTS * (K * H + H * N)
BYTES = 4 * K * T + E * (K * H + H * N) // 2 + E * (K * H + H * N) // 32 + 4 * SLOTS + 2 * 2 * SLOTS + 4 * N * T

F32 = mybir.dt.float32
BF16 = mybir.dt.bfloat16
I32 = mybir.dt.int32
U32 = mybir.dt.uint32
U16 = mybir.dt.uint16
U8 = mybir.dt.uint8
FP8X4 = mybir.dt.float8_e4m3fn_x4
FP4X4 = mybir.dt.float4_e2m1fn_x4
ACT = mybir.ActivationFunctionType
MULT = mybir.AluOpType.mult
ADD = mybir.AluOpType.add

P = 128
PACK = 4
K_PASS = P * PACK
PASSES = K // K_PASS
PER_COLUMN = 16
RUN = 4
GROUP = 128
GROUPS = SLOTS // GROUP
THIRD = 512
WINDOW = T + PER_COLUMN

CUT_1, CUT_2, CUT_3, CUT_4, CUT_5 = 456, 384, 184, 192, 200


def tile_moe_pre_mlp_relu2_kernel(
    tc, xT, w1_words, w1_scales, w2_words, w2_scales, gate, offs, pos1, pos2, pos3, out
):
    nc = tc.nc
    with ExitStack() as ctx:
        keep = ctx.enter_context(tc.tile_pool(name="keep", bufs=1))
        psum = ctx.enter_context(tc.psum_pool(name="psum", bufs=1))

        offs_sb = keep.tile([P, SLOTS // PER_COLUMN], U16, name="offs_sb")
        pos_sb = [keep.tile([P, T // PER_COLUMN], U16, name="pos_sb%d" % r) for r in range(3)]
        gate_sb = keep.tile([P, SLOTS], F32, name="gate_sb")
        x_sb = [keep.tile([P, WINDOW], F32, name="x_sb%d" % b, align_bytes=64) for b in range(PASSES * PACK)]
        w1_sb = [keep.tile([P, PASSES, 2 * H], U8, name="w1_sb%d" % e, align_bytes=64) for e in range(E)]
        w1_sc = [keep.tile([P, 2 * PASSES, H], U8, name="w1_sc%d" % u, align_bytes=64) for u in range(E // 2)]
        w2_sb = keep.tile([P, E, 2 * N], U8, name="w2_sb", align_bytes=64)
        w2_sc = keep.tile([P, E, N], U8, name="w2_sc", align_bytes=64)
        codes = keep.tile([P, PASSES * SLOTS - C], U32, name="codes", align_bytes=64)
        scales = keep.tile([P, PASSES * SLOTS - C], U8, name="scales", align_bytes=64)
        h_codes = keep.tile([P, SLOTS], U32, name="h_codes", align_bytes=64)
        h_scales = keep.tile([P, SLOTS], U8, name="h_scales", align_bytes=64)
        h_rest = keep.tile([P, 2 * THIRD, PACK], BF16, name="h_rest", align_bytes=64)
        y_sb = keep.tile([P, SLOTS], F32, name="y_sb", align_bytes=64)
        ident = keep.tile([P, P], F32, name="ident")

        def load_x(s, t):
            rows_of_pass = xT[K_PASS * s:K_PASS * (s + 1), :].rearrange("(p j) w -> p j w", j=PACK)
            nc.sync.dma_start(out=x_sb[PACK * s + t][:, :T], in_=rows_of_pass[:, t, :])

        def load_gate(j0, j1):
            nc.sync.dma_start(out=gate_sb[:, j0:j1], in_=gate[:P, j0:j1])

        def load_scale_rows(tile, src):
            for r in range(4):
                nc.sync.dma_start(out=tile[r:P:32, :, :].bitcast(I32), in_=src[r].bitcast(I32))

        def load_w1_scales(u):
            load_scale_rows(w1_sc[u], w1_scales[2 * u:2 * u + 2].rearrange("e s (q r) i -> r q (e s) i", r=4))

        def load_w1(e):
            nc.sync.dma_start(
                out=w1_sb[e][:].bitcast(I32), in_=w1_words[e].rearrange("s p b -> p s b").bitcast(I32)
            )

        warm = keep.tile([P, 16], F32, name="warm")
        nc.vector.memset(warm[:, :8], 0.0)
        nc.scalar.activation(warm[:, 8:9], warm[:, 0:1], ACT.Copy)

        wide = [keep.tile([P, PACK * 2 * THIRD], F32, name="wide%d" % u) for u in range(3)]
        wide = [tile[:].rearrange("p (t j) -> p t j", t=PACK) for tile in wide]
        narrow_pair = keep.tile([P, 2 * PACK * THIRD], F32, name="narrow_pair")
        narrow = narrow_pair[:].rearrange("p (u t j) -> p u t j", u=2, t=PACK)

        seams = narrow_pair[:].rearrange("p (u h j) -> p u h j", u=2, h=2)[:, :, :, THIRD - 1:THIRD + 1]
        first_cols = keep.tile([P, 2, 2], F32, name="first_cols")
        gate_cols = [first_cols[:], seams[:, 0], seams[:, 1]]

        def load_gate_cols(queue, third):
            row = gate[0, third * THIRD:(third + 1) * THIRD]
            queue.dma_start(out=gate_cols[third], in_=row.rearrange("(c h e) -> c h e", h=2, e=2))

        make_identity(nc, ident[:])
        nc.vector.memset(w1_sc[0][:].bitcast(I32), 0)
        nc.vector.memset(w1_sc[1][:].bitcast(I32), 0)
        nc.gpsimd.memset(w1_sc[2][:].bitcast(I32), 0)
        nc.gpsimd.memset(w2_sc[:].bitcast(I32), 0)

        load_x(0, 0)
        nc.sync.dma_start(offs_sb[:], offs)
        load_gate_cols(nc.scalar, 0)
        for t in range(1, PACK):
            load_x(0, t)
        load_gate(0, 2 * THIRD)
        for s in range(1, PASSES):
            for t in range(PACK):
                load_x(s, t)
        load_gate_cols(nc.sync, 1)
        load_gate_cols(nc.sync, 2)
        load_gate(2 * THIRD, SLOTS)
        for u in range(E // 2):
            load_w1_scales(u)
            load_w1(2 * u)
            load_w1(2 * u + 1)
        load_scale_rows(w2_sc, w2_scales.rearrange("e s (q r) n -> r q (e s) n", r=4))
        nc.sync.dma_start(
            out=w2_sb[:].bitcast(I32), in_=w2_words.rearrange("e s p b -> p (e s) b").bitcast(I32)
        )
        for tile, pos in zip(pos_sb, (pos1, pos2, pos3)):
            nc.sync.dma_start(tile[:], pos)

        a0, a1, a2, a3 = [(0, THIRD, s) for s in range(PASSES)]
        b0, b1, b2, b3 = [(THIRD, THIRD, s) for s in range(PASSES)]
        c0, c1, c2 = [(2 * THIRD, THIRD, s) for s in range(3)]
        d2, d3 = [(2 * THIRD, C, s) for s in (2, 3)]
        e2, e3 = [(SLOTS - C, C, s) for s in (2, 3)]

        gathered = {
            a0: (wide[0], 0), b0: (wide[0], THIRD), c0: (wide[0], C),
            a1: (wide[1], 0), b1: (wide[1], THIRD), c1: (wide[1], 0),
            a3: (wide[2], 0), a2: (wide[2], THIRD), c2: (wide[2], C), d2: (wide[2], C), e2: (wide[2], THIRD),
            b3: (narrow[:, 0], 0), e3: (narrow[:, 0], 0),
            b2: (narrow[:, 1], 0), d3: (narrow[:, 1], 0),
        }

        line = keep.tile([P, 13 * GROUP, PACK], BF16, name="line", align_bytes=64)
        stretches = [
            (264, [(0, 8, 0)]),
            (0, [(0, 4, 2), (0, 2, 1), (0, 4, 3), (2, 2, 1)]),
            (128, [(5, 3, 1), (4, 4, 3), (4, 4, 2), (4, 1, 1)]),
            (128, [(8, 2, 2), (8, 2, 0), (8, 2, 1), (8, 2, 3)]),
            (120, [(10, 2, 0), (10, 2, 2), (10, 2, 1)]),
            (768, [(10, 2, 3)]),
        ]
        place, column, filled = {}, {}, 0
        for start, pieces in stretches:
            for g0, count, s in pieces:
                for g in range(g0, g0 + count):
                    place[g, s], column[g, s] = start, filled
                    start, filled = start + GROUP, filled + GROUP

        def window(s, t, a, b):
            return x_sb[PACK * s + t][:].indirect(offs_sb[:, a // PER_COLUMN:b // PER_COLUMN])

        def planes(unit, a, b):
            buffer, start = gathered[unit]
            return buffer[:, :, start + a:start + b]

        def rounded(unit, a, b):
            j0, n, s = unit
            start = place[(j0 + a) // GROUP, s] + a % GROUP
            return line[:, start:start + b - a, :]

        def gather_scalar(unit):
            j0, n, s = unit
            for t in range(PACK):
                nc.scalar.activation(planes(unit, 0, n)[:, t, :], window(s, t, j0, j0 + n), ACT.Copy)

        def gather_vector(unit):
            j0, n, s = unit
            for t in range(PACK):
                nc.vector.tensor_copy(planes(unit, 0, n)[:, t, :], window(s, t, j0, j0 + n))

        banks = [psum.tile([P, H], F32, name="bank%d" % u) for u in range(8)]
        sums = [banks[u] for u in (0, 1, 2, 3, 4, 7, 6, 0, 1, 2, 3, 5)]
        gate_banks = [banks[7], banks[6], banks[5]]

        def spread_gate(third):
            for i in range(RUN):
                col = gate_cols[third][:, i // 2, i % 2:i % 2 + 1].to_broadcast([P, P])
                nc.tensor.transpose(gate_banks[third][:, i * P:(i + 1) * P], col, ident[:])

        def weave_gpsimd(unit, a, b):
            j0 = unit[0]
            weights = gate_sb[:, j0 + a:j0 + b].unsqueeze(2).to_broadcast([P, b - a, PACK])
            nc.gpsimd.tensor_tensor(
                rounded(unit, a, b), planes(unit, a, b).rearrange("p t j -> p j t"), weights, MULT
            )

        def weave_in_runs(unit, a, b, weights):
            nc.vector.tensor_tensor(
                rounded(unit, a, b).rearrange("p (c i) t -> p c t i", i=RUN),
                planes(unit, a, b).rearrange("p t (c i) -> p c t i", i=RUN),
                weights.unsqueeze(2).to_broadcast([P, (b - a) // RUN, PACK, RUN]),
                MULT,
            )

        def weave_vector(unit, a, b):
            j0 = unit[0] % THIRD
            spread = gate_banks[unit[0] // THIRD][:].rearrange("p (i c) -> p c i", i=RUN)
            weave_in_runs(unit, a, b, spread[:, (j0 + a) // RUN:(j0 + b) // RUN, :])

        late = {
            GROUPS - 2: (h_codes[:, 64:64 + GROUP], h_scales[:, 64:64 + GROUP]),
            GROUPS - 1: (h_codes[:, THIRD - 64:THIRD + 64], h_scales[:, 2 * THIRD + 64:2 * THIRD + 64 + GROUP]),
        }

        def x_operand(g, s, n=GROUP):
            if s == PASSES - 1 and g in late:
                return late[g]
            cols = slice(column[g, s], column[g, s] + n)
            return codes[:, cols], scales[:, cols]

        def quantise_x(g, s, n):
            words, exponents = x_operand(g, s, n)
            nc.vector.quantize_mx(
                out=words.bitcast(FP8X4),
                scales=exponents,
                in_=line[:, place[g, s]:place[g, s] + n, :].rearrange("p j t -> p (j t)"),
            )

        passes_done = {g: 0 for g in range(GROUPS)}

        def multiply(groups, passes):
            for g in groups:
                e = g * GROUP // C
                for s in passes:
                    words, exponents = x_operand(g, s)
                    nc.tensor.matmul_mx(
                        out=sums[g][:],
                        lhsT=words.bitcast(FP8X4),
                        lhsT_scale=exponents,
                        rhs=w1_sb[e][:, s, :].bitcast(FP4X4),
                        rhs_scale=w1_sc[e // 2][:, e % 2 * PASSES + s, :],
                        start=(passes_done[g] == 0),
                        stop=(passes_done[g] == PASSES - 1),
                    )
                    passes_done[g] = passes_done[g] + 1

        relu_spare = keep.tile([P, H], F32, name="relu_spare")
        h_b_words = h_rest[:, :THIRD, :].rearrange("p j t -> p (j t)").bitcast(F32)
        relu_places = (
            [wide[1][:, u, :H] for u in range(4)]
            + [narrow[:, 0, u, :] for u in range(4)]
            + [h_b_words[:, :H], h_b_words[:, H:]]
            + [relu_spare[:], y_sb[:, THIRD:2 * THIRD]]
        )

        def rectify(g):
            relu = relu_places[g].rearrange("j (t p) -> j t p", t=PACK)
            by_plane = sums[g][:].rearrange("j (p t) -> j t p", t=PACK)
            if g == GROUPS - 2:
                nc.vector.tensor_scalar_max(relu, by_plane, 0.0)
            else:
                nc.scalar.activation(relu, by_plane, ACT.Relu)
            turned = sums[g][:].rearrange("p (t j) -> p t j", t=PACK)
            for t in range(PACK):
                nc.tensor.transpose(turned[:, t, :], relu[:, t, :], ident[:])

        def square(g, h):
            turned = sums[g][:].rearrange("p (t j) -> p j t", t=PACK)
            nc.scalar.activation(h, turned, ACT.Square)

        def quantise_h(j0, h):
            n = h.shape[1]
            nc.vector.quantize_mx(
                out=h_codes[:, j0:j0 + n].bitcast(FP8X4),
                scales=h_scales[:, j0:j0 + n],
                in_=h.rearrange("p j t -> p (j t)"),
            )

        def later_h(j0, n):
            return h_rest[:, j0 - THIRD:j0 - THIRD + n, :]

        def second_layer(j0, n, bank, col):
            for j in range(0, n, C):
                width = min(C, n)
                cols = slice(j0 + j, j0 + j + width)
                nc.tensor.matmul_mx(
                    out=bank[:, col + j:col + j + width],
                    lhsT=w2_sb[:, (j0 + j) // C, :].bitcast(FP4X4),
                    lhsT_scale=w2_sc[:, (j0 + j) // C, :],
                    rhs=h_codes[:, cols].bitcast(FP8X4),
                    rhs_scale=h_scales[:, cols],
                    start=True,
                    stop=True,
                )

        for third in range(3):
            spread_gate(third)
        gather_scalar(a0)
        gather_vector(b0)
        for unit in (a1, a2, a3, b3, b2):
            gather_scalar(unit)

        weave_gpsimd(a0, CUT_1, 2 * THIRD)
        weave_vector(a0, 0, CUT_1)
        gather_vector(b1)
        quantise_x(4, 0, THIRD)
        quantise_x(0, 0, THIRD)
        multiply(range(0, 5), [0])

        weave_gpsimd(a1, C, THIRD + GROUP)
        weave_gpsimd(a2, 0, CUT_2)
        weave_vector(a1, 0, C)
        gather_vector(c0)
        weave_vector(a2, CUT_2, THIRD)
        weave_vector(a3, 0, THIRD)
        quantise_x(0, 2, 2 * THIRD)
        quantise_x(2, 3, THIRD)
        multiply([0, 1], [1, 2, 3])
        multiply([2, 3], [2, 3, 1])
        multiply([5], [0])

        weave_gpsimd(b3, 0, THIRD)
        weave_gpsimd(b2, 0, CUT_3)
        weave_vector(b1, GROUP, THIRD)
        for g in range(0, 4):
            rectify(g)
        gather_vector(c2)
        weave_vector(b2, CUT_3, THIRD)
        gather_scalar(c1)
        quantise_x(5, 1, 2 * THIRD)
        quantise_x(5, 2, THIRD)
        h_first = keep.tile([P, THIRD, PACK], BF16, name="x_sb%d" % (2 * PACK - 1), align_bytes=64)
        for g in range(0, 4):
            square(g, h_first[:, g * GROUP:(g + 1) * GROUP, :])
        multiply([4], [3, 2, 1])
        multiply([5], [3, 1, 2])
        multiply([6, 7], [3, 1, 0, 2])
        for s in range(PASSES):
            words, exponents = x_operand(7, s)
            nc.tensor.matmul_mx(
                out=sums[10][:],
                lhsT=words.bitcast(FP8X4),
                lhsT_scale=exponents,
                rhs=w1_sb[3][:, s, :].bitcast(FP4X4),
                rhs_scale=w1_sc[1][:, PASSES + s, :],
                start=True,
                stop=True,
            )

        weave_gpsimd(d2, 0, C)
        weave_gpsimd(c0, 0, CUT_4)
        gather_vector(d3)
        weave_vector(c1, 0, C)
        weave_vector(d3, 0, C)
        weave_vector(c0, CUT_4, C)
        quantise_x(8, 1, THIRD)
        quantise_x(8, 2, THIRD)
        multiply([8, 9], [1, 3, 2, 0])

        weave_gpsimd(e2, 0, CUT_5)
        weave_vector(c0, C, THIRD)
        weave_vector(c1, C, THIRD)
        weave_vector(e2, CUT_5, C)
        for g in range(4, 8):
            rectify(g)
        gather_scalar(e3)
        rectify(8)
        rectify(9)
        quantise_x(10, 0, 3 * GROUP)
        quantise_x(11, 2, 3 * GROUP)
        for g in range(4, 8):
            square(g, later_h(g * GROUP, GROUP))
        multiply([10, 11], [0, 2, 1])

        for a in (0, GROUP):
            weights = gate_sb[:, SLOTS - C + a:SLOTS - C + a + GROUP]
            weave_in_runs(e3, a, a + GROUP, weights.rearrange("p (c i) -> p c i", i=RUN))
        quantise_x(10, 3, GROUP)
        quantise_x(11, 3, GROUP)
        multiply([10, 11], [3])
        rectify(10)
        rectify(11)
        for g in range(8, 12):
            square(g, later_h(g * GROUP, GROUP))

        quantise_h(0, h_first[:, :C, :])
        quantise_h(C, h_first[:, C:, :])
        second_layer(0, THIRD, banks[4], 0)
        quantise_h(THIRD, later_h(THIRD, THIRD))
        second_layer(THIRD, THIRD, banks[7], 0)
        nc.vector.tensor_copy(y_sb[:, :THIRD], banks[4][:])
        quantise_h(2 * THIRD, later_h(2 * THIRD, C))
        second_layer(2 * THIRD, C, banks[6], 0)
        nc.scalar.copy(y_sb[:, THIRD:2 * THIRD], banks[7][:])
        quantise_h(SLOTS - C, later_h(SLOTS - C, GROUP))
        second_layer(SLOTS - C, GROUP, banks[6], C)
        quantise_h(SLOTS - GROUP, later_h(SLOTS - GROUP, GROUP))
        second_layer(SLOTS - GROUP, GROUP, banks[0], 0)
        nc.scalar.copy(y_sb[:, 2 * THIRD:SLOTS - GROUP], banks[6][:, :C + GROUP])
        nc.vector.tensor_copy(y_sb[:, SLOTS - GROUP:], banks[0][:, :GROUP])

        quarter = T // 4
        head, middle, rest = slice(0, quarter), slice(quarter, 2 * quarter), slice(2 * quarter, T)
        first = keep.tile([P, T], F32, name="first")
        second = keep.tile([P, T], F32, name="second")
        part = keep.tile([P, T], F32, name="part")
        total = keep.tile([P, T], F32, name="total")

        def fetched(r, cols):
            return y_sb[:].indirect(pos_sb[r][:, cols.start // PER_COLUMN:cols.stop // PER_COLUMN])

        nc.scalar.activation(first[:, middle], fetched(0, middle), ACT.Copy)
        nc.scalar.activation(first[:, rest], fetched(0, rest), ACT.Copy)
        nc.scalar.activation(second[:, rest], fetched(1, rest), ACT.Copy)
        nc.scalar.activation(first[:, head], fetched(0, head), ACT.Copy)
        nc.vector.tensor_copy(second[:, head], fetched(1, head))
        nc.vector.tensor_tensor(part[:, head], fetched(2, head), second[:, head], ADD)
        nc.vector.tensor_tensor(part[:, middle], fetched(1, middle), first[:, middle], ADD)
        nc.vector.tensor_tensor(part[:, rest], fetched(2, rest), first[:, rest], ADD)
        nc.vector.tensor_tensor(total[:, middle], fetched(2, middle), part[:, middle], ADD)
        nc.vector.tensor_tensor(total[:, rest], part[:, rest], second[:, rest], ADD)
        nc.vector.tensor_tensor(total[:, head], part[:, head], first[:, head], ADD)
        for cols, queue in zip((middle, rest, head), (nc.sync, nc.scalar, nc.sync)):
            queue.dma_start(out=out[:, cols], in_=total[:, cols])
